import numpy as np
import ml_dtypes


def mxq(x, axis, fmt="e4m3"):
    dtype, down = {"e4m3": (ml_dtypes.float8_e4m3fn, 7), "e5m2": (ml_dtypes.float8_e5m2, 14)}[fmt]
    v = np.moveaxis(np.asarray(x, np.float32).astype(ml_dtypes.bfloat16).astype(np.float64), axis, -1)
    blocks = v.reshape(v.shape[:-1] + (-1, 32))
    amax = np.abs(blocks).max(-1, keepdims=True)
    byte = np.maximum(np.where(amax > 0, np.frexp(amax)[1] - 1 + 127, 0) - down, 1)
    scale = np.exp2(byte - 127.0)
    codes = (blocks / scale).astype(np.float32).astype(dtype).astype(np.float64)
    return np.moveaxis((codes * scale).reshape(v.shape), -1, axis)


WIDE = False


def mx_kscale(k):
    if not WIDE:
        return np.ones(k)
    levels = np.array([10, -10, 5, -5, 0])
    if k % 512:
        return np.exp2(np.random.permutation(np.resize(levels, k // 32))).repeat(32)
    a = np.empty((k // 512, 16))
    for p in range(k // 512):
        a[p, :8] = np.random.permutation(np.resize(levels, 8))
        for g in range(8):
            far = levels[np.abs(levels - a[p, g]) >= 10]
            a[p, g + 8] = far[np.random.randint(len(far))]
    return np.exp2(a.ravel()).repeat(32)


BF16 = ml_dtypes.bfloat16


def bf(x):
    return np.asarray(x, np.float32).astype(BF16)


def f64(x):
    return np.asarray(x).astype(np.float64)


E2M1 = np.array([0.0, 0.5, 1.0, 1.5, 2.0, 3.0, 4.0, 6.0, -0.0, -0.5, -1.0, -1.5, -2.0, -3.0, -4.0, -6.0])


def pack_weight(w, fmt):
    k, n = w.shape
    w = f64(bf(w)).reshape(k // 32, 32, n)
    amax = np.abs(w).max(1)
    if fmt == "e4m3":
        byte = np.frexp(amax)[1] - 1 + 127 - 7
    else:
        mant, ex = np.frexp(amax / 6.0)
        byte = np.where(mant > 0.5, ex, ex - 1) + 127
    byte = np.clip(np.where(amax > 0, byte, 1), 1, 254)
    scaled = (w * np.exp2(127.0 - byte)[:, None, :]).reshape(k, n).astype(np.float32)
    by_word = np.ascontiguousarray(scaled.reshape(k // 512, 128, 4, n).transpose(0, 1, 3, 2))
    if fmt == "e4m3":
        words = by_word.astype(ml_dtypes.float8_e4m3fn).view(np.uint8)
    else:
        c = by_word.astype(ml_dtypes.float4_e2m1fn).view(np.uint8) & 0xF
        words = c[..., 0::2] | (c[..., 1::2] << 4)
    return np.ascontiguousarray(words), np.ascontiguousarray(byte.astype(np.uint8).reshape(k // 512, 16, n))


def unpack_weight(words, scales, fmt):
    g, p, n, _ = words.shape
    if fmt == "e4m3":
        vals = np.ascontiguousarray(words).view(ml_dtypes.float8_e4m3fn).astype(np.float64)
    else:
        nib = np.empty((g, p, n, 4), np.uint8)
        nib[..., 0::2] = words & 0xF
        nib[..., 1::2] = words >> 4
        vals = E2M1[nib]
    vals = vals * np.repeat(np.exp2(scales.astype(np.float64) - 127.0), 8, axis=1)[..., None]
    return vals.transpose(0, 1, 3, 2).reshape(g * 512, n)
def pack4(w):
    words, scales = pack_weight(w, "e2m1")
    return words.reshape(words.shape[0], 128, -1), scales


def unpack4(words, scales):
    return unpack_weight(words.reshape(words.shape[0], 128, -1, 2), scales, "e2m1")


M, K, C, R = 2048, 1024, 512, 512


def draw0():
    s = mx_kscale(K)
    t = mx_kscale(C)
    u = mx_kscale(M)
    gain = np.random.standard_normal((C, K)) / np.sqrt(C) / t[:, None]
    gain_words, gain_scales = pack4(gain)
    return {"bands": bf(np.random.standard_normal((M, K)) * s * u[:, None]),
            "mix": bf(np.random.standard_normal((K, C)) / np.sqrt(K) / s[:, None] * t),
            "pan": bf(np.random.standard_normal((M, C)) * t * u[:, None]),
            "radio": bf((1 + 0.1 * np.random.standard_normal(K)) / s),
            "gain_words": gain_words,
            "gain_scales": gain_scales,
            "mtf": bf(np.random.standard_normal((R, M)) / np.sqrt(M) / u)}


def core(bands, mix, pan, radio, gain_words, gain_scales, mtf):
    x = f64(bands)
    intensity = mxq(x, 1, "e4m3") @ mxq(f64(mix), 0, "e4m3")
    detail = f64(pan) - intensity
    injected = mxq(detail, 1, "e4m3") @ unpack4(gain_words, gain_scales)
    sharp = x * f64(radio) + injected
    coarse = mxq(f64(mtf), 1, "e4m3") @ mxq(detail, 0, "e4m3")
    return sharp, coarse


def e4m3fn_bytes(y):
    return np.clip(np.asarray(y, np.float64), -448.0, 448.0).astype(np.float32).astype(ml_dtypes.float8_e4m3fn).view(np.uint8)


def e4m3fn_values(b):
    return np.asarray(b, np.uint8).view(ml_dtypes.float8_e4m3fn).astype(np.float64)


def setup_inputs():
    d = draw0()
    x0 = np.asarray(d['mtf']).astype(np.float64)
    s = (np.max(np.abs(x0), axis=(0,), keepdims=True) / 448.0).astype(np.float32)
    out = {}
    for k, v in d.items():
        if k == 'mtf':
            out['mtf_bytes'] = e4m3fn_bytes(x0 / s.astype(np.float64))
            out['mtf_scale'] = s
        else:
            out[k] = v
    return out


def reference(bands, mix, pan, radio, gain_words, gain_scales, mtf_bytes, mtf_scale):
    return core(bands, mix, pan, radio, gain_words, gain_scales, e4m3fn_values(mtf_bytes) * mtf_scale.astype(np.float64))

@@ -1,0 +1,376 @@
+from contextlib import ExitStack
+
+import concourse.mybir as mybir
+from concourse.masks import make_identity
+
+M, K, C, R = 2048, 1024, 512, 512
+FLOPS = 2 * M * K * C + 2 * M * C * K + 2 * R * M * C
+BYTES = 2 * M * K + 2 * K * C + 2 * M * C + 2 * K + 128 * 2 * K + 16 * K + R * M + 4 * M + 4 * M * K + 4 * R * C
+
+F32 = mybir.dt.float32
+BF16 = mybir.dt.bfloat16
+I32 = mybir.dt.int32
+U32 = mybir.dt.uint32
+U8 = mybir.dt.uint8
+FP8 = mybir.dt.float8_e4m3fn
+FP8X4 = mybir.dt.float8_e4m3fn_x4
+FP4X4 = mybir.dt.float4_e2m1fn_x4
+MULT = mybir.AluOpType.mult
+ADD = mybir.AluOpType.add
+COPY = mybir.ActivationFunctionType.Copy
+SUB = mybir.AluOpType.subtract
+
+P = 128
+LOADS = """m1 a0 s m0 a1 r p0 c0 c1 b0 p1 b1 g G p2 B2 p3 B3"""
+HEAD = """w m1 z w t0 w t1 Z1 w m0 w Z3 w Z0 t2 M0 w w t3 w Z2 w M1 b0 I0 v w w D S0"""
+STEP = """i1 j0 p0 j1 i2 j2 f0 w w s1 t0 f1 p1 s2 i3 w t1 t2 t3 f2 s3 v j3 q6 w q7 p2 w u1 v f3 p3 j4 b0 y d0 d1 f4 j5 f5 j6 j7 w c0 c1 x0 v w f6 v f7 I0 u7 p4 x1 p5 r1 u3 S0 u5 w"""
+TAIL = """j0 v v w j1 f0 f1 j2 q6 v v j3 v v f2 v w v f3 v v w q7 v v j4 f4 v j5 v f5 j6 v j7 f6 v v w f7 w v v v v v v v v v v"""
+GU = (1, 3, 5, 7)
+MIX_SCALAR = (0, 0)
+G = M // 512
+H = K // 512
+
+
+def tile_pansharpen_detail_injection_s8_kernel(
+    tc, bands, mix, pan, radio, gain_words, gain_scales, mtf_bytes, mtf_scale, sharp, coarse
+):
+    nc = tc.nc
+    with ExitStack() as ctx:
+        const = ctx.enter_context(tc.tile_pool(name="const", bufs=1))
+        work = ctx.enter_context(tc.tile_pool(name="work", bufs=2))
+        turned_pool = ctx.enter_context(tc.tile_pool(name="turned_pool", bufs=3))
+        mtf_pool = ctx.enter_context(tc.tile_pool(name="mtf_pool", bufs=4))
+        prod_pool = ctx.enter_context(tc.tile_pool(name="prod_pool", bufs=1))
+        outs = ctx.enter_context(tc.tile_pool(name="outs", bufs=8))
+        ps_t = ctx.enter_context(tc.psum_pool(name="ps_t", bufs=3))
+        ps_i = ctx.enter_context(tc.psum_pool(name="ps_i", bufs=2))
+        ps_e = ctx.enter_context(tc.psum_pool(name="ps_e", bufs=3))
+
+        ident = const.tile([P, P], F32, name="ident")
+        make_identity(nc, ident[:])
+        ident_b = const.tile([P, P], BF16, name="ident_b", align_bytes=64)
+        nc.scalar.copy(out=ident_b[:], in_=ident[:])
+        ones_b = const.tile([P, P], BF16, name="ones_b", align_bytes=64)
+        nc.gpsimd.memset(ones_b[:], 1.0)
+        sc_rows = const.tile([P, P], F32, name="sc_rows")
+        nc.gpsimd.memset(sc_rows[:], 0.0)
+        gs = const.tile([P, K], U8, name="gs", align_bytes=64)
+        nc.gpsimd.memset(gs[:].bitcast(I32), 0)
+
+        mix_raw = const.tile([P, H, 4, C], BF16, name="mix_raw", align_bytes=64)
+        bands_sb = [const.tile([P, 4, K], BF16, name=f"bands{g}", align_bytes=64) for g in range(G)]
+        pan_sb = [const.tile([P, 4, C], BF16, name=f"pan{g}", align_bytes=64) for g in range(G)]
+        scale_bc = const.tile([P, M], F32, name="scale_bc", align_bytes=64)
+        codes_sb = [const.tile([P, 2, M], U8, name=f"codes{i}", align_bytes=64) for i in range(2)]
+        gw = const.tile([P, 2 * K], U8, name="gw", align_bytes=64)
+        radio_col = const.tile([P, H, 4], BF16, name="radio_col", align_bytes=64)
+
+        bands_v = bands.rearrange("(g p t) k -> g p t k", p=P, t=4)
+        pan_v = pan.rearrange("(g p t) c -> g p t c", p=P, t=4)
+        mix_v = mix.rearrange("(h p j) c -> h p j c", p=P, j=4)
+        mtf_v = mtf_bytes.rearrange("(p i r) k -> i p r k", i=2, r=2)
+        sharp_v = sharp.rearrange("(g p t) n -> g p t n", p=P, t=4)
+        coarse_v = coarse.rearrange("(p r) c -> r p c", r=4)
+
+        ctx.enter_context(tc.manual_schedule())
+
+        def load(dst, src):
+            nc.sync.dma_start(out=dst, in_=src)
+
+        for tok in LOADS.split():
+            c, k = tok[0], int(tok[1:] or 0)
+            if c == "m":
+                load(mix_raw[:, k], mix_v[k])
+            if c == "a":
+                load(bands_sb[0][:, 2 * k : 2 * k + 2], bands_v[0][:, 2 * k : 2 * k + 2])
+            if c == "b":
+                load(bands_sb[1][:, 2 * k : 2 * k + 2], bands_v[1][:, 2 * k : 2 * k + 2])
+            if c == "r":
+                load(radio_col[:], radio.rearrange("(h p t) -> p h t", p=P, t=4))
+            if c == "p":
+                load(pan_sb[k][:], pan_v[k])
+            if c == "s":
+                load(sc_rows[0:16, :], mtf_scale.rearrange("o (m n) -> (o m) n", n=P))
+            if c == "c":
+                load(codes_sb[k][:], mtf_v[k])
+            if c == "g":
+                load(gw[:].bitcast(I32), gain_words[0].bitcast(I32))
+            if c == "G":
+                for q in range(4):
+                    load(gs[32 * q : 32 * q + 4, :].bitcast(I32), gain_scales[0][4 * q : 4 * q + 4, :].bitcast(I32))
+            if c == "B":
+                load(bands_sb[k][:], bands_v[k])
+
+        radio_f = const.tile([P, H, 4], F32, name="radio_f")
+        diag = const.tile([P, H, 4, P], BF16, name="diag", align_bytes=64)
+        def diag_build():
+          nc.scalar.copy(out=radio_f[:], in_=radio_col[:])
+          for h in range(H):
+            for j in range(4):
+                nc.scalar.activation(
+                    out=diag[:, h, j, :], in_=ident_b[:], func=COPY, scale=radio_f[:, h, j : j + 1]
+                )
+        radio_bc = const.tile([P, H, P, 4], BF16, name="radio_bc", align_bytes=64)
+
+        def radio_spread(h):
+            xt = ps_t.tile([P, 4, P], F32, name="xt")
+            for j in range(4):
+                nc.tensor.matmul(xt[:, j, :], ones_b[:], diag[:, h, j, :], start=True, stop=True)
+            nc.scalar.copy(out=radio_bc[:, h], in_=xt[:].rearrange("p j m -> p m j"))
+
+        sc_T = const.tile([P, 16], F32, name="sc_T")
+
+        def scale_turn():
+            xt = ps_t.tile([P, 4, P], F32, name="xt")
+            nc.tensor.transpose(xt[:, 0, :], sc_rows[:], ident[:])
+            nc.scalar.copy(out=sc_T[:], in_=xt[:, 0, 0:16])
+
+        def scale_spread(b):
+            xt = ps_t.tile([P, 4, P], F32, name="xt")
+            for i in range(4):
+                m = 4 * b + i
+                nc.tensor.transpose(xt[:, i, :], sc_T[:, m : m + 1].to_broadcast([P, P]), ident[:])
+            nc.scalar.copy(out=scale_bc[:, 512 * b : 512 * (b + 1)], in_=xt[:].rearrange("p i x -> p (i x)"))
+
+
+        mix_c = const.tile([P, H, C], U32, name="mix_c", align_bytes=64)
+        mix_s = const.tile([P, H, C], U8, name="mix_s", align_bytes=64)
+        mix_il = [const.tile([P, C, 4], BF16, name=f"mix_il{h}", align_bytes=64) for h in range(H)]
+        mtf_il = const.tile([P, G, 512, 4], BF16, name="mtf_il", align_bytes=64)
+        mtf_il_w = mtf_il[:].rearrange("p g x j -> p (g x j)").bitcast(F32).rearrange("p (g x u) -> p g x u", g=G, u=2)
+        mtf_c = const.tile([P, G, 512], U32, name="mtf_c", align_bytes=64)
+        mtf_s = const.tile([P, G, 512], U8, name="mtf_s", align_bytes=64)
+        dy_c = const.tile([P, G, C], U32, name="dy_c", align_bytes=64)
+        dy_s = const.tile([P, G, C], U8, name="dy_s", align_bytes=64)
+
+        xT, xT_w, xc, xs, d, dx, dx_c, dx_s, prod, o, s, mtf_b = ({} for _ in range(12))
+        ib, eb, xb = {}, {}, {}
+
+        def open_bands(g):
+            xT[g] = turned_pool.tile([P, H, 512, 4], BF16, name="xT", align_bytes=64)
+            xT_w[g] = xT[g][:].rearrange("p h x j -> p (h x j)").bitcast(F32).rearrange("p (h x u) -> p h x u", h=H, u=2)
+            xc[g] = work.tile([P, H, 512], U32, name="xc", align_bytes=64)
+            xs[g] = work.tile([P, H, 512], U8, name="xs", align_bytes=64)
+
+        def turn_bands(g, t):
+            words = bands_sb[g][:, t].bitcast(F32)
+            xt = ps_t.tile([P, H, 2, P], F32, name="xt")
+            for h in range(H):
+                for u in range(2):
+                    nc.tensor.transpose(xt[:, h, u, :], words[:, 256 * h + u : 256 * (h + 1) : 2], ident[:])
+            nc.scalar.copy(out=xT_w[g][:, :, P * t : P * (t + 1), :], in_=xt[:].rearrange("p h u x -> p h x u"))
+
+        def quantize_bands(g):
+            nc.vector.quantize_mx(
+                out=xc[g][:].rearrange("p h x -> p (h x)").bitcast(FP8X4),
+                scales=xs[g][:].rearrange("p h x -> p (h x)"),
+                in_=xT[g][:].rearrange("p h x j -> p (h x j)"),
+            )
+
+        def scale_mtf(r, hh):
+            mtf_b[r, hh] = mtf_pool.tile([P, 1024], BF16, name="mtf_b", align_bytes=64)
+            cols = slice(1024 * hh, 1024 * hh + 1024)
+            nc.vector.tensor_tensor(
+                out=mtf_b[r, hh][:], in0=codes_sb[r // 2][:, r % 2, cols].bitcast(FP8), in1=scale_bc[:, cols], op=MULT
+            )
+
+        def turn_mtf(r, hh):
+            words = mtf_b[r, hh][:].bitcast(F32)
+            xt = ps_t.tile([P, 2, 2, P], F32, name="xt")
+            for i in range(2):
+                for u in range(2):
+                    nc.tensor.transpose(xt[:, i, u, :], words[:, 256 * i + u : 256 * (i + 1) : 2], ident[:])
+            nc.scalar.copy(
+                out=mtf_il_w[:, 2 * hh : 2 * hh + 2, P * r : P * (r + 1), :], in_=xt[:].rearrange("p i u x -> p i x u")
+            )
+
+        def quantize_mtf(hh):
+            gs2 = slice(2 * hh, 2 * hh + 2)
+            nc.vector.quantize_mx(
+                out=mtf_c[:, gs2].rearrange("p g x -> p (g x)").bitcast(FP8X4),
+                scales=mtf_s[:, gs2].rearrange("p g x -> p (g x)"),
+                in_=mtf_il[:, gs2].rearrange("p g x j -> p (g x j)"),
+            )
+
+        def intensity(g, cb):
+            cs = slice(P * cb, P * (cb + 1))
+            if cb == 0:
+                d[g] = work.tile([P, C, 4], BF16, name="d", align_bytes=64)
+            bank = ps_i.tile([P, 4, P], F32, name="bank_i")
+            ib[cb] = bank
+            for t in range(4):
+                for h in range(H):
+                    nc.tensor.matmul_mx(
+                        out=bank[:, t, :],
+                        lhsT=xc[g][:, h, P * t : P * (t + 1)].bitcast(FP8X4),
+                        lhsT_scale=xs[g][:, h, P * t : P * (t + 1)],
+                        rhs=mix_c[:, h, cs].bitcast(FP8X4),
+                        rhs_scale=mix_s[:, h, cs],
+                        start=(h == 0),
+                        stop=(h == H - 1),
+                    )
+
+        def subtract(g, cb):
+            cs = slice(P * cb, P * (cb + 1))
+            nc.vector.tensor_tensor(
+                out=d[g][:].rearrange("p (i b m) t -> p b m t i", i=4, b=4)[:, cb],
+                in0=pan_sb[g][:, :, cs].rearrange("p t (m i) -> p m t i", i=4),
+                in1=ib[cb][:].rearrange("p t (m i) -> p m t i", i=4),
+                op=SUB,
+            )
+
+        def turn_detail(g, u):
+            words = d[g][:].rearrange("p c t -> p (c t)").bitcast(F32)
+            if u == 0:
+                dx[g] = work.tile([P, 512, 4], BF16, name="dx", align_bytes=64)
+            xb[u] = ps_t.tile([P, 4, P], F32, name="xt")
+            for j in range(4):
+                nc.tensor.transpose(xb[u][:, j, :], words[:, 256 * j + u : 256 * (j + 1) : 2], ident[:])
+
+        def copy_detail(g, u):
+            pairs = xb[u][:].rearrange("p j x -> p (j x)").bitcast(BF16)
+            nc.scalar.copy(
+                out=dx[g][:, 256 * u : 256 * (u + 1), :].rearrange("p (e x) j -> p e x j", e=2),
+                in_=pairs.rearrange("p (j x e) -> p e x j", j=4, e=2),
+            )
+
+        def quantize_dx(g, u):
+            if u == 0:
+                dx_c[g] = work.tile([P, 512], U32, name="dx_c", align_bytes=64)
+                dx_s[g] = work.tile([P, 512], U8, name="dx_s", align_bytes=64)
+            cols = slice(256 * u, 256 * (u + 1))
+            nc.vector.quantize_mx(
+                out=dx_c[g][:, cols].bitcast(FP8X4),
+                scales=dx_s[g][:, cols],
+                in_=dx[g][:, cols].rearrange("p x j -> p (x j)"),
+            )
+
+        def quantize_dy(g):
+            nc.vector.quantize_mx(
+                out=dy_c[:, g].bitcast(FP8X4), scales=dy_s[:, g], in_=d[g][:].rearrange("p c t -> p (c t)")
+            )
+
+        def products(g, t, h):
+            if t == 0 and h == 0:
+                o[g] = [outs.tile([P, K], F32, name="o", align_bytes=64) for i in range(4)]
+            bank = ps_t.tile([P, 4, P], F32, name="xt")
+            for j in range(4):
+                nc.tensor.matmul(
+                    bank[:, j, :], xT[g][:, h, P * t : P * (t + 1), j], diag[:, h, j, :], start=True, stop=True
+                )
+            nc.scalar.copy(
+                out=o[g][t][:, 512 * h : 512 * (h + 1)].rearrange("p (m j) -> p m j", j=4),
+                in_=bank[:].rearrange("p j m -> p m j"),
+            )
+
+        def products_g(g, t, h):
+            prod[g, t, h] = prod_pool.tile([P, 512], F32, name=f"prod{t}{h}", align_bytes=64)
+            nc.gpsimd.tensor_tensor(
+                out=prod[g, t, h][:],
+                in0=bands_sb[g][:, t, 512 * h : 512 * (h + 1)],
+                in1=radio_bc[:, h].rearrange("p m j -> p (m j)"),
+                op=MULT,
+            )
+
+        def inject(g, t, h):
+            bank = ps_e.tile([P, 512], F32, name="bank_e")
+            eb[t, h] = bank
+            nc.tensor.matmul_mx(
+                out=bank[:],
+                lhsT=dx_c[g][:, P * t : P * (t + 1)].bitcast(FP8X4),
+                lhsT_scale=dx_s[g][:, P * t : P * (t + 1)],
+                rhs=gw[:, 1024 * h : 1024 * (h + 1)].bitcast(FP4X4),
+                rhs_scale=gs[:, 512 * h : 512 * (h + 1)],
+                start=True,
+                stop=True,
+            )
+
+        def finish(g, t, h):
+            cols = slice(512 * h, 512 * (h + 1))
+            first = prod[g, t, h][:] if (g, t, h) in prod else o[g][t][:, cols]
+            nc.vector.tensor_tensor(out=o[g][t][:, cols], in0=first, in1=eb[t, h][:], op=ADD)
+            if g == G - 1:
+                nc.sync.dma_start(out=sharp_v[g][:, t, cols], in_=o[g][t][:, cols])
+            elif h == H - 1:
+                nc.sync.dma_start(out=sharp_v[g][:, t], in_=o[g][t][:])
+
+        def coarse_rows(r):
+            bank = ps_i.tile([P, C], F32, name="bank_i")
+            for g in range(G):
+                nc.tensor.matmul_mx(
+                    out=bank[:],
+                    lhsT=mtf_c[:, g, P * r : P * (r + 1)].bitcast(FP8X4),
+                    lhsT_scale=mtf_s[:, g, P * r : P * (r + 1)],
+                    rhs=dy_c[:, g].bitcast(FP8X4),
+                    rhs_scale=dy_s[:, g],
+                    start=(g == 0),
+                    stop=(g == G - 1),
+                )
+            res = work.tile([P, C], F32, name="res", align_bytes=64)
+            nc.scalar.copy(
+                out=res[:].rearrange("p (m i) -> p m i", i=4), in_=bank[:].rearrange("p (i m) -> p m i", i=4)
+            )
+            nc.sync.dma_start(out=coarse_v[r], in_=res[:])
+
+        def mix_interleave(h):
+            eng = (nc.vector.tensor_copy, nc.scalar.copy)[MIX_SCALAR[h]]
+            eng(out=mix_il[h][:].rearrange("p (m i) j -> p m j i", i=4), in_=mix_raw[:, h].rearrange("p j (m i) -> p m j i", i=4))
+
+        def mix_quantize(h):
+            nc.vector.quantize_mx(
+                out=mix_c[:, h].bitcast(FP8X4), scales=mix_s[:, h], in_=mix_il[h][:].rearrange("p c j -> p (c j)")
+            )
+
+        def sm(r, hh):
+            return lambda: scale_mtf(r, hh)
+
+        def tm(r, hh):
+            return lambda: turn_mtf(r, hh)
+
+        def qm(g):
+            return lambda: quantize_mtf(g)
+
+        def cr(r):
+            return lambda: coarse_rows(r)
+
+        def step(order, g, vx, px):
+            e, n = g - 1, g + 1
+            E, I, T = 0 <= e, 0 <= g < G, n < G
+            vx, px = list(vx), list(px)
+            for tok in order.split():
+                c, k = tok[0], int(tok[1:] or 0)
+                u = (k // 2, k % 2)
+                if c == "j" and E: inject(e, u[0], u[1])
+                if c == "f" and E: finish(e, u[0], u[1])
+                if c == "i" and I: intensity(g, k)
+                if c == "s" and I: subtract(g, k)
+                if c == "I" and T: intensity(n, k)
+                if c == "S" and T: subtract(n, k)
+                if c == "t" and T:
+                    if k == 0: open_bands(n)
+                    turn_bands(n, k)
+                if c == "b" and T: quantize_bands(n)
+                if c == "p" and I and (g == 0 or k not in GU): products(g, u[0], u[1])
+                if c == "u" and 0 < g < G: products_g(g, u[0], u[1])
+                if c == "z" and g == -1: scale_turn()
+                if c == "D" and g == -1: diag_build()
+                if c == "Z" and g == -1: scale_spread(k)
+                if c == "r" and g == 0: radio_spread(k)
+                if c == "q" and E and (e == 0 or k not in GU): products(e, u[0], u[1])
+                if c == "d" and I: turn_detail(g, k)
+                if c == "c" and I: copy_detail(g, k)
+                if c == "y" and I: quantize_dy(g)
+                if c == "x" and I: quantize_dx(g, k)
+                if c == "m" and g == -1: mix_interleave(k)
+                if c == "M" and g == -1: mix_quantize(k)
+                if c == "v" and vx: vx.pop(0)()
+                if c == "w" and px: px.pop(0)()
+            for f in vx + px:
+                f()
+
+        step(HEAD, -1, [sm(0, 0), sm(1, 0), sm(3, 0)], [])
+        step(STEP, 0, [sm(1, 1), sm(0, 1), sm(2, 0)], [tm(0, 0), tm(1, 0)])
+        step(STEP, 1, [sm(2, 1), qm(0)], [tm(3, 0), tm(2, 0), tm(0, 1)])
+        step(STEP, 2, [sm(3, 1)], [tm(1, 1)])
+        step(STEP, 3, [qm(1)], [tm(2, 1), tm(3, 1)])
+        step(TAIL, 4, [], [cr(1), cr(2), cr(3), cr(0)])

@@ -17,18 +17,20 @@ FP8X4 = mybir.dt.float8_e4m3fn_x4
 FP4X4 = mybir.dt.float4_e2m1fn_x4
 MULT = mybir.AluOpType.mult
 ADD = mybir.AluOpType.add
-COPY = mybir.ActivationFunctionType.Copy
 SUB = mybir.AluOpType.subtract
 
 P = 128
-LOADS = """m1 a0 s m0 a1 r p0 c0 c1 b0 p1 b1 g G p2 B2 p3 B3"""
-HEAD = """w m1 z w t0 w t1 Z1 w m0 w Z3 w Z0 t2 M0 w w t3 w Z2 w M1 b0 I0 v w w D S0"""
-STEP = """i1 j0 p0 j1 i2 j2 f0 w w s1 t0 f1 p1 s2 i3 w t1 t2 t3 f2 s3 v j3 q6 w q7 p2 w u1 v f3 p3 j4 b0 y d0 d1 f4 j5 f5 j6 j7 w c0 c1 x0 v w f6 v f7 I0 u7 p4 x1 p5 r1 u3 S0 u5 w"""
-TAIL = """j0 v v w j1 f0 f1 j2 q6 v v j3 v v f2 v w v f3 v v w q7 v v j4 f4 v j5 v f5 j6 v j7 f6 v v w f7 w v v v v v v v v v v"""
-GU = (1, 3, 5, 7)
-MIX_SCALAR = (0, 0)
-G = M // 512
-H = K // 512
+BANK = 512
+GROUPS = M // 512
+HALVES = K // 512
+PAIRS = M // (2 * P)
+POOL_PIECES = 3
+TURN_BANKS = 3
+INT_BANKS = 2
+INJ_BANKS = 3
+XT_SLOTS = 3
+OUT_SLOTS = 5
+SHARE_SLOTS = 3
 
 
 def tile_pansharpen_detail_injection_s8_kernel(
@@ -36,341 +38,385 @@ def tile_pansharpen_detail_injection_s8_kernel(
 ):
     nc = tc.nc
     with ExitStack() as ctx:
-        const = ctx.enter_context(tc.tile_pool(name="const", bufs=1))
-        work = ctx.enter_context(tc.tile_pool(name="work", bufs=2))
-        turned_pool = ctx.enter_context(tc.tile_pool(name="turned_pool", bufs=3))
-        mtf_pool = ctx.enter_context(tc.tile_pool(name="mtf_pool", bufs=4))
-        prod_pool = ctx.enter_context(tc.tile_pool(name="prod_pool", bufs=1))
-        outs = ctx.enter_context(tc.tile_pool(name="outs", bufs=8))
-        ps_t = ctx.enter_context(tc.psum_pool(name="ps_t", bufs=3))
-        ps_i = ctx.enter_context(tc.psum_pool(name="ps_i", bufs=2))
-        ps_e = ctx.enter_context(tc.psum_pool(name="ps_e", bufs=3))
+        sb = ctx.enter_context(tc.tile_pool(name="sb", bufs=1))
+        ps = ctx.enter_context(tc.psum_pool(name="ps", bufs=1))
 
-        ident = const.tile([P, P], F32, name="ident")
-        make_identity(nc, ident[:])
-        ident_b = const.tile([P, P], BF16, name="ident_b", align_bytes=64)
-        nc.scalar.copy(out=ident_b[:], in_=ident[:])
-        ones_b = const.tile([P, P], BF16, name="ones_b", align_bytes=64)
-        nc.gpsimd.memset(ones_b[:], 1.0)
-        sc_rows = const.tile([P, P], F32, name="sc_rows")
-        nc.gpsimd.memset(sc_rows[:], 0.0)
-        gs = const.tile([P, K], U8, name="gs", align_bytes=64)
-        nc.gpsimd.memset(gs[:].bitcast(I32), 0)
+        def tiles(name, count, width, dtype):
+            return [sb.tile([P, width], dtype, name=f"{name}{i}", align_bytes=64) for i in range(count)]
 
-        mix_raw = const.tile([P, H, 4, C], BF16, name="mix_raw", align_bytes=64)
-        bands_sb = [const.tile([P, 4, K], BF16, name=f"bands{g}", align_bytes=64) for g in range(G)]
-        pan_sb = [const.tile([P, 4, C], BF16, name=f"pan{g}", align_bytes=64) for g in range(G)]
-        scale_bc = const.tile([P, M], F32, name="scale_bc", align_bytes=64)
-        codes_sb = [const.tile([P, 2, M], U8, name=f"codes{i}", align_bytes=64) for i in range(2)]
-        gw = const.tile([P, 2 * K], U8, name="gw", align_bytes=64)
-        radio_col = const.tile([P, H, 4], BF16, name="radio_col", align_bytes=64)
+        def one(name, width, dtype):
+            return tiles(name, 1, width, dtype)[0]
 
-        bands_v = bands.rearrange("(g p t) k -> g p t k", p=P, t=4)
-        pan_v = pan.rearrange("(g p t) c -> g p t c", p=P, t=4)
-        mix_v = mix.rearrange("(h p j) c -> h p j c", p=P, j=4)
-        mtf_v = mtf_bytes.rearrange("(p i r) k -> i p r k", i=2, r=2)
-        sharp_v = sharp.rearrange("(g p t) n -> g p t n", p=P, t=4)
+        banks = [ps.tile([P, BANK], F32, name=f"bank{i}") for i in range(8)]
+        turn_banks = banks[:TURN_BANKS]
+        int_banks = banks[TURN_BANKS : TURN_BANKS + INT_BANKS]
+        inj_banks = banks[TURN_BANKS + INT_BANKS :]
+
+        ident = one("ident", P, F32)
+        ident_b = one("ident_b", P, BF16)
+        ones_b = one("ones_b", P, BF16)
+        scale_col = one("scale_col", 4 * GROUPS, F32)
+        radio_col = one("radio_col", 8, BF16)
+        radio_bc = one("radio_bc", K, BF16)
+        diag = one("diag", K, BF16)
+        gain_w = one("gain_w", 2 * K, U8)
+        gain_s = one("gain_s", K, U8)
+        mix_raw = tiles("mix_raw", HALVES, 4 * C, BF16)
+        mix_il = tiles("mix_il", HALVES, 4 * C, BF16)
+        mix_c = tiles("mix_c", HALVES, C, U32)
+        mix_s = tiles("mix_s", HALVES, C, U8)
+        bands_sb = tiles("bands_sb", PAIRS, 2 * K, BF16)
+        pan_sb = tiles("pan_sb", PAIRS, 2 * C, BF16)
+        codes = tiles("codes", 4, M, U8)
+        mtf_b = tiles("mtf_b", 2, 1024, BF16)
+        mtf_il = tiles("mtf_il", 2, 1024, BF16)
+        mtf_c = tiles("mtf_c", 4, 512, U32)
+        mtf_s = tiles("mtf_s", 4, 512, U8)
+        x_il = tiles("x_il", XT_SLOTS, 2 * K, BF16)
+        x_c = tiles("x_c", 2, 512, U32)
+        x_s = tiles("x_s", 2, 512, U8)
+        detail = tiles("detail", 2, 4 * C, BF16)
+        share = tiles("share", SHARE_SLOTS, POOL_PIECES * 512, F32)
+        dx_c = tiles("dx_c", 3, 256, U32)
+        dx_s = tiles("dx_s", 3, 256, U8)
+        dy_il = tiles("dy_il", 2, 2 * C, BF16)
+        dy_c = tiles("dy_c", GROUPS, C, U32)
+        dy_s = tiles("dy_s", GROUPS, C, U8)
+        out_sb = tiles("out_sb", OUT_SLOTS, 2 * K, F32)
+        res = tiles("res", 4, C, F32)
+
+        bands_v = bands.rearrange("(g p a t) k -> g a p (t k)", p=P, a=2, t=2)
+        pan_v = pan.rearrange("(g p a t) c -> g a p (t c)", p=P, a=2, t=2)
+        sharp_v = sharp.rearrange("(g p a t) k -> g a p (t k)", p=P, a=2, t=2)
+        mix_v = mix.rearrange("(h p j) c -> h p (j c)", p=P, j=4)
+        mtf_v = mtf_bytes.rearrange("(p r) k -> r p k", r=4)
         coarse_v = coarse.rearrange("(p r) c -> r p c", r=4)
 
         ctx.enter_context(tc.manual_schedule())
 
+        make_identity(nc, ident[:])
+        nc.gpsimd.memset(ones_b[:], 1.0)
+        nc.vector.memset(gain_s[:].bitcast(I32), 0)
+        nc.scalar.copy(out=ident_b[:], in_=ident[:])
+
         def load(dst, src):
             nc.sync.dma_start(out=dst, in_=src)
 
-        for tok in LOADS.split():
-            c, k = tok[0], int(tok[1:] or 0)
-            if c == "m":
-                load(mix_raw[:, k], mix_v[k])
-            if c == "a":
-                load(bands_sb[0][:, 2 * k : 2 * k + 2], bands_v[0][:, 2 * k : 2 * k + 2])
-            if c == "b":
-                load(bands_sb[1][:, 2 * k : 2 * k + 2], bands_v[1][:, 2 * k : 2 * k + 2])
-            if c == "r":
-                load(radio_col[:], radio.rearrange("(h p t) -> p h t", p=P, t=4))
-            if c == "p":
-                load(pan_sb[k][:], pan_v[k])
-            if c == "s":
-                load(sc_rows[0:16, :], mtf_scale.rearrange("o (m n) -> (o m) n", n=P))
-            if c == "c":
-                load(codes_sb[k][:], mtf_v[k])
-            if c == "g":
-                load(gw[:].bitcast(I32), gain_words[0].bitcast(I32))
-            if c == "G":
-                for q in range(4):
-                    load(gs[32 * q : 32 * q + 4, :].bitcast(I32), gain_scales[0][4 * q : 4 * q + 4, :].bitcast(I32))
-            if c == "B":
-                load(bands_sb[k][:], bands_v[k])
+        def load_bands(s):
+            load(bands_sb[s][:], bands_v[s // 2, s % 2])
 
-        radio_f = const.tile([P, H, 4], F32, name="radio_f")
-        diag = const.tile([P, H, 4, P], BF16, name="diag", align_bytes=64)
-        def diag_build():
-          nc.scalar.copy(out=radio_f[:], in_=radio_col[:])
-          for h in range(H):
-            for j in range(4):
-                nc.scalar.activation(
-                    out=diag[:, h, j, :], in_=ident_b[:], func=COPY, scale=radio_f[:, h, j : j + 1]
-                )
-        radio_bc = const.tile([P, H, P, 4], BF16, name="radio_bc", align_bytes=64)
+        def load_pan(s):
+            load(pan_sb[s][:], pan_v[s // 2, s % 2])
 
-        def radio_spread(h):
-            xt = ps_t.tile([P, 4, P], F32, name="xt")
-            for j in range(4):
-                nc.tensor.matmul(xt[:, j, :], ones_b[:], diag[:, h, j, :], start=True, stop=True)
-            nc.scalar.copy(out=radio_bc[:, h], in_=xt[:].rearrange("p j m -> p m j"))
+        load(radio_col[:].rearrange("p (h j) -> p h j", j=4), radio.rearrange("(h p j) -> p h j", p=P, j=4))
+        load(mix_raw[0][:], mix_v[0])
+        load_bands(0)
+        load(codes[0][:], mtf_v[0])
+        load(scale_col[:].rearrange("p (g t) -> p g t", t=4), mtf_scale.rearrange("o (g p t) -> p (o g) t", p=P, t=4))
+        load(mix_raw[1][:], mix_v[1])
+        load_pan(0)
+        load_bands(1)
+        load_bands(2)
+        load(codes[1][:], mtf_v[1])
+        load_pan(1)
+        load(gain_w[:].bitcast(I32), gain_words[0].bitcast(I32))
+        for q in range(4):
+            load(gain_s[32 * q : 32 * q + 4, :].bitcast(I32), gain_scales[0][4 * q : 4 * q + 4, :].bitcast(I32))
+        for s in range(3, PAIRS):
+            load_bands(s)
+            load_pan(s - 1)
+            if s < 5:
+                load(codes[s - 1][:], mtf_v[s - 1])
+        load_pan(PAIRS - 1)
 
-        sc_T = const.tile([P, 16], F32, name="sc_T")
-
-        def scale_turn():
-            xt = ps_t.tile([P, 4, P], F32, name="xt")
-            nc.tensor.transpose(xt[:, 0, :], sc_rows[:], ident[:])
-            nc.scalar.copy(out=sc_T[:], in_=xt[:, 0, 0:16])
-
-        def scale_spread(b):
-            xt = ps_t.tile([P, 4, P], F32, name="xt")
-            for i in range(4):
-                m = 4 * b + i
-                nc.tensor.transpose(xt[:, i, :], sc_T[:, m : m + 1].to_broadcast([P, P]), ident[:])
-            nc.scalar.copy(out=scale_bc[:, 512 * b : 512 * (b + 1)], in_=xt[:].rearrange("p i x -> p (i x)"))
-
-
-        mix_c = const.tile([P, H, C], U32, name="mix_c", align_bytes=64)
-        mix_s = const.tile([P, H, C], U8, name="mix_s", align_bytes=64)
-        mix_il = [const.tile([P, C, 4], BF16, name=f"mix_il{h}", align_bytes=64) for h in range(H)]
-        mtf_il = const.tile([P, G, 512, 4], BF16, name="mtf_il", align_bytes=64)
-        mtf_il_w = mtf_il[:].rearrange("p g x j -> p (g x j)").bitcast(F32).rearrange("p (g x u) -> p g x u", g=G, u=2)
-        mtf_c = const.tile([P, G, 512], U32, name="mtf_c", align_bytes=64)
-        mtf_s = const.tile([P, G, 512], U8, name="mtf_s", align_bytes=64)
-        dy_c = const.tile([P, G, C], U32, name="dy_c", align_bytes=64)
-        dy_s = const.tile([P, G, C], U8, name="dy_s", align_bytes=64)
-
-        xT, xT_w, xc, xs, d, dx, dx_c, dx_s, prod, o, s, mtf_b = ({} for _ in range(12))
-        ib, eb, xb = {}, {}, {}
-
-        def open_bands(g):
-            xT[g] = turned_pool.tile([P, H, 512, 4], BF16, name="xT", align_bytes=64)
-            xT_w[g] = xT[g][:].rearrange("p h x j -> p (h x j)").bitcast(F32).rearrange("p (h x u) -> p h x u", h=H, u=2)
-            xc[g] = work.tile([P, H, 512], U32, name="xc", align_bytes=64)
-            xs[g] = work.tile([P, H, 512], U8, name="xs", align_bytes=64)
-
-        def turn_bands(g, t):
-            words = bands_sb[g][:, t].bitcast(F32)
-            xt = ps_t.tile([P, H, 2, P], F32, name="xt")
-            for h in range(H):
-                for u in range(2):
-                    nc.tensor.transpose(xt[:, h, u, :], words[:, 256 * h + u : 256 * (h + 1) : 2], ident[:])
-            nc.scalar.copy(out=xT_w[g][:, :, P * t : P * (t + 1), :], in_=xt[:].rearrange("p h u x -> p h x u"))
-
-        def quantize_bands(g):
-            nc.vector.quantize_mx(
-                out=xc[g][:].rearrange("p h x -> p (h x)").bitcast(FP8X4),
-                scales=xs[g][:].rearrange("p h x -> p (h x)"),
-                in_=xT[g][:].rearrange("p h x j -> p (h x j)"),
+        def turn_words(src, dst, bank):
+            words = src.bitcast(F32)
+            for n in range(4):
+                start = 256 * (n // 2) + n % 2
+                nc.tensor.transpose(bank[:, P * n : P * (n + 1)], words[:, start : 256 * (n // 2 + 1) : 2], ident[:])
+            nc.scalar.copy(
+                out=dst.bitcast(F32).rearrange("p (h x u) -> p h x u", h=2, u=2),
+                in_=bank[:].rearrange("p (h u x) -> p h x u", h=2, u=2),
             )
 
-        def scale_mtf(r, hh):
-            mtf_b[r, hh] = mtf_pool.tile([P, 1024], BF16, name="mtf_b", align_bytes=64)
-            cols = slice(1024 * hh, 1024 * hh + 1024)
+        def quantize(codes_out, scales_out, src):
+            nc.vector.quantize_mx(out=codes_out.bitcast(FP8X4), scales=scales_out, in_=src)
+
+        def build_diag():
             nc.vector.tensor_tensor(
-                out=mtf_b[r, hh][:], in0=codes_sb[r // 2][:, r % 2, cols].bitcast(FP8), in1=scale_bc[:, cols], op=MULT
-            )
-
-        def turn_mtf(r, hh):
-            words = mtf_b[r, hh][:].bitcast(F32)
-            xt = ps_t.tile([P, 2, 2, P], F32, name="xt")
-            for i in range(2):
-                for u in range(2):
-                    nc.tensor.transpose(xt[:, i, u, :], words[:, 256 * i + u : 256 * (i + 1) : 2], ident[:])
-            nc.scalar.copy(
-                out=mtf_il_w[:, 2 * hh : 2 * hh + 2, P * r : P * (r + 1), :], in_=xt[:].rearrange("p i u x -> p i x u")
-            )
-
-        def quantize_mtf(hh):
-            gs2 = slice(2 * hh, 2 * hh + 2)
-            nc.vector.quantize_mx(
-                out=mtf_c[:, gs2].rearrange("p g x -> p (g x)").bitcast(FP8X4),
-                scales=mtf_s[:, gs2].rearrange("p g x -> p (g x)"),
-                in_=mtf_il[:, gs2].rearrange("p g x j -> p (g x j)"),
-            )
-
-        def intensity(g, cb):
-            cs = slice(P * cb, P * (cb + 1))
-            if cb == 0:
-                d[g] = work.tile([P, C, 4], BF16, name="d", align_bytes=64)
-            bank = ps_i.tile([P, 4, P], F32, name="bank_i")
-            ib[cb] = bank
-            for t in range(4):
-                for h in range(H):
-                    nc.tensor.matmul_mx(
-                        out=bank[:, t, :],
-                        lhsT=xc[g][:, h, P * t : P * (t + 1)].bitcast(FP8X4),
-                        lhsT_scale=xs[g][:, h, P * t : P * (t + 1)],
-                        rhs=mix_c[:, h, cs].bitcast(FP8X4),
-                        rhs_scale=mix_s[:, h, cs],
-                        start=(h == 0),
-                        stop=(h == H - 1),
-                    )
-
-        def subtract(g, cb):
-            cs = slice(P * cb, P * (cb + 1))
-            nc.vector.tensor_tensor(
-                out=d[g][:].rearrange("p (i b m) t -> p b m t i", i=4, b=4)[:, cb],
-                in0=pan_sb[g][:, :, cs].rearrange("p t (m i) -> p m t i", i=4),
-                in1=ib[cb][:].rearrange("p t (m i) -> p m t i", i=4),
-                op=SUB,
-            )
-
-        def turn_detail(g, u):
-            words = d[g][:].rearrange("p c t -> p (c t)").bitcast(F32)
-            if u == 0:
-                dx[g] = work.tile([P, 512, 4], BF16, name="dx", align_bytes=64)
-            xb[u] = ps_t.tile([P, 4, P], F32, name="xt")
-            for j in range(4):
-                nc.tensor.transpose(xb[u][:, j, :], words[:, 256 * j + u : 256 * (j + 1) : 2], ident[:])
-
-        def copy_detail(g, u):
-            pairs = xb[u][:].rearrange("p j x -> p (j x)").bitcast(BF16)
-            nc.scalar.copy(
-                out=dx[g][:, 256 * u : 256 * (u + 1), :].rearrange("p (e x) j -> p e x j", e=2),
-                in_=pairs.rearrange("p (j x e) -> p e x j", j=4, e=2),
-            )
-
-        def quantize_dx(g, u):
-            if u == 0:
-                dx_c[g] = work.tile([P, 512], U32, name="dx_c", align_bytes=64)
-                dx_s[g] = work.tile([P, 512], U8, name="dx_s", align_bytes=64)
-            cols = slice(256 * u, 256 * (u + 1))
-            nc.vector.quantize_mx(
-                out=dx_c[g][:, cols].bitcast(FP8X4),
-                scales=dx_s[g][:, cols],
-                in_=dx[g][:, cols].rearrange("p x j -> p (x j)"),
-            )
-
-        def quantize_dy(g):
-            nc.vector.quantize_mx(
-                out=dy_c[:, g].bitcast(FP8X4), scales=dy_s[:, g], in_=d[g][:].rearrange("p c t -> p (c t)")
-            )
-
-        def products(g, t, h):
-            if t == 0 and h == 0:
-                o[g] = [outs.tile([P, K], F32, name="o", align_bytes=64) for i in range(4)]
-            bank = ps_t.tile([P, 4, P], F32, name="xt")
-            for j in range(4):
-                nc.tensor.matmul(
-                    bank[:, j, :], xT[g][:, h, P * t : P * (t + 1), j], diag[:, h, j, :], start=True, stop=True
-                )
-            nc.scalar.copy(
-                out=o[g][t][:, 512 * h : 512 * (h + 1)].rearrange("p (m j) -> p m j", j=4),
-                in_=bank[:].rearrange("p j m -> p m j"),
-            )
-
-        def products_g(g, t, h):
-            prod[g, t, h] = prod_pool.tile([P, 512], F32, name=f"prod{t}{h}", align_bytes=64)
-            nc.gpsimd.tensor_tensor(
-                out=prod[g, t, h][:],
-                in0=bands_sb[g][:, t, 512 * h : 512 * (h + 1)],
-                in1=radio_bc[:, h].rearrange("p m j -> p (m j)"),
+                out=diag[:].rearrange("p (n m) -> p n m", m=P),
+                in0=ident_b[:].unsqueeze(1).to_broadcast([P, 8, P]),
+                in1=radio_col[:].unsqueeze(2).to_broadcast([P, 8, P]),
                 op=MULT,
             )
 
-        def inject(g, t, h):
-            bank = ps_e.tile([P, 512], F32, name="bank_e")
-            eb[t, h] = bank
+        def spread_radio(h):
+            bank = int_banks[h]
+            nc.tensor.matmul(bank[:], ones_b[:], diag[:, 512 * h : 512 * (h + 1)], start=True, stop=True)
+            nc.scalar.copy(
+                out=radio_bc[:, 512 * h : 512 * (h + 1)].rearrange("p (m j) -> p m j", j=4),
+                in_=bank[:].rearrange("p (j m) -> p m j", j=4),
+            )
+
+        def interleave(engine_copy, dst, src):
+            engine_copy(
+                out=dst.rearrange("p (m i j) -> p m j i", i=4, j=4), in_=src.rearrange("p (j m i) -> p m j i", i=4, j=4)
+            )
+
+        def widen_mtf(n):
+            start = 1024 * (n % 2)
+            nc.scalar.copy(out=mtf_b[n % 2][:], in_=codes[n // 2][:, start : start + 1024].bitcast(FP8))
+
+        def turn_mtf(n):
+            words = mtf_b[n % 2][:].bitcast(F32)
+            for u in range(2):
+                for i in range(2):
+                    c0 = 256 * u + P * i
+                    nc.tensor.transpose(turn_banks[1][:, c0 : c0 + P], words[:, 256 * i + u : 256 * (i + 1) : 2], ident[:])
+
+        def scale_mtf(n):
+            scales = scale_col[:, 8 * (n % 2) : 8 * (n % 2 + 1)].rearrange("p (i u e) -> p i u e", i=2, u=2)
+            nc.vector.tensor_tensor(
+                out=mtf_il[n % 2][:].rearrange("p (i x u e) -> p i x u e", i=2, u=2, e=2),
+                in0=turn_banks[1][:].bitcast(BF16).rearrange("p (u i x e) -> p i x u e", i=2, u=2, e=2),
+                in1=scales.unsqueeze(2).to_broadcast([P, 2, P, 2, 2]),
+                op=MULT,
+            )
+
+        def quantize_mtf(n):
+            cols = slice(256 * (n % 2), 256 * (n % 2 + 1))
+            quantize(mtf_c[n // 2][:, cols], mtf_s[n // 2][:, cols], mtf_il[n % 2][:])
+
+        def turn_bands(s, t, bank):
+            cols = slice(K * t, K * (t + 1))
+            turn_words(bands_sb[s][:, cols], x_il[s % XT_SLOTS][:, cols], bank)
+
+        def quantize_bands(s):
+            quantize(x_c[s % 2][:], x_s[s % 2][:], x_il[s % XT_SLOTS][:])
+
+        def intensity(s, t):
+            for h in range(HALVES):
+                cols = slice(256 * t + P * h, 256 * t + P * (h + 1))
+                nc.tensor.matmul_mx(
+                    out=int_banks[(2 * s + t) % INT_BANKS][:],
+                    lhsT=x_c[s % 2][:, cols].bitcast(FP8X4),
+                    lhsT_scale=x_s[s % 2][:, cols],
+                    rhs=mix_c[h][:].bitcast(FP8X4),
+                    rhs_scale=mix_s[h][:],
+                    start=(h == 0),
+                    stop=(h == HALVES - 1),
+                )
+
+        def subtract(s, t):
+            row = 2 * (s % 2) + t
+            nc.vector.tensor_tensor(
+                out=detail[s // 2 % 2][:, C * row : C * (row + 1)],
+                in0=pan_sb[s][:, C * t : C * (t + 1)],
+                in1=int_banks[(2 * s + t) % INT_BANKS][:],
+                op=SUB,
+            )
+
+        def dx_il(s):
+            return share[s % SHARE_SLOTS][:, 0:512].bitcast(BF16)
+
+        def turn_detail(s):
+            turn_words(detail[s // 2 % 2][:, 1024 * (s % 2) : 1024 * (s % 2 + 1)], dx_il(s), turn_banks[0])
+
+        def quantize_dx(s):
+            quantize(dx_c[s % 3][:], dx_s[s % 3][:], dx_il(s))
+
+        def interleave_dy(g, half):
+            cols = slice(256 * half, 256 * (half + 1))
+            nc.scalar.copy(
+                out=dy_il[half][:].rearrange("p (m i t) -> p m t i", i=4, t=4),
+                in_=detail[g % 2][:].rearrange("p (t c) -> p t c", t=4)[:, :, cols].rearrange("p t (m i) -> p m t i", i=4),
+            )
+
+        def quantize_dy(g, half):
+            cols = slice(256 * half, 256 * (half + 1))
+            quantize(dy_c[g][:, cols], dy_s[g][:, cols], dy_il[half][:])
+
+        def pool_pieces(s):
+            return POOL_PIECES if 0 < s < PAIRS - 1 else 2
+
+        def pool_slot(s):
+            return share[(s - 1) % SHARE_SLOTS][:] if s > 0 else mix_il[1][:].bitcast(F32)
+
+        def products_pool(s):
+            n = pool_pieces(s)
+            whole = min(n, 2) * 512
+            nc.gpsimd.tensor_tensor(
+                out=pool_slot(s)[:, 0:whole], in0=bands_sb[s][:, 0:whole], in1=radio_bc[:, 0:whole], op=MULT
+            )
+            if n > 2:
+                rest = (n - 2) * 512
+                nc.gpsimd.tensor_tensor(
+                    out=pool_slot(s)[:, K : K + rest], in0=bands_sb[s][:, K : K + rest], in1=radio_bc[:, 0:rest], op=MULT
+                )
+
+        def diag_matmuls(s, n, bank):
+            turned = x_il[s % XT_SLOTS][:, 512 * n : 512 * (n + 1)]
+            for j in range(4):
+                d0 = 512 * (n % 2) + P * j
+                nc.tensor.matmul(
+                    bank[:, P * j : P * (j + 1)], turned[:, j:512:4], diag[:, d0 : d0 + P], start=True, stop=True
+                )
+
+        def diag_out(s, n, bank):
+            nc.scalar.copy(
+                out=out_sb[s % OUT_SLOTS][:, 512 * n : 512 * (n + 1)].rearrange("p (m j) -> p m j", j=4),
+                in_=bank[:].rearrange("p (j m) -> p m j", j=4),
+            )
+
+        def products_diag(s):
+            for n in range(pool_pieces(s), 4):
+                bank = turn_banks[2 * (n % 2)]
+                diag_matmuls(s, n, bank)
+                diag_out(s, n, bank)
+
+        def inject(s, n):
+            t, h = n // 2, n % 2
             nc.tensor.matmul_mx(
-                out=bank[:],
-                lhsT=dx_c[g][:, P * t : P * (t + 1)].bitcast(FP8X4),
-                lhsT_scale=dx_s[g][:, P * t : P * (t + 1)],
-                rhs=gw[:, 1024 * h : 1024 * (h + 1)].bitcast(FP4X4),
-                rhs_scale=gs[:, 512 * h : 512 * (h + 1)],
+                out=inj_banks[(4 * s + n) % INJ_BANKS][:],
+                lhsT=dx_c[s % 3][:, P * t : P * (t + 1)].bitcast(FP8X4),
+                lhsT_scale=dx_s[s % 3][:, P * t : P * (t + 1)],
+                rhs=gain_w[:, 1024 * h : 1024 * (h + 1)].bitcast(FP4X4),
+                rhs_scale=gain_s[:, 512 * h : 512 * (h + 1)],
                 start=True,
                 stop=True,
             )
 
-        def finish(g, t, h):
-            cols = slice(512 * h, 512 * (h + 1))
-            first = prod[g, t, h][:] if (g, t, h) in prod else o[g][t][:, cols]
-            nc.vector.tensor_tensor(out=o[g][t][:, cols], in0=first, in1=eb[t, h][:], op=ADD)
-            if g == G - 1:
-                nc.sync.dma_start(out=sharp_v[g][:, t, cols], in_=o[g][t][:, cols])
-            elif h == H - 1:
-                nc.sync.dma_start(out=sharp_v[g][:, t], in_=o[g][t][:])
-
-        def coarse_rows(r):
-            bank = ps_i.tile([P, C], F32, name="bank_i")
-            for g in range(G):
-                nc.tensor.matmul_mx(
-                    out=bank[:],
-                    lhsT=mtf_c[:, g, P * r : P * (r + 1)].bitcast(FP8X4),
-                    lhsT_scale=mtf_s[:, g, P * r : P * (r + 1)],
-                    rhs=dy_c[:, g].bitcast(FP8X4),
-                    rhs_scale=dy_s[:, g],
-                    start=(g == 0),
-                    stop=(g == G - 1),
-                )
-            res = work.tile([P, C], F32, name="res", align_bytes=64)
-            nc.scalar.copy(
-                out=res[:].rearrange("p (m i) -> p m i", i=4), in_=bank[:].rearrange("p (i m) -> p m i", i=4)
+        def finish(s, n):
+            cols = slice(512 * n, 512 * (n + 1))
+            out = out_sb[s % OUT_SLOTS]
+            product = pool_slot(s) if n < pool_pieces(s) else out[:]
+            nc.vector.tensor_tensor(
+                out=out[:, cols], in0=product[:, cols], in1=inj_banks[(4 * s + n) % INJ_BANKS][:], op=ADD
             )
-            nc.sync.dma_start(out=coarse_v[r], in_=res[:])
+            if s == PAIRS - 1:
+                nc.sync.dma_start(out=sharp_v[s // 2, s % 2][:, cols], in_=out[:, cols])
+            elif n % 2 == 1:
+                row = slice(K * (n // 2), K * (n // 2 + 1))
+                nc.sync.dma_start(out=sharp_v[s // 2, s % 2][:, row], in_=out[:, row])
 
-        def mix_interleave(h):
-            eng = (nc.vector.tensor_copy, nc.scalar.copy)[MIX_SCALAR[h]]
-            eng(out=mix_il[h][:].rearrange("p (m i) j -> p m j i", i=4), in_=mix_raw[:, h].rearrange("p j (m i) -> p m j i", i=4))
+        coarse_banks = turn_banks[1:3] + int_banks
 
-        def mix_quantize(h):
-            nc.vector.quantize_mx(
-                out=mix_c[:, h].bitcast(FP8X4), scales=mix_s[:, h], in_=mix_il[h][:].rearrange("p c j -> p (c j)")
+        def coarse_pass(r, g):
+            nc.tensor.matmul_mx(
+                out=coarse_banks[r][:],
+                lhsT=mtf_c[r][:, P * g : P * (g + 1)].bitcast(FP8X4),
+                lhsT_scale=mtf_s[r][:, P * g : P * (g + 1)],
+                rhs=dy_c[g][:].bitcast(FP8X4),
+                rhs_scale=dy_s[g][:],
+                start=(g == 0),
+                stop=(g == GROUPS - 1),
             )
 
-        def sm(r, hh):
-            return lambda: scale_mtf(r, hh)
+        def coarse_early(r):
+            for g in range(GROUPS - 1):
+                coarse_pass(r, g)
 
-        def tm(r, hh):
-            return lambda: turn_mtf(r, hh)
+        def coarse_out(r, engine_copy):
+            engine_copy(out=res[r][:], in_=coarse_banks[r][:])
+            nc.sync.dma_start(out=coarse_v[r], in_=res[r][:])
 
-        def qm(g):
-            return lambda: quantize_mtf(g)
+        build_diag()
+        interleave(nc.vector.tensor_copy, mix_il[0][:], mix_raw[0][:])
+        spread_radio(0)
+        spread_radio(1)
+        turn_bands(0, 0, turn_banks[0])
+        turn_bands(0, 1, turn_banks[2])
+        quantize(mix_c[0][:], mix_s[0][:], mix_il[0][:])
+        widen_mtf(0)
+        widen_mtf(1)
+        interleave(nc.vector.tensor_copy, mix_il[1][:], mix_raw[1][:])
+        quantize_bands(0)
+        quantize(mix_c[1][:], mix_s[1][:], mix_il[1][:])
+        products_pool(0)
+        for n in (2, 3):
+            diag_matmuls(0, n, inj_banks[n - 2])
+        turn_mtf(0)
+        scale_mtf(0)
+        turn_bands(1, 0, turn_banks[0])
+        intensity(0, 0)
+        intensity(0, 1)
+        diag_out(0, 2, inj_banks[0])
+        turn_bands(1, 1, turn_banks[2])
+        diag_out(0, 3, inj_banks[1])
+        subtract(0, 0)
+        subtract(0, 1)
+        turn_mtf(1)
+        turn_bands(2, 0, turn_banks[0])
+        turn_bands(2, 1, inj_banks[2])
+        quantize_bands(1)
+        quantize_mtf(0)
+        scale_mtf(1)
+        intensity(1, 0)
+        turn_detail(0)
+        products_diag(1)
+        intensity(1, 1)
+        widen_mtf(2)
 
-        def cr(r):
-            return lambda: coarse_rows(r)
+        last = PAIRS - 1
+        for s in range(1, PAIRS):
+            turning = s + 2 <= last
+            if s < last:
+                quantize_bands(s + 1)
+            if s >= 3:
+                quantize_dy((s - 3) // 2, (s - 3) % 2)
+            if s == last:
+                quantize_dy((s - 3) // 2, 1)
+            quantize_mtf(s)
+            quantize_dx(s - 1)
+            products_pool(s)
+            if turning:
+                turn_bands(s + 2, 0, turn_banks[0])
+                turn_bands(s + 2, 1, turn_banks[2])
+            if s >= 2 and (turning or s % 2 == 0):
+                interleave_dy((s - 2) // 2, s % 2)
+            if s % 2 == 0 and not turning:
+                interleave_dy((s - 2) // 2, 1)
+            for n in range(INJ_BANKS):
+                inject(s - 1, n)
+            subtract(s, 0)
+            if s < last:
+                intensity(s + 1, 0)
+            else:
+                coarse_early(0)
+            subtract(s, 1)
+            finish(s - 1, 0)
+            inject(s - 1, 3)
+            if s < last:
+                turn_mtf(s + 1)
+            else:
+                interleave_dy(GROUPS - 1, 0)
+            turn_detail(s)
+            for n in range(1, 4):
+                finish(s - 1, n)
+            if s < last:
+                scale_mtf(s + 1)
+                intensity(s + 1, 1)
+                products_diag(s + 1)
+            if turning:
+                widen_mtf(s + 2)
 
-        def step(order, g, vx, px):
-            e, n = g - 1, g + 1
-            E, I, T = 0 <= e, 0 <= g < G, n < G
-            vx, px = list(vx), list(px)
-            for tok in order.split():
-                c, k = tok[0], int(tok[1:] or 0)
-                u = (k // 2, k % 2)
-                if c == "j" and E: inject(e, u[0], u[1])
-                if c == "f" and E: finish(e, u[0], u[1])
-                if c == "i" and I: intensity(g, k)
-                if c == "s" and I: subtract(g, k)
-                if c == "I" and T: intensity(n, k)
-                if c == "S" and T: subtract(n, k)
-                if c == "t" and T:
-                    if k == 0: open_bands(n)
-                    turn_bands(n, k)
-                if c == "b" and T: quantize_bands(n)
-                if c == "p" and I and (g == 0 or k not in GU): products(g, u[0], u[1])
-                if c == "u" and 0 < g < G: products_g(g, u[0], u[1])
-                if c == "z" and g == -1: scale_turn()
-                if c == "D" and g == -1: diag_build()
-                if c == "Z" and g == -1: scale_spread(k)
-                if c == "r" and g == 0: radio_spread(k)
-                if c == "q" and E and (e == 0 or k not in GU): products(e, u[0], u[1])
-                if c == "d" and I: turn_detail(g, k)
-                if c == "c" and I: copy_detail(g, k)
-                if c == "y" and I: quantize_dy(g)
-                if c == "x" and I: quantize_dx(g, k)
-                if c == "m" and g == -1: mix_interleave(k)
-                if c == "M" and g == -1: mix_quantize(k)
-                if c == "v" and vx: vx.pop(0)()
-                if c == "w" and px: px.pop(0)()
-            for f in vx + px:
-                f()
-
-        step(HEAD, -1, [sm(0, 0), sm(1, 0), sm(3, 0)], [])
-        step(STEP, 0, [sm(1, 1), sm(0, 1), sm(2, 0)], [tm(0, 0), tm(1, 0)])
-        step(STEP, 1, [sm(2, 1), qm(0)], [tm(3, 0), tm(2, 0), tm(0, 1)])
-        step(STEP, 2, [sm(3, 1)], [tm(1, 1)])
-        step(STEP, 3, [qm(1)], [tm(2, 1), tm(3, 1)])
-        step(TAIL, 4, [], [cr(1), cr(2), cr(3), cr(0)])
+        interleave_dy(GROUPS - 1, 1)
+        coarse_early(1)
+        coarse_early(2)
+        quantize_dy(GROUPS - 1, 0)
+        quantize_dx(last)
+        for n in range(INJ_BANKS):
+            inject(last, n)
+        coarse_early(3)
+        finish(last, 0)
+        inject(last, 3)
+        quantize_dy(GROUPS - 1, 1)
+        for r in range(4):
+            coarse_pass(r, GROUPS - 1)
+        finish(last, 1)
+        finish(last, 2)
+        coarse_out(0, nc.scalar.copy)
+        finish(last, 3)
+        coarse_out(1, nc.scalar.copy)
+        coarse_out(3, nc.vector.tensor_copy)
+        coarse_out(2, nc.scalar.copy)

@@ -24,13 +24,10 @@ BANK = 512
 GROUPS = M // 512
 HALVES = K // 512
 PAIRS = M // (2 * P)
-POOL_PIECES = 3
-TURN_BANKS = 3
-INT_BANKS = 2
-INJ_BANKS = 3
-XT_SLOTS = 3
-OUT_SLOTS = 5
-SHARE_SLOTS = 3
+SHARED_PAIRS = (0, 1, PAIRS - 1)
+CALLS = PAIRS + 2
+STAGE_SLOTS = 3
+OUT_SLOTS = 4
 
 
 def tile_pansharpen_detail_injection_s8_kernel(
@@ -47,10 +44,17 @@ def tile_pansharpen_detail_injection_s8_kernel(
         def one(name, width, dtype):
             return tiles(name, 1, width, dtype)[0]
 
-        banks = [ps.tile([P, BANK], F32, name=f"bank{i}") for i in range(8)]
-        turn_banks = banks[:TURN_BANKS]
-        int_banks = banks[TURN_BANKS : TURN_BANKS + INT_BANKS]
-        inj_banks = banks[TURN_BANKS + INT_BANKS :]
+        def bank_tile(name, first, count=1):
+            return ps.tile([P, count * BANK], F32, name=name, offset=4 * BANK * first)[:]
+
+        head_banks = [bank_tile(f"head_bank{i}", i) for i in range(4)]
+        inj_psum = bank_tile("inj_psum", 0, 4)
+        tail_banks = [bank_tile(f"tail_bank{i}", i) for i in range(4)]
+        int_banks = [bank_tile(f"int_bank{i}", 4 + i) for i in range(2)]
+        turn_banks = [bank_tile(f"turn_bank{i}", 6 + i) for i in range(2)]
+
+        def inj_bank(s, n):
+            return inj_psum[:, BANK * n : BANK * (n + 1)] if s < PAIRS - 2 else tail_banks[n]
 
         ident = one("ident", P, F32)
         ident_b = one("ident_b", P, BF16)
@@ -62,28 +66,21 @@ def tile_pansharpen_detail_injection_s8_kernel(
         gain_w = one("gain_w", 2 * K, U8)
         gain_s = one("gain_s", K, U8)
         mix_raw = tiles("mix_raw", HALVES, 4 * C, BF16)
-        mix_il = tiles("mix_il", HALVES, 4 * C, BF16)
         mix_c = tiles("mix_c", HALVES, C, U32)
         mix_s = tiles("mix_s", HALVES, C, U8)
         bands_sb = tiles("bands_sb", PAIRS, 2 * K, BF16)
         pan_sb = tiles("pan_sb", PAIRS, 2 * C, BF16)
         codes = tiles("codes", 4, M, U8)
         mtf_b = tiles("mtf_b", 2, 1024, BF16)
-        mtf_il = tiles("mtf_il", 2, 1024, BF16)
-        mtf_c = tiles("mtf_c", 4, 512, U32)
-        mtf_s = tiles("mtf_s", 4, 512, U8)
-        x_il = tiles("x_il", XT_SLOTS, 2 * K, BF16)
-        x_c = tiles("x_c", 2, 512, U32)
-        x_s = tiles("x_s", 2, 512, U8)
+        stage = tiles("stage", STAGE_SLOTS, 4096, BF16)
+        call_c = tiles("call_c", CALLS, 1024, U32)
+        call_s = tiles("call_s", CALLS, 1024, U8)
         detail = tiles("detail", 2, 4 * C, BF16)
-        share = tiles("share", SHARE_SLOTS, POOL_PIECES * 512, F32)
-        dx_c = tiles("dx_c", 3, 256, U32)
-        dx_s = tiles("dx_s", 3, 256, U8)
-        dy_il = tiles("dy_il", 2, 2 * C, BF16)
-        dy_c = tiles("dy_c", GROUPS, C, U32)
-        dy_s = tiles("dy_s", GROUPS, C, U8)
+        dx_c = tiles("dx_c", 2, 256, U32)
+        dx_s = tiles("dx_s", 2, 256, U8)
         out_sb = tiles("out_sb", OUT_SLOTS, 2 * K, F32)
         res = tiles("res", 4, C, F32)
+        mix_il = [one("mix_il", 4 * C, BF16)[:], out_sb[0][:, 0:K].bitcast(BF16)]
 
         bands_v = bands.rearrange("(g p a t) k -> g a p (t k)", p=P, a=2, t=2)
         pan_v = pan.rearrange("(g p a t) c -> g a p (t c)", p=P, a=2, t=2)
@@ -111,9 +108,9 @@ def tile_pansharpen_detail_injection_s8_kernel(
         load(radio_col[:].rearrange("p (h j) -> p h j", j=4), radio.rearrange("(h p j) -> p h j", p=P, j=4))
         load(mix_raw[0][:], mix_v[0])
         load_bands(0)
+        load(mix_raw[1][:], mix_v[1])
         load(codes[0][:], mtf_v[0])
         load(scale_col[:].rearrange("p (g t) -> p g t", t=4), mtf_scale.rearrange("o (g p t) -> p (o g) t", p=P, t=4))
-        load(mix_raw[1][:], mix_v[1])
         load_pan(0)
         load_bands(1)
         load_bands(2)
@@ -129,14 +126,10 @@ def tile_pansharpen_detail_injection_s8_kernel(
                 load(codes[s - 1][:], mtf_v[s - 1])
         load_pan(PAIRS - 1)
 
-        def turn_words(src, dst, bank):
-            words = src.bitcast(F32)
-            for n in range(4):
-                start = 256 * (n // 2) + n % 2
-                nc.tensor.transpose(bank[:, P * n : P * (n + 1)], words[:, start : 256 * (n // 2 + 1) : 2], ident[:])
+        def turn_out(bank, dst):
             nc.scalar.copy(
                 out=dst.bitcast(F32).rearrange("p (h x u) -> p h x u", h=2, u=2),
-                in_=bank[:].rearrange("p (h u x) -> p h x u", h=2, u=2),
+                in_=bank.rearrange("p (h u x) -> p h x u", h=2, u=2),
             )
 
         def quantize(codes_out, scales_out, src):
@@ -152,55 +145,72 @@ def tile_pansharpen_detail_injection_s8_kernel(
 
         def spread_radio(h):
             bank = int_banks[h]
-            nc.tensor.matmul(bank[:], ones_b[:], diag[:, 512 * h : 512 * (h + 1)], start=True, stop=True)
+            nc.tensor.matmul(bank, ones_b[:], diag[:, 512 * h : 512 * (h + 1)], start=True, stop=True)
             nc.scalar.copy(
                 out=radio_bc[:, 512 * h : 512 * (h + 1)].rearrange("p (m j) -> p m j", j=4),
-                in_=bank[:].rearrange("p (j m) -> p m j", j=4),
+                in_=bank.rearrange("p (j m) -> p m j", j=4),
             )
 
-        def interleave(engine_copy, dst, src):
-            engine_copy(
-                out=dst.rearrange("p (m i j) -> p m j i", i=4, j=4), in_=src.rearrange("p (j m i) -> p m j i", i=4, j=4)
+        def interleave_mix(h):
+            nc.vector.tensor_copy(
+                out=mix_il[h].rearrange("p (u m e j) -> p m j u e", u=2, e=2, j=4),
+                in_=mix_raw[h][:].rearrange("p (j m u e) -> p m j u e", u=2, e=2, j=4),
             )
+
+        def quantize_mix(h):
+            quantize(mix_c[h][:], mix_s[h][:], mix_il[h])
+
+        mtf_place = [(1, 1)] + [(2 * r + 2, 1) for r in range(1, 4)]
+        dy_place = [(5, 1), (7, 1), (8, 0), (9, 0)]
+
+        def staged(call, half, start, width):
+            first = 2048 * half + start
+            return stage[call % STAGE_SLOTS][:, first : first + width]
+
+        def operand(call, half, start, width):
+            cols = slice(512 * half + start, 512 * half + start + width)
+            return call_c[call][:, cols].bitcast(FP8X4), call_s[call][:, cols]
+
+        def quantize_call(call, start=0, width=None):
+            if width is None:
+                width = 4096 if (call, 1) in mtf_place + dy_place else 2048
+            cols = slice(start // 4, (start + width) // 4)
+            quantize(call_c[call][:, cols], call_s[call][:, cols], staged(call, 0, start, width))
 
         def widen_mtf(n):
             start = 1024 * (n % 2)
             nc.scalar.copy(out=mtf_b[n % 2][:], in_=codes[n // 2][:, start : start + 1024].bitcast(FP8))
 
-        def turn_mtf(n):
+        def turn_mtf(n, bank):
             words = mtf_b[n % 2][:].bitcast(F32)
             for u in range(2):
                 for i in range(2):
                     c0 = 256 * u + P * i
-                    nc.tensor.transpose(turn_banks[1][:, c0 : c0 + P], words[:, 256 * i + u : 256 * (i + 1) : 2], ident[:])
+                    nc.tensor.transpose(bank[:, c0 : c0 + P], words[:, 256 * i + u : 256 * (i + 1) : 2], ident[:])
 
-        def scale_mtf(n):
+        def scale_mtf(n, bank):
             scales = scale_col[:, 8 * (n % 2) : 8 * (n % 2 + 1)].rearrange("p (i u e) -> p i u e", i=2, u=2)
             nc.vector.tensor_tensor(
-                out=mtf_il[n % 2][:].rearrange("p (i x u e) -> p i x u e", i=2, u=2, e=2),
-                in0=turn_banks[1][:].bitcast(BF16).rearrange("p (u i x e) -> p i x u e", i=2, u=2, e=2),
+                out=staged(*mtf_place[n // 2], 1024 * (n % 2), 1024).rearrange("p (i x u e) -> p i x u e", i=2, u=2, e=2),
+                in0=bank.bitcast(BF16).rearrange("p (u i x e) -> p i x u e", i=2, u=2, e=2),
                 in1=scales.unsqueeze(2).to_broadcast([P, 2, P, 2, 2]),
                 op=MULT,
             )
 
-        def quantize_mtf(n):
-            cols = slice(256 * (n % 2), 256 * (n % 2 + 1))
-            quantize(mtf_c[n // 2][:, cols], mtf_s[n // 2][:, cols], mtf_il[n % 2][:])
-
         def turn_bands(s, t, bank):
-            cols = slice(K * t, K * (t + 1))
-            turn_words(bands_sb[s][:, cols], x_il[s % XT_SLOTS][:, cols], bank)
-
-        def quantize_bands(s):
-            quantize(x_c[s % 2][:], x_s[s % 2][:], x_il[s % XT_SLOTS][:])
+            words = bands_sb[s][:, K * t : K * (t + 1)].bitcast(F32)
+            for n in range(4):
+                start = 256 * (n // 2) + n % 2
+                nc.tensor.transpose(bank[:, P * n : P * (n + 1)], words[:, start : 256 * (n // 2 + 1) : 2], ident[:])
+            turn_out(bank, staged(s, 0, K * t, K))
 
         def intensity(s, t):
             for h in range(HALVES):
-                cols = slice(256 * t + P * h, 256 * t + P * (h + 1))
+                x_c, x_s = operand(s, 0, 256 * t + P * h, P)
                 nc.tensor.matmul_mx(
-                    out=int_banks[(2 * s + t) % INT_BANKS][:],
-                    lhsT=x_c[s % 2][:, cols].bitcast(FP8X4),
-                    lhsT_scale=x_s[s % 2][:, cols],
+                    out=int_banks[t],
+                    lhsT=x_c,
+                    lhsT_scale=x_s,
                     rhs=mix_c[h][:].bitcast(FP8X4),
                     rhs_scale=mix_s[h][:],
                     start=(h == 0),
@@ -210,52 +220,42 @@ def tile_pansharpen_detail_injection_s8_kernel(
         def subtract(s, t):
             row = 2 * (s % 2) + t
             nc.vector.tensor_tensor(
-                out=detail[s // 2 % 2][:, C * row : C * (row + 1)],
-                in0=pan_sb[s][:, C * t : C * (t + 1)],
-                in1=int_banks[(2 * s + t) % INT_BANKS][:],
+                out=detail[s // 2 % 2][:, C * row : C * (row + 1)].rearrange("p (u m e) -> p u m e", u=2, e=2),
+                in0=pan_sb[s][:, C * t : C * (t + 1)].rearrange("p (m u e) -> p u m e", u=2, e=2),
+                in1=int_banks[t].rearrange("p (u m e) -> p u m e", u=2, e=2),
                 op=SUB,
             )
 
         def dx_il(s):
-            return share[s % SHARE_SLOTS][:, 0:512].bitcast(BF16)
+            return out_sb[(s + 1) % OUT_SLOTS][:, 0:512].bitcast(BF16)
 
-        def turn_detail(s):
-            turn_words(detail[s // 2 % 2][:, 1024 * (s % 2) : 1024 * (s % 2 + 1)], dx_il(s), turn_banks[0])
+        def turn_detail(s, bank):
+            words = detail[s // 2 % 2][:, 1024 * (s % 2) : 1024 * (s % 2 + 1)].bitcast(F32)
+            for n in range(4):
+                nc.tensor.transpose(bank[:, P * n : P * (n + 1)], words[:, P * n : P * (n + 1)], ident[:])
+            turn_out(bank, dx_il(s))
 
         def quantize_dx(s):
-            quantize(dx_c[s % 3][:], dx_s[s % 3][:], dx_il(s))
+            quantize(dx_c[s % 2][:], dx_s[s % 2][:], dx_il(s))
 
-        def interleave_dy(g, half):
+        def interleave_dy(g, half, engine_copy=nc.scalar.copy):
             cols = slice(256 * half, 256 * (half + 1))
-            nc.scalar.copy(
-                out=dy_il[half][:].rearrange("p (m i t) -> p m t i", i=4, t=4),
+            engine_copy(
+                out=staged(*dy_place[g], 1024 * half, 1024).rearrange("p (m i t) -> p m t i", i=4, t=4),
                 in_=detail[g % 2][:].rearrange("p (t c) -> p t c", t=4)[:, :, cols].rearrange("p t (m i) -> p m t i", i=4),
             )
 
-        def quantize_dy(g, half):
-            cols = slice(256 * half, 256 * (half + 1))
-            quantize(dy_c[g][:, cols], dy_s[g][:, cols], dy_il[half][:])
-
-        def pool_pieces(s):
-            return POOL_PIECES if 0 < s < PAIRS - 1 else 2
-
-        def pool_slot(s):
-            return share[(s - 1) % SHARE_SLOTS][:] if s > 0 else mix_il[1][:].bitcast(F32)
-
         def products_pool(s):
-            n = pool_pieces(s)
-            whole = min(n, 2) * 512
+            rows = 1 if s in SHARED_PAIRS else 2
             nc.gpsimd.tensor_tensor(
-                out=pool_slot(s)[:, 0:whole], in0=bands_sb[s][:, 0:whole], in1=radio_bc[:, 0:whole], op=MULT
+                out=out_sb[s % OUT_SLOTS][:, 0 : rows * K].rearrange("p (t k) -> p t k", t=rows),
+                in0=bands_sb[s][:, 0 : rows * K].rearrange("p (t k) -> p t k", t=rows),
+                in1=radio_bc[:].unsqueeze(1).to_broadcast([P, rows, K]),
+                op=MULT,
             )
-            if n > 2:
-                rest = (n - 2) * 512
-                nc.gpsimd.tensor_tensor(
-                    out=pool_slot(s)[:, K : K + rest], in0=bands_sb[s][:, K : K + rest], in1=radio_bc[:, 0:rest], op=MULT
-                )
 
         def diag_matmuls(s, n, bank):
-            turned = x_il[s % XT_SLOTS][:, 512 * n : 512 * (n + 1)]
+            turned = staged(s, 0, 512 * n, 512)
             for j in range(4):
                 d0 = 512 * (n % 2) + P * j
                 nc.tensor.matmul(
@@ -265,49 +265,48 @@ def tile_pansharpen_detail_injection_s8_kernel(
         def diag_out(s, n, bank):
             nc.scalar.copy(
                 out=out_sb[s % OUT_SLOTS][:, 512 * n : 512 * (n + 1)].rearrange("p (m j) -> p m j", j=4),
-                in_=bank[:].rearrange("p (j m) -> p m j", j=4),
+                in_=bank.rearrange("p (j m) -> p m j", j=4),
             )
 
-        def products_diag(s):
-            for n in range(pool_pieces(s), 4):
-                bank = turn_banks[2 * (n % 2)]
+        def products_diag(s, banks):
+            for n, bank in zip((2, 3), banks):
                 diag_matmuls(s, n, bank)
                 diag_out(s, n, bank)
 
         def inject(s, n):
             t, h = n // 2, n % 2
             nc.tensor.matmul_mx(
-                out=inj_banks[(4 * s + n) % INJ_BANKS][:],
-                lhsT=dx_c[s % 3][:, P * t : P * (t + 1)].bitcast(FP8X4),
-                lhsT_scale=dx_s[s % 3][:, P * t : P * (t + 1)],
+                out=inj_bank(s, n),
+                lhsT=dx_c[s % 2][:, P * t : P * (t + 1)].bitcast(FP8X4),
+                lhsT_scale=dx_s[s % 2][:, P * t : P * (t + 1)],
                 rhs=gain_w[:, 1024 * h : 1024 * (h + 1)].bitcast(FP4X4),
                 rhs_scale=gain_s[:, 512 * h : 512 * (h + 1)],
                 start=True,
                 stop=True,
             )
 
-        def finish(s, n):
+        def finish(s):
+            out = out_sb[s % OUT_SLOTS]
+            nc.vector.tensor_tensor(out=out[:], in0=out[:], in1=inj_psum, op=ADD)
+            nc.sync.dma_start(out=sharp_v[s // 2, s % 2], in_=out[:])
+
+        def finish_piece(s, n):
             cols = slice(512 * n, 512 * (n + 1))
             out = out_sb[s % OUT_SLOTS]
-            product = pool_slot(s) if n < pool_pieces(s) else out[:]
-            nc.vector.tensor_tensor(
-                out=out[:, cols], in0=product[:, cols], in1=inj_banks[(4 * s + n) % INJ_BANKS][:], op=ADD
-            )
-            if s == PAIRS - 1:
-                nc.sync.dma_start(out=sharp_v[s // 2, s % 2][:, cols], in_=out[:, cols])
-            elif n % 2 == 1:
-                row = slice(K * (n // 2), K * (n // 2 + 1))
-                nc.sync.dma_start(out=sharp_v[s // 2, s % 2][:, row], in_=out[:, row])
+            nc.vector.tensor_tensor(out=out[:, cols], in0=out[:, cols], in1=inj_bank(s, n), op=ADD)
+            nc.sync.dma_start(out=sharp_v[s // 2, s % 2][:, cols], in_=out[:, cols])
 
-        coarse_banks = turn_banks[1:3] + int_banks
+        coarse_banks = [turn_banks[1]] + int_banks + [turn_banks[0]]
 
         def coarse_pass(r, g):
+            mtf_c, mtf_s = operand(*mtf_place[r], P * g, P)
+            dy_c, dy_s = operand(*dy_place[g], 0, C)
             nc.tensor.matmul_mx(
-                out=coarse_banks[r][:],
-                lhsT=mtf_c[r][:, P * g : P * (g + 1)].bitcast(FP8X4),
-                lhsT_scale=mtf_s[r][:, P * g : P * (g + 1)],
-                rhs=dy_c[g][:].bitcast(FP8X4),
-                rhs_scale=dy_s[g][:],
+                out=coarse_banks[r],
+                lhsT=mtf_c,
+                lhsT_scale=mtf_s,
+                rhs=dy_c,
+                rhs_scale=dy_s,
                 start=(g == 0),
                 stop=(g == GROUPS - 1),
             )
@@ -317,106 +316,99 @@ def tile_pansharpen_detail_injection_s8_kernel(
                 coarse_pass(r, g)
 
         def coarse_out(r, engine_copy):
-            engine_copy(out=res[r][:], in_=coarse_banks[r][:])
+            engine_copy(
+                out=res[r][:].rearrange("p (m u e) -> p m u e", u=2, e=2),
+                in_=coarse_banks[r].rearrange("p (u m e) -> p m u e", u=2, e=2),
+            )
             nc.sync.dma_start(out=coarse_v[r], in_=res[r][:])
 
         build_diag()
-        interleave(nc.vector.tensor_copy, mix_il[0][:], mix_raw[0][:])
+        interleave_mix(0)
+        turn_bands(0, 0, turn_banks[0])
+        turn_bands(0, 1, turn_banks[1])
+        quantize_mix(0)
+        interleave_mix(1)
+        widen_mtf(0)
         spread_radio(0)
         spread_radio(1)
-        turn_bands(0, 0, turn_banks[0])
-        turn_bands(0, 1, turn_banks[2])
-        quantize(mix_c[0][:], mix_s[0][:], mix_il[0][:])
-        widen_mtf(0)
         widen_mtf(1)
-        interleave(nc.vector.tensor_copy, mix_il[1][:], mix_raw[1][:])
-        quantize_bands(0)
-        quantize(mix_c[1][:], mix_s[1][:], mix_il[1][:])
+        quantize_call(0)
+        quantize_mix(1)
         products_pool(0)
-        for n in (2, 3):
-            diag_matmuls(0, n, inj_banks[n - 2])
-        turn_mtf(0)
-        scale_mtf(0)
-        turn_bands(1, 0, turn_banks[0])
+        products_diag(0, head_banks)
+        turn_mtf(0, head_banks[2])
+        scale_mtf(0, head_banks[2])
         intensity(0, 0)
         intensity(0, 1)
-        diag_out(0, 2, inj_banks[0])
-        turn_bands(1, 1, turn_banks[2])
-        diag_out(0, 3, inj_banks[1])
+        turn_bands(1, 0, turn_banks[0])
+        turn_mtf(1, head_banks[3])
+        turn_bands(1, 1, turn_banks[1])
         subtract(0, 0)
         subtract(0, 1)
-        turn_mtf(1)
-        turn_bands(2, 0, turn_banks[0])
-        turn_bands(2, 1, inj_banks[2])
-        quantize_bands(1)
-        quantize_mtf(0)
-        scale_mtf(1)
-        intensity(1, 0)
-        turn_detail(0)
-        products_diag(1)
-        intensity(1, 1)
+        scale_mtf(1, head_banks[3])
+        turn_bands(2, 0, head_banks[0])
+        turn_bands(2, 1, head_banks[1])
+        turn_detail(0, head_banks[2])
+        quantize_call(1)
+        turn_bands(3, 0, turn_banks[0])
+        products_diag(1, [head_banks[3], turn_banks[1]])
         widen_mtf(2)
+        intensity(1, 0)
+        intensity(1, 1)
 
         last = PAIRS - 1
         for s in range(1, PAIRS):
-            turning = s + 2 <= last
-            if s < last:
-                quantize_bands(s + 1)
-            if s >= 3:
-                quantize_dy((s - 3) // 2, (s - 3) % 2)
-            if s == last:
-                quantize_dy((s - 3) // 2, 1)
-            quantize_mtf(s)
+            if s == 1:
+                quantize_call(s + 1)
             quantize_dx(s - 1)
+            if s > 1:
+                quantize_call(s + 1)
             products_pool(s)
-            if turning:
-                turn_bands(s + 2, 0, turn_banks[0])
-                turn_bands(s + 2, 1, turn_banks[2])
-            if s >= 2 and (turning or s % 2 == 0):
-                interleave_dy((s - 2) // 2, s % 2)
-            if s % 2 == 0 and not turning:
-                interleave_dy((s - 2) // 2, 1)
-            for n in range(INJ_BANKS):
+            for n in range(4):
                 inject(s - 1, n)
+            if 2 <= s < last:
+                interleave_dy((s - 2) // 2, s % 2)
+            if s == last - 1:
+                interleave_dy((s - 2) // 2, 1)
+            if s + 2 <= last:
+                turn_bands(s + 2, 1, turn_banks[1])
             subtract(s, 0)
             if s < last:
                 intensity(s + 1, 0)
             else:
                 coarse_early(0)
             subtract(s, 1)
-            finish(s - 1, 0)
-            inject(s - 1, 3)
-            if s < last:
-                turn_mtf(s + 1)
-            else:
+            if s == last:
                 interleave_dy(GROUPS - 1, 0)
-            turn_detail(s)
-            for n in range(1, 4):
-                finish(s - 1, n)
+            turn_detail(s, turn_banks[0])
             if s < last:
-                scale_mtf(s + 1)
-                intensity(s + 1, 1)
-                products_diag(s + 1)
-            if turning:
+                turn_mtf(s + 1, turn_banks[1])
+                finish(s - 1)
+                scale_mtf(s + 1, turn_banks[1])
+            if s + 3 <= last:
+                turn_bands(s + 3, 0, turn_banks[0])
+            if s + 2 <= last:
                 widen_mtf(s + 2)
+            if s < last:
+                intensity(s + 1, 1)
+            if s == last - 1:
+                products_diag(last, turn_banks)
 
-        interleave_dy(GROUPS - 1, 1)
         coarse_early(1)
         coarse_early(2)
-        quantize_dy(GROUPS - 1, 0)
-        quantize_dx(last)
-        for n in range(INJ_BANKS):
-            inject(last, n)
+        finish_piece(last - 1, 0)
+        finish_piece(last - 1, 1)
+        interleave_dy(GROUPS - 1, 1, nc.vector.tensor_copy)
+        finish_piece(last - 1, 2)
         coarse_early(3)
-        finish(last, 0)
-        inject(last, 3)
-        quantize_dy(GROUPS - 1, 1)
+        quantize_call(CALLS - 1)
+        quantize_dx(last)
+        finish_piece(last - 1, 3)
         for r in range(4):
-            coarse_pass(r, GROUPS - 1)
-        finish(last, 1)
-        finish(last, 2)
-        coarse_out(0, nc.scalar.copy)
-        finish(last, 3)
-        coarse_out(1, nc.scalar.copy)
-        coarse_out(3, nc.vector.tensor_copy)
-        coarse_out(2, nc.scalar.copy)
+            if r % 2 == 0:
+                coarse_pass(r, GROUPS - 1)
+                coarse_pass(r + 1, GROUPS - 1)
+                inject(last, r)
+                inject(last, r + 1)
+            coarse_out(r, nc.scalar.copy)
+            finish_piece(last, r)

@@ -60,6 +60,7 @@ def tile_pansharpen_detail_injection_s8_kernel(
         ident_b = one("ident_b", P, BF16)
         ones_b = one("ones_b", P, BF16)
         scale_col = one("scale_col", 4 * GROUPS, F32)
+        scale_wide = tiles("scale_wide", HALVES, 1024, F32)
         radio_col = one("radio_col", 8, BF16)
         radio_bc = one("radio_bc", K, BF16)
         diag = one("diag", K, BF16)
@@ -106,11 +107,11 @@ def tile_pansharpen_detail_injection_s8_kernel(
             load(pan_sb[s][:], pan_v[s // 2, s % 2])
 
         load(radio_col[:].rearrange("p (h j) -> p h j", j=4), radio.rearrange("(h p j) -> p h j", p=P, j=4))
+        load(scale_col[:].rearrange("p (g t) -> p g t", t=4), mtf_scale.rearrange("o (g p t) -> p (o g) t", p=P, t=4))
         load(mix_raw[0][:], mix_v[0])
         load_bands(0)
         load(mix_raw[1][:], mix_v[1])
         load(codes[0][:], mtf_v[0])
-        load(scale_col[:].rearrange("p (g t) -> p g t", t=4), mtf_scale.rearrange("o (g p t) -> p (o g) t", p=P, t=4))
         load_pan(0)
         load_bands(1)
         load_bands(2)
@@ -181,19 +182,25 @@ def tile_pansharpen_detail_injection_s8_kernel(
             start = 1024 * (n % 2)
             nc.scalar.copy(out=mtf_b[n % 2][:], in_=codes[n // 2][:, start : start + 1024].bitcast(FP8))
 
+        def spread_scale(hh):
+            scales = scale_col[:, 8 * hh : 8 * (hh + 1)].rearrange("p (i j) -> p i j", i=2)
+            nc.scalar.copy(
+                out=scale_wide[hh][:].rearrange("p (i x j) -> p i x j", i=2, j=4),
+                in_=scales.unsqueeze(2).to_broadcast([P, 2, P, 4]),
+            )
+
         def turn_mtf(n, bank):
             words = mtf_b[n % 2][:].bitcast(F32)
-            for u in range(2):
-                for i in range(2):
-                    c0 = 256 * u + P * i
-                    nc.tensor.transpose(bank[:, c0 : c0 + P], words[:, 256 * i + u : 256 * (i + 1) : 2], ident[:])
+            for i in range(2):
+                for u in range(2):
+                    every_2nd = slice(256 * i + u, 256 * (i + 1), 2)
+                    nc.tensor.transpose(bank[:, every_2nd], words[:, every_2nd], ident[:])
 
         def scale_mtf(n, bank):
-            scales = scale_col[:, 8 * (n % 2) : 8 * (n % 2 + 1)].rearrange("p (i u e) -> p i u e", i=2, u=2)
             nc.vector.tensor_tensor(
-                out=staged(*mtf_place[n // 2], 1024 * (n % 2), 1024).rearrange("p (i x u e) -> p i x u e", i=2, u=2, e=2),
-                in0=bank.bitcast(BF16).rearrange("p (u i x e) -> p i x u e", i=2, u=2, e=2),
-                in1=scales.unsqueeze(2).to_broadcast([P, 2, P, 2, 2]),
+                out=staged(*mtf_place[n // 2], 1024 * (n % 2), 1024),
+                in0=bank.bitcast(BF16),
+                in1=scale_wide[n % 2][:],
                 op=MULT,
             )
 
@@ -323,6 +330,8 @@ def tile_pansharpen_detail_injection_s8_kernel(
             nc.sync.dma_start(out=coarse_v[r], in_=res[r][:])
 
         build_diag()
+        spread_scale(0)
+        spread_scale(1)
         interleave_mix(0)
         turn_bands(0, 0, turn_banks[0])
         turn_bands(0, 1, turn_banks[1])
@@ -364,14 +373,16 @@ def tile_pansharpen_detail_injection_s8_kernel(
             if s > 1:
                 quantize_call(s + 1)
             products_pool(s)
+            if 1 < s <= last - 2:
+                turn_bands(s + 2, 1, turn_banks[1])
             for n in range(4):
                 inject(s - 1, n)
+            if s == 1:
+                turn_bands(s + 2, 1, turn_banks[1])
             if 2 <= s < last:
                 interleave_dy((s - 2) // 2, s % 2)
             if s == last - 1:
                 interleave_dy((s - 2) // 2, 1)
-            if s + 2 <= last:
-                turn_bands(s + 2, 1, turn_banks[1])
             subtract(s, 0)
             if s < last:
                 intensity(s + 1, 0)

@@ -24,7 +24,8 @@ BANK = 512
 GROUPS = M // 512
 HALVES = K // 512
 PAIRS = M // (2 * P)
-SHARED_PAIRS = (0, 1, PAIRS - 1)
+SHARED_PAIRS = (0, PAIRS - 1)
+HEAD_UNITS = 2
 CALLS = PAIRS + 2
 STAGE_SLOTS = 3
 OUT_SLOTS = 4
@@ -161,7 +162,7 @@ def tile_pansharpen_detail_injection_s8_kernel(
         def quantize_mix(h):
             quantize(mix_c[h][:], mix_s[h][:], mix_il[h])
 
-        mtf_place = [(1, 1)] + [(2 * r + 2, 1) for r in range(1, 4)]
+        mtf_place = [(2 * r + 2, 1) for r in range(4)]
         dy_place = [(5, 1), (7, 1), (8, 0), (9, 0)]
 
         def staged(call, half, start, width):
@@ -189,18 +190,25 @@ def tile_pansharpen_detail_injection_s8_kernel(
                 in_=scales.unsqueeze(2).to_broadcast([P, 2, P, 4]),
             )
 
+        def bank_words(n, bank):
+            if n < HEAD_UNITS:
+                return bank.rearrange("p (u i x) -> p i x u", u=2, i=2)
+            return bank.rearrange("p (i x u) -> p i x u", u=2, i=2)
+
         def turn_mtf(n, bank):
             words = mtf_b[n % 2][:].bitcast(F32)
-            for i in range(2):
-                for u in range(2):
-                    every_2nd = slice(256 * i + u, 256 * (i + 1), 2)
-                    nc.tensor.transpose(bank[:, every_2nd], words[:, every_2nd], ident[:])
+            for u in range(2):
+                for i in range(2):
+                    nc.tensor.transpose(
+                        bank_words(n, bank)[:, i, :, u], words[:, 256 * i + u : 256 * (i + 1) : 2], ident[:]
+                    )
 
         def scale_mtf(n, bank):
+            pairs = "p (i x u e) -> p i x u e"
             nc.vector.tensor_tensor(
-                out=staged(*mtf_place[n // 2], 1024 * (n % 2), 1024),
-                in0=bank.bitcast(BF16),
-                in1=scale_wide[n % 2][:],
+                out=staged(*mtf_place[n // 2], 1024 * (n % 2), 1024).rearrange(pairs, i=2, u=2, e=2),
+                in0=bank_words(n, bank).unsqueeze(4).bitcast(BF16),
+                in1=scale_wide[n % 2][:].rearrange(pairs, i=2, u=2, e=2),
                 op=MULT,
             )
 
@@ -344,41 +352,44 @@ def tile_pansharpen_detail_injection_s8_kernel(
         quantize_call(0)
         quantize_mix(1)
         products_pool(0)
-        products_diag(0, head_banks)
+        for n in (2, 3):
+            diag_matmuls(0, n, head_banks[n - 2])
         turn_mtf(0, head_banks[2])
         scale_mtf(0, head_banks[2])
+        turn_bands(1, 0, turn_banks[0])
+        turn_bands(1, 1, turn_banks[1])
         intensity(0, 0)
         intensity(0, 1)
-        turn_bands(1, 0, turn_banks[0])
         turn_mtf(1, head_banks[3])
-        turn_bands(1, 1, turn_banks[1])
         subtract(0, 0)
         subtract(0, 1)
-        scale_mtf(1, head_banks[3])
-        turn_bands(2, 0, head_banks[0])
-        turn_bands(2, 1, head_banks[1])
-        turn_detail(0, head_banks[2])
         quantize_call(1)
-        turn_bands(3, 0, turn_banks[0])
-        products_diag(1, [head_banks[3], turn_banks[1]])
-        widen_mtf(2)
+        scale_mtf(1, head_banks[3])
+        diag_out(0, 2, head_banks[0])
+        turn_bands(2, 0, turn_banks[0])
+        turn_bands(2, 1, turn_banks[1])
+        turn_detail(0, head_banks[2])
+        diag_out(0, 3, head_banks[1])
         intensity(1, 0)
         intensity(1, 1)
+        widen_mtf(2)
+        turn_bands(3, 0, turn_banks[0])
+        turn_bands(3, 1, turn_banks[1])
 
         last = PAIRS - 1
         for s in range(1, PAIRS):
             if s == 1:
-                quantize_call(s + 1)
+                quantize_call(s + 1, 0, 2048)
             quantize_dx(s - 1)
-            if s > 1:
+            if s == 1:
+                quantize_call(s + 1, 2048, 2048)
+            else:
                 quantize_call(s + 1)
             products_pool(s)
             if 1 < s <= last - 2:
                 turn_bands(s + 2, 1, turn_banks[1])
             for n in range(4):
                 inject(s - 1, n)
-            if s == 1:
-                turn_bands(s + 2, 1, turn_banks[1])
             if 2 <= s < last:
                 interleave_dy((s - 2) // 2, s % 2)
             if s == last - 1:

@@ -25,7 +25,7 @@ GROUPS = M // 512
 HALVES = K // 512
 PAIRS = M // (2 * P)
 SHARED_PAIRS = (0, PAIRS - 1)
-HEAD_UNITS = 2
+HEAD_UNITS = 3
 CALLS = PAIRS + 2
 STAGE_SLOTS = 3
 OUT_SLOTS = 4
@@ -55,7 +55,7 @@ def tile_pansharpen_detail_injection_s8_kernel(
         turn_banks = [bank_tile(f"turn_bank{i}", 6 + i) for i in range(2)]
 
         def inj_bank(s, n):
-            return inj_psum[:, BANK * n : BANK * (n + 1)] if s < PAIRS - 2 else tail_banks[n]
+            return inj_psum[:, BANK * n : BANK * (n + 1)] if s < PAIRS - 3 else tail_banks[n]
 
         ident = one("ident", P, F32)
         ident_b = one("ident_b", P, BF16)
@@ -96,7 +96,6 @@ def tile_pansharpen_detail_injection_s8_kernel(
         make_identity(nc, ident[:])
         nc.gpsimd.memset(ones_b[:], 1.0)
         nc.vector.memset(gain_s[:].bitcast(I32), 0)
-        nc.scalar.copy(out=ident_b[:], in_=ident[:])
 
         def load(dst, src):
             nc.sync.dma_start(out=dst, in_=src)
@@ -109,24 +108,27 @@ def tile_pansharpen_detail_injection_s8_kernel(
 
         load(radio_col[:].rearrange("p (h j) -> p h j", j=4), radio.rearrange("(h p j) -> p h j", p=P, j=4))
         load(scale_col[:].rearrange("p (g t) -> p g t", t=4), mtf_scale.rearrange("o (g p t) -> p (o g) t", p=P, t=4))
+        load(codes[0][:], mtf_v[0])
         load(mix_raw[0][:], mix_v[0])
         load_bands(0)
         load(mix_raw[1][:], mix_v[1])
-        load(codes[0][:], mtf_v[0])
         load_pan(0)
         load_bands(1)
-        load_bands(2)
         load(codes[1][:], mtf_v[1])
+        load_bands(2)
         load_pan(1)
+        load_bands(3)
         load(gain_w[:].bitcast(I32), gain_words[0].bitcast(I32))
         for q in range(4):
             load(gain_s[32 * q : 32 * q + 4, :].bitcast(I32), gain_scales[0][4 * q : 4 * q + 4, :].bitcast(I32))
-        for s in range(3, PAIRS):
-            load_bands(s)
-            load_pan(s - 1)
-            if s < 5:
-                load(codes[s - 1][:], mtf_v[s - 1])
-        load_pan(PAIRS - 1)
+        for s in range(2, PAIRS):
+            load_pan(s)
+            if s + 2 < PAIRS:
+                load_bands(s + 2)
+            if s < 4:
+                load(codes[s][:], mtf_v[s])
+
+        nc.scalar.copy(out=ident_b[:], in_=ident[:])
 
         def turn_out(bank, dst):
             nc.scalar.copy(
@@ -153,17 +155,18 @@ def tile_pansharpen_detail_injection_s8_kernel(
                 in_=bank.rearrange("p (j m) -> p m j", j=4),
             )
 
-        def interleave_mix(h):
+        def interleave_mix(h, u):
             nc.vector.tensor_copy(
-                out=mix_il[h].rearrange("p (u m e j) -> p m j u e", u=2, e=2, j=4),
-                in_=mix_raw[h][:].rearrange("p (j m u e) -> p m j u e", u=2, e=2, j=4),
+                out=mix_il[h][:, K * u : K * (u + 1)].rearrange("p (m e j) -> p m j e", e=2, j=4),
+                in_=mix_raw[h][:].rearrange("p (j m u e) -> p u m j e", u=2, e=2, j=4)[:, u],
             )
 
-        def quantize_mix(h):
-            quantize(mix_c[h][:], mix_s[h][:], mix_il[h])
+        def quantize_mix(h, u):
+            cols = slice(256 * u, 256 * (u + 1))
+            quantize(mix_c[h][:, cols], mix_s[h][:, cols], mix_il[h][:, K * u : K * (u + 1)])
 
-        mtf_place = [(2 * r + 2, 1) for r in range(4)]
-        dy_place = [(5, 1), (7, 1), (8, 0), (9, 0)]
+        mtf_place = [(2, 1), (3, 1), (5, 1), (7, 1)]
+        dy_place = [(4, 1), (6, 1), (8, 0), (9, 0)]
 
         def staged(call, half, start, width):
             first = 2048 * half + start
@@ -203,12 +206,19 @@ def tile_pansharpen_detail_injection_s8_kernel(
                         bank_words(n, bank)[:, i, :, u], words[:, 256 * i + u : 256 * (i + 1) : 2], ident[:]
                     )
 
+        pairs = "p (i x u e) -> p i x u e"
+
+        def scales(n):
+            if n < HEAD_UNITS:
+                four = scale_col[:, 8 * (n % 2) : 8 * (n % 2 + 1)].rearrange("p (i u e) -> p i u e", i=2, u=2)
+                return four.unsqueeze(2).to_broadcast([P, 2, P, 2, 2])
+            return scale_wide[n % 2][:].rearrange(pairs, i=2, u=2, e=2)
+
         def scale_mtf(n, bank):
-            pairs = "p (i x u e) -> p i x u e"
             nc.vector.tensor_tensor(
                 out=staged(*mtf_place[n // 2], 1024 * (n % 2), 1024).rearrange(pairs, i=2, u=2, e=2),
                 in0=bank_words(n, bank).unsqueeze(4).bitcast(BF16),
-                in1=scale_wide[n % 2][:].rearrange(pairs, i=2, u=2, e=2),
+                in1=scales(n),
                 op=MULT,
             )
 
@@ -326,9 +336,10 @@ def tile_pansharpen_detail_injection_s8_kernel(
                 stop=(g == GROUPS - 1),
             )
 
-        def coarse_early(r):
-            for g in range(GROUPS - 1):
-                coarse_pass(r, g)
+        def coarse_passes(row_tiles, groups):
+            for r in row_tiles:
+                for g in groups:
+                    coarse_pass(r, g)
 
         def coarse_out(r, engine_copy):
             engine_copy(
@@ -338,46 +349,53 @@ def tile_pansharpen_detail_injection_s8_kernel(
             nc.sync.dma_start(out=coarse_v[r], in_=res[r][:])
 
         build_diag()
-        spread_scale(0)
-        spread_scale(1)
-        interleave_mix(0)
-        turn_bands(0, 0, turn_banks[0])
-        turn_bands(0, 1, turn_banks[1])
-        quantize_mix(0)
-        interleave_mix(1)
         widen_mtf(0)
+        widen_mtf(1)
         spread_radio(0)
         spread_radio(1)
-        widen_mtf(1)
-        quantize_call(0)
-        quantize_mix(1)
-        products_pool(0)
-        for n in (2, 3):
-            diag_matmuls(0, n, head_banks[n - 2])
+        interleave_mix(0, 0)
+        interleave_mix(0, 1)
+        quantize_mix(0, 0)
+        quantize_mix(0, 1)
         turn_mtf(0, head_banks[2])
         scale_mtf(0, head_banks[2])
+        turn_bands(0, 0, turn_banks[0])
+        turn_bands(0, 1, turn_banks[1])
+        turn_mtf(1, head_banks[3])
+        interleave_mix(1, 0)
+        interleave_mix(1, 1)
+        quantize_mix(1, 0)
+        quantize_call(0)
+        quantize_mix(1, 1)
+        products_pool(0)
+        scale_mtf(1, head_banks[3])
+        spread_scale(1)
+        widen_mtf(2)
+        for n in (2, 3):
+            diag_matmuls(0, n, head_banks[n - 2])
         turn_bands(1, 0, turn_banks[0])
         turn_bands(1, 1, turn_banks[1])
+        diag_out(0, 2, head_banks[0])
         intensity(0, 0)
         intensity(0, 1)
-        turn_mtf(1, head_banks[3])
         subtract(0, 0)
         subtract(0, 1)
         quantize_call(1)
-        scale_mtf(1, head_banks[3])
-        diag_out(0, 2, head_banks[0])
+        turn_mtf(2, head_banks[3])
+        scale_mtf(2, head_banks[3])
         turn_bands(2, 0, turn_banks[0])
         turn_bands(2, 1, turn_banks[1])
         turn_detail(0, head_banks[2])
         diag_out(0, 3, head_banks[1])
         intensity(1, 0)
         intensity(1, 1)
-        widen_mtf(2)
+        widen_mtf(3)
         turn_bands(3, 0, turn_banks[0])
         turn_bands(3, 1, turn_banks[1])
+        spread_scale(0)
 
         last = PAIRS - 1
-        for s in range(1, PAIRS):
+        for s in range(1, last - 1):
             if s == 1:
                 quantize_call(s + 1, 0, 2048)
             quantize_dx(s - 1)
@@ -386,51 +404,67 @@ def tile_pansharpen_detail_injection_s8_kernel(
             else:
                 quantize_call(s + 1)
             products_pool(s)
-            if 1 < s <= last - 2:
+            if s > 1:
                 turn_bands(s + 2, 1, turn_banks[1])
             for n in range(4):
                 inject(s - 1, n)
-            if 2 <= s < last:
-                interleave_dy((s - 2) // 2, s % 2)
-            if s == last - 1:
+            if s % 2 == 0:
                 interleave_dy((s - 2) // 2, 1)
             subtract(s, 0)
-            if s < last:
-                intensity(s + 1, 0)
-            else:
-                coarse_early(0)
+            intensity(s + 1, 0)
             subtract(s, 1)
-            if s == last:
-                interleave_dy(GROUPS - 1, 0)
             turn_detail(s, turn_banks[0])
-            if s < last:
-                turn_mtf(s + 1, turn_banks[1])
-                finish(s - 1)
-                scale_mtf(s + 1, turn_banks[1])
+            if s % 2 == 1:
+                interleave_dy(s // 2, 0)
+            turn_mtf(s + 2, turn_banks[1])
+            finish(s - 1)
+            scale_mtf(s + 2, turn_banks[1])
             if s + 3 <= last:
                 turn_bands(s + 3, 0, turn_banks[0])
-            if s + 2 <= last:
-                widen_mtf(s + 2)
-            if s < last:
-                intensity(s + 1, 1)
-            if s == last - 1:
-                products_diag(last, turn_banks)
+                widen_mtf(s + 3)
+            intensity(s + 1, 1)
 
-        coarse_early(1)
-        coarse_early(2)
+        quantize_dx(last - 2)
+        quantize_call(last)
+        products_pool(last - 1)
+        interleave_dy(GROUPS - 2, 1)
+        products_diag(last, turn_banks[::-1])
+        for n in range(4):
+            inject(last - 2, n)
+        for t in range(2):
+            subtract(last - 1, t)
+            intensity(last, t)
+        turn_detail(last - 1, turn_banks[0])
+        coarse_passes([0], range(2))
+        finish_piece(last - 2, 0)
+        finish_piece(last - 2, 1)
+        subtract(last, 0)
+        coarse_passes([1], range(2))
+        subtract(last, 1)
+        interleave_dy(GROUPS - 1, 0)
+        turn_detail(last, turn_banks[0])
+        interleave_dy(GROUPS - 1, 1)
+        coarse_passes([2], range(2))
+        finish_piece(last - 2, 2)
+        finish_piece(last - 2, 3)
+        quantize_dx(last - 1)
+        quantize_call(CALLS - 2)
+        products_pool(last)
+        for n in range(4):
+            inject(last - 1, n)
+        coarse_passes(range(3), [2])
+        coarse_passes([3], range(3))
         finish_piece(last - 1, 0)
         finish_piece(last - 1, 1)
-        interleave_dy(GROUPS - 1, 1, nc.vector.tensor_copy)
         finish_piece(last - 1, 2)
-        coarse_early(3)
-        quantize_call(CALLS - 1)
         quantize_dx(last)
+        quantize_call(CALLS - 1)
         finish_piece(last - 1, 3)
         for r in range(4):
-            if r % 2 == 0:
-                coarse_pass(r, GROUPS - 1)
-                coarse_pass(r + 1, GROUPS - 1)
-                inject(last, r)
-                inject(last, r + 1)
-            coarse_out(r, nc.scalar.copy)
+            inject(last, r)
+            if r > 0:
+                coarse_pass(r - 1, GROUPS - 1)
+        coarse_pass(3, GROUPS - 1)
+        for r in range(4):
             finish_piece(last, r)
+            coarse_out(r, nc.scalar.copy)

@@ -208,17 +208,11 @@ def tile_pansharpen_detail_injection_s8_kernel(
 
         pairs = "p (i x u e) -> p i x u e"
 
-        def scales(n):
-            if n < HEAD_UNITS:
-                four = scale_col[:, 8 * (n % 2) : 8 * (n % 2 + 1)].rearrange("p (i u e) -> p i u e", i=2, u=2)
-                return four.unsqueeze(2).to_broadcast([P, 2, P, 2, 2])
-            return scale_wide[n % 2][:].rearrange(pairs, i=2, u=2, e=2)
-
         def scale_mtf(n, bank):
             nc.vector.tensor_tensor(
                 out=staged(*mtf_place[n // 2], 1024 * (n % 2), 1024).rearrange(pairs, i=2, u=2, e=2),
                 in0=bank_words(n, bank).unsqueeze(4).bitcast(BF16),
-                in1=scales(n),
+                in1=scale_wide[n % 2][:].rearrange(pairs, i=2, u=2, e=2),
                 op=MULT,
             )
 
@@ -349,6 +343,7 @@ def tile_pansharpen_detail_injection_s8_kernel(
             nc.sync.dma_start(out=coarse_v[r], in_=res[r][:])
 
         build_diag()
+        spread_scale(0)
         widen_mtf(0)
         widen_mtf(1)
         spread_radio(0)
@@ -368,8 +363,8 @@ def tile_pansharpen_detail_injection_s8_kernel(
         quantize_call(0)
         quantize_mix(1, 1)
         products_pool(0)
-        scale_mtf(1, head_banks[3])
         spread_scale(1)
+        scale_mtf(1, head_banks[3])
         widen_mtf(2)
         for n in (2, 3):
             diag_matmuls(0, n, head_banks[n - 2])
@@ -392,7 +387,6 @@ def tile_pansharpen_detail_injection_s8_kernel(
         widen_mtf(3)
         turn_bands(3, 0, turn_banks[0])
         turn_bands(3, 1, turn_banks[1])
-        spread_scale(0)
 
         last = PAIRS - 1
         for s in range(1, last - 1):

@@ -25,7 +25,6 @@ GROUPS = M // 512
 HALVES = K // 512
 PAIRS = M // (2 * P)
 SHARED_PAIRS = (0, PAIRS - 1)
-HEAD_UNITS = 3
 CALLS = PAIRS + 2
 STAGE_SLOTS = 3
 OUT_SLOTS = 4
@@ -193,25 +192,18 @@ def tile_pansharpen_detail_injection_s8_kernel(
                 in_=scales.unsqueeze(2).to_broadcast([P, 2, P, 4]),
             )
 
-        def bank_words(n, bank):
-            if n < HEAD_UNITS:
-                return bank.rearrange("p (u i x) -> p i x u", u=2, i=2)
-            return bank.rearrange("p (i x u) -> p i x u", u=2, i=2)
-
         def turn_mtf(n, bank):
             words = mtf_b[n % 2][:].bitcast(F32)
             for u in range(2):
                 for i in range(2):
-                    nc.tensor.transpose(
-                        bank_words(n, bank)[:, i, :, u], words[:, 256 * i + u : 256 * (i + 1) : 2], ident[:]
-                    )
-
-        pairs = "p (i x u e) -> p i x u e"
+                    first = 256 * u + P * i
+                    nc.tensor.transpose(bank[:, first : first + P], words[:, 256 * i + u : 256 * (i + 1) : 2], ident[:])
 
         def scale_mtf(n, bank):
+            pairs = "p (i x u e) -> p i x u e"
             nc.vector.tensor_tensor(
                 out=staged(*mtf_place[n // 2], 1024 * (n % 2), 1024).rearrange(pairs, i=2, u=2, e=2),
-                in0=bank_words(n, bank).unsqueeze(4).bitcast(BF16),
+                in0=bank.bitcast(BF16).rearrange("p (u i x e) -> p i x u e", i=2, u=2, e=2),
                 in1=scale_wide[n % 2][:].rearrange(pairs, i=2, u=2, e=2),
                 op=MULT,
             )
@@ -451,9 +443,9 @@ def tile_pansharpen_detail_injection_s8_kernel(
         finish_piece(last - 1, 0)
         finish_piece(last - 1, 1)
         finish_piece(last - 1, 2)
+        finish_piece(last - 1, 3)
         quantize_dx(last)
         quantize_call(CALLS - 1)
-        finish_piece(last - 1, 3)
         for r in range(4):
             inject(last, r)
             if r > 0:

@@ -62,7 +62,7 @@ def tile_pansharpen_detail_injection_s8_kernel(
         scale_col = one("scale_col", 4 * GROUPS, F32)
         scale_wide = tiles("scale_wide", HALVES, 1024, F32)
         radio_col = one("radio_col", 8, BF16)
-        radio_bc = one("radio_bc", K, BF16)
+        radio_bc = one("radio_bc", K + 512, BF16)
         diag = one("diag", K, BF16)
         gain_w = one("gain_w", 2 * K, U8)
         gain_s = one("gain_s", K, U8)
@@ -153,6 +153,9 @@ def tile_pansharpen_detail_injection_s8_kernel(
                 out=radio_bc[:, 512 * h : 512 * (h + 1)].rearrange("p (m j) -> p m j", j=4),
                 in_=bank.rearrange("p (j m) -> p m j", j=4),
             )
+
+        def repeat_radio():
+            nc.scalar.copy(out=radio_bc[:, K : K + 512], in_=radio_bc[:, 0:512])
 
         def interleave_mix(h, u):
             nc.vector.tensor_copy(
@@ -257,12 +260,9 @@ def tile_pansharpen_detail_injection_s8_kernel(
             )
 
         def products_pool(s):
-            rows = 1 if s in SHARED_PAIRS else 2
+            cols = slice(0, K if s in SHARED_PAIRS else K + 512)
             nc.gpsimd.tensor_tensor(
-                out=out_sb[s % OUT_SLOTS][:, 0 : rows * K].rearrange("p (t k) -> p t k", t=rows),
-                in0=bands_sb[s][:, 0 : rows * K].rearrange("p (t k) -> p t k", t=rows),
-                in1=radio_bc[:].unsqueeze(1).to_broadcast([P, rows, K]),
-                op=MULT,
+                out=out_sb[s % OUT_SLOTS][:, cols], in0=bands_sb[s][:, cols], in1=radio_bc[:, cols], op=MULT
             )
 
         def diag_matmuls(s, n, bank):
@@ -374,11 +374,13 @@ def tile_pansharpen_detail_injection_s8_kernel(
         turn_bands(2, 1, turn_banks[1])
         turn_detail(0, head_banks[2])
         diag_out(0, 3, head_banks[1])
+        repeat_radio()
         intensity(1, 0)
         intensity(1, 1)
+        diag_matmuls(1, 3, turn_banks[1])
+        diag_out(1, 3, turn_banks[1])
         widen_mtf(3)
         turn_bands(3, 0, turn_banks[0])
-        turn_bands(3, 1, turn_banks[1])
 
         last = PAIRS - 1
         for s in range(1, last - 1):
@@ -390,25 +392,27 @@ def tile_pansharpen_detail_injection_s8_kernel(
             else:
                 quantize_call(s + 1)
             products_pool(s)
-            if s > 1:
-                turn_bands(s + 2, 1, turn_banks[1])
             for n in range(4):
                 inject(s - 1, n)
             if s % 2 == 0:
                 interleave_dy((s - 2) // 2, 1)
+            turn_mtf(s + 2, turn_banks[1])
             subtract(s, 0)
-            intensity(s + 1, 0)
+            diag_matmuls(s + 1, 3, int_banks[0])
+            diag_out(s + 1, 3, int_banks[0])
             subtract(s, 1)
+            turn_bands(s + 2, 1, int_banks[1])
             turn_detail(s, turn_banks[0])
+            if s + 3 <= last:
+                widen_mtf(s + 3)
             if s % 2 == 1:
                 interleave_dy(s // 2, 0)
-            turn_mtf(s + 2, turn_banks[1])
+            intensity(s + 1, 0)
+            intensity(s + 1, 1)
             finish(s - 1)
             scale_mtf(s + 2, turn_banks[1])
             if s + 3 <= last:
                 turn_bands(s + 3, 0, turn_banks[0])
-                widen_mtf(s + 3)
-            intensity(s + 1, 1)
 
         quantize_dx(last - 2)
         quantize_call(last)

@@ -25,6 +25,7 @@ GROUPS = M // 512
 HALVES = K // 512
 PAIRS = M // (2 * P)
 SHARED_PAIRS = (0, PAIRS - 1)
+HEAD_UNITS = 3
 CALLS = PAIRS + 2
 STAGE_SLOTS = 3
 OUT_SLOTS = 4
@@ -195,18 +196,25 @@ def tile_pansharpen_detail_injection_s8_kernel(
                 in_=scales.unsqueeze(2).to_broadcast([P, 2, P, 4]),
             )
 
-        def turn_mtf(n, bank):
+        def bank_words(n, bank):
+            if n < HEAD_UNITS:
+                return bank.rearrange("p (u i x) -> p i x u", u=2, i=2)
+            return bank.rearrange("p (i x u) -> p i x u", u=2, i=2)
+
+        def turn_mtf(n, bank, passes=(0, 1)):
             words = mtf_b[n % 2][:].bitcast(F32)
-            for u in range(2):
-                for i in range(2):
-                    first = 256 * u + P * i
-                    nc.tensor.transpose(bank[:, first : first + P], words[:, 256 * i + u : 256 * (i + 1) : 2], ident[:])
+            for i in passes:
+                for u in range(2):
+                    nc.tensor.transpose(
+                        bank_words(n, bank)[:, i, :, u], words[:, 256 * i + u : 256 * (i + 1) : 2], ident[:]
+                    )
+
+        pairs = "p (i x u e) -> p i x u e"
 
         def scale_mtf(n, bank):
-            pairs = "p (i x u e) -> p i x u e"
             nc.vector.tensor_tensor(
                 out=staged(*mtf_place[n // 2], 1024 * (n % 2), 1024).rearrange(pairs, i=2, u=2, e=2),
-                in0=bank.bitcast(BF16).rearrange("p (u i x e) -> p i x u e", i=2, u=2, e=2),
+                in0=bank_words(n, bank).unsqueeze(4).bitcast(BF16),
                 in1=scale_wide[n % 2][:].rearrange(pairs, i=2, u=2, e=2),
                 op=MULT,
             )
@@ -363,6 +371,8 @@ def tile_pansharpen_detail_injection_s8_kernel(
         turn_bands(1, 0, turn_banks[0])
         turn_bands(1, 1, turn_banks[1])
         diag_out(0, 2, head_banks[0])
+        diag_out(0, 3, head_banks[1])
+        repeat_radio()
         intensity(0, 0)
         intensity(0, 1)
         subtract(0, 0)
@@ -373,13 +383,11 @@ def tile_pansharpen_detail_injection_s8_kernel(
         turn_bands(2, 0, turn_banks[0])
         turn_bands(2, 1, turn_banks[1])
         turn_detail(0, head_banks[2])
-        diag_out(0, 3, head_banks[1])
-        repeat_radio()
         intensity(1, 0)
         intensity(1, 1)
+        widen_mtf(3)
         diag_matmuls(1, 3, turn_banks[1])
         diag_out(1, 3, turn_banks[1])
-        widen_mtf(3)
         turn_bands(3, 0, turn_banks[0])
 
         last = PAIRS - 1
@@ -396,13 +404,14 @@ def tile_pansharpen_detail_injection_s8_kernel(
                 inject(s - 1, n)
             if s % 2 == 0:
                 interleave_dy((s - 2) // 2, 1)
-            turn_mtf(s + 2, turn_banks[1])
+            turn_mtf(s + 2, turn_banks[1], [0])
             subtract(s, 0)
             diag_matmuls(s + 1, 3, int_banks[0])
             diag_out(s + 1, 3, int_banks[0])
             subtract(s, 1)
             turn_bands(s + 2, 1, int_banks[1])
             turn_detail(s, turn_banks[0])
+            turn_mtf(s + 2, turn_banks[1], [1])
             if s + 3 <= last:
                 widen_mtf(s + 3)
             if s % 2 == 1:

@@ -24,8 +24,10 @@ BANK = 512
 GROUPS = M // 512
 HALVES = K // 512
 PAIRS = M // (2 * P)
-SHARED_PAIRS = (0, PAIRS - 1)
-HEAD_UNITS = 3
+ROW_TILES = R // P
+END_PAIRS = (0, PAIRS - 1)
+HEAD_SECTIONS = 3
+WHOLE_PAIRS = PAIRS - 3
 CALLS = PAIRS + 2
 STAGE_SLOTS = 3
 OUT_SLOTS = 4
@@ -55,13 +57,13 @@ def tile_pansharpen_detail_injection_s8_kernel(
         turn_banks = [bank_tile(f"turn_bank{i}", 6 + i) for i in range(2)]
 
         def inj_bank(s, n):
-            return inj_psum[:, BANK * n : BANK * (n + 1)] if s < PAIRS - 3 else tail_banks[n]
+            return inj_psum[:, BANK * n : BANK * (n + 1)] if s < WHOLE_PAIRS else tail_banks[n]
 
         ident = one("ident", P, F32)
         ident_b = one("ident_b", P, BF16)
         ones_b = one("ones_b", P, BF16)
         scale_col = one("scale_col", 4 * GROUPS, F32)
-        scale_wide = tiles("scale_wide", HALVES, 1024, F32)
+        scale_wide = tiles("scale_wide", 2, 1024, F32)
         radio_col = one("radio_col", 8, BF16)
         radio_bc = one("radio_bc", K + 512, BF16)
         diag = one("diag", K, BF16)
@@ -72,7 +74,7 @@ def tile_pansharpen_detail_injection_s8_kernel(
         mix_s = tiles("mix_s", HALVES, C, U8)
         bands_sb = tiles("bands_sb", PAIRS, 2 * K, BF16)
         pan_sb = tiles("pan_sb", PAIRS, 2 * C, BF16)
-        codes = tiles("codes", 4, M, U8)
+        codes = tiles("codes", ROW_TILES, M, U8)
         mtf_b = tiles("mtf_b", 2, 1024, BF16)
         stage = tiles("stage", STAGE_SLOTS, 4096, BF16)
         call_c = tiles("call_c", CALLS, 1024, U32)
@@ -81,15 +83,15 @@ def tile_pansharpen_detail_injection_s8_kernel(
         dx_c = tiles("dx_c", 2, 256, U32)
         dx_s = tiles("dx_s", 2, 256, U8)
         out_sb = tiles("out_sb", OUT_SLOTS, 2 * K, F32)
-        res = tiles("res", 4, C, F32)
+        res = tiles("res", ROW_TILES // 2, 2 * C, F32)
         mix_il = [one("mix_il", 4 * C, BF16)[:], out_sb[0][:, 0:K].bitcast(BF16)]
 
         bands_v = bands.rearrange("(g p a t) k -> g a p (t k)", p=P, a=2, t=2)
         pan_v = pan.rearrange("(g p a t) c -> g a p (t c)", p=P, a=2, t=2)
         sharp_v = sharp.rearrange("(g p a t) k -> g a p (t k)", p=P, a=2, t=2)
         mix_v = mix.rearrange("(h p j) c -> h p (j c)", p=P, j=4)
-        mtf_v = mtf_bytes.rearrange("(p r) k -> r p k", r=4)
-        coarse_v = coarse.rearrange("(p r) c -> r p c", r=4)
+        mtf_v = mtf_bytes.rearrange("(p r) k -> r p k", r=ROW_TILES)
+        coarse_v = coarse.rearrange("(p i r) c -> i p (r c)", i=2, r=2)
 
         ctx.enter_context(tc.manual_schedule())
 
@@ -107,7 +109,7 @@ def tile_pansharpen_detail_injection_s8_kernel(
             load(pan_sb[s][:], pan_v[s // 2, s % 2])
 
         load(radio_col[:].rearrange("p (h j) -> p h j", j=4), radio.rearrange("(h p j) -> p h j", p=P, j=4))
-        load(scale_col[:].rearrange("p (g t) -> p g t", t=4), mtf_scale.rearrange("o (g p t) -> p (o g) t", p=P, t=4))
+        load(scale_col[:].rearrange("p (g j) -> p g j", j=4), mtf_scale.rearrange("o (g p j) -> p (o g) j", p=P, j=4))
         load(codes[0][:], mtf_v[0])
         load(mix_raw[0][:], mix_v[0])
         load_bands(0)
@@ -125,7 +127,7 @@ def tile_pansharpen_detail_injection_s8_kernel(
             load_pan(s)
             if s + 2 < PAIRS:
                 load_bands(s + 2)
-            if s < 4:
+            if s < ROW_TILES:
                 load(codes[s][:], mtf_v[s])
 
         nc.scalar.copy(out=ident_b[:], in_=ident[:])
@@ -189,41 +191,40 @@ def tile_pansharpen_detail_injection_s8_kernel(
             start = 1024 * (n % 2)
             nc.scalar.copy(out=mtf_b[n % 2][:], in_=codes[n // 2][:, start : start + 1024].bitcast(FP8))
 
-        def spread_scale(hh):
-            scales = scale_col[:, 8 * hh : 8 * (hh + 1)].rearrange("p (i j) -> p i j", i=2)
+        def spread_scale(side):
+            scales = scale_col[:, 8 * side : 8 * (side + 1)].rearrange("p (i j) -> p i j", i=2)
             nc.scalar.copy(
-                out=scale_wide[hh][:].rearrange("p (i x j) -> p i x j", i=2, j=4),
+                out=scale_wide[side][:].rearrange("p (i x j) -> p i x j", i=2, j=4),
                 in_=scales.unsqueeze(2).to_broadcast([P, 2, P, 4]),
             )
 
-        def bank_words(n, bank):
-            if n < HEAD_UNITS:
+        def bank_doubles(n, bank):
+            if n < HEAD_SECTIONS:
                 return bank.rearrange("p (u i x) -> p i x u", u=2, i=2)
             return bank.rearrange("p (i x u) -> p i x u", u=2, i=2)
 
         def turn_mtf(n, bank, passes=(0, 1)):
-            words = mtf_b[n % 2][:].bitcast(F32)
+            doubles = mtf_b[n % 2][:].bitcast(F32)
             for i in passes:
                 for u in range(2):
                     nc.tensor.transpose(
-                        bank_words(n, bank)[:, i, :, u], words[:, 256 * i + u : 256 * (i + 1) : 2], ident[:]
+                        bank_doubles(n, bank)[:, i, :, u], doubles[:, 256 * i + u : 256 * (i + 1) : 2], ident[:]
                     )
 
-        pairs = "p (i x u e) -> p i x u e"
-
         def scale_mtf(n, bank):
+            by_value = "p (i x u e) -> p i x u e"
             nc.vector.tensor_tensor(
-                out=staged(*mtf_place[n // 2], 1024 * (n % 2), 1024).rearrange(pairs, i=2, u=2, e=2),
-                in0=bank_words(n, bank).unsqueeze(4).bitcast(BF16),
-                in1=scale_wide[n % 2][:].rearrange(pairs, i=2, u=2, e=2),
+                out=staged(*mtf_place[n // 2], 1024 * (n % 2), 1024).rearrange(by_value, i=2, u=2, e=2),
+                in0=bank_doubles(n, bank).unsqueeze(4).bitcast(BF16),
+                in1=scale_wide[n % 2][:].rearrange(by_value, i=2, u=2, e=2),
                 op=MULT,
             )
 
         def turn_bands(s, t, bank):
-            words = bands_sb[s][:, K * t : K * (t + 1)].bitcast(F32)
+            doubles = bands_sb[s][:, K * t : K * (t + 1)].bitcast(F32)
             for n in range(4):
                 start = 256 * (n // 2) + n % 2
-                nc.tensor.transpose(bank[:, P * n : P * (n + 1)], words[:, start : 256 * (n // 2 + 1) : 2], ident[:])
+                nc.tensor.transpose(bank[:, P * n : P * (n + 1)], doubles[:, start : 256 * (n // 2 + 1) : 2], ident[:])
             turn_out(bank, staged(s, 0, K * t, K))
 
         def intensity(s, t):
@@ -252,23 +253,24 @@ def tile_pansharpen_detail_injection_s8_kernel(
             return out_sb[(s + 1) % OUT_SLOTS][:, 0:512].bitcast(BF16)
 
         def turn_detail(s, bank):
-            words = detail[s // 2 % 2][:, 1024 * (s % 2) : 1024 * (s % 2 + 1)].bitcast(F32)
+            doubles = detail[s // 2 % 2][:, 1024 * (s % 2) : 1024 * (s % 2 + 1)].bitcast(F32)
             for n in range(4):
-                nc.tensor.transpose(bank[:, P * n : P * (n + 1)], words[:, P * n : P * (n + 1)], ident[:])
+                nc.tensor.transpose(bank[:, P * n : P * (n + 1)], doubles[:, P * n : P * (n + 1)], ident[:])
             turn_out(bank, dx_il(s))
 
         def quantize_dx(s):
             quantize(dx_c[s % 2][:], dx_s[s % 2][:], dx_il(s))
 
-        def interleave_dy(g, half, engine_copy=nc.scalar.copy):
+        def interleave_dy(g, half):
             cols = slice(256 * half, 256 * (half + 1))
-            engine_copy(
-                out=staged(*dy_place[g], 1024 * half, 1024).rearrange("p (m i t) -> p m t i", i=4, t=4),
-                in_=detail[g % 2][:].rearrange("p (t c) -> p t c", t=4)[:, :, cols].rearrange("p t (m i) -> p m t i", i=4),
+            rows = detail[g % 2][:].rearrange("p (j c) -> p j c", j=4)[:, :, cols]
+            nc.scalar.copy(
+                out=staged(*dy_place[g], 1024 * half, 1024).rearrange("p (m i j) -> p m j i", i=4, j=4),
+                in_=rows.rearrange("p j (m i) -> p m j i", i=4),
             )
 
         def products_pool(s):
-            cols = slice(0, K if s in SHARED_PAIRS else K + 512)
+            cols = slice(0, K if s in END_PAIRS else K + 512)
             nc.gpsimd.tensor_tensor(
                 out=out_sb[s % OUT_SLOTS][:, cols], in0=bands_sb[s][:, cols], in1=radio_bc[:, cols], op=MULT
             )
@@ -287,10 +289,9 @@ def tile_pansharpen_detail_injection_s8_kernel(
                 in_=bank.rearrange("p (j m) -> p m j", j=4),
             )
 
-        def products_diag(s, banks):
-            for n, bank in zip((2, 3), banks):
-                diag_matmuls(s, n, bank)
-                diag_out(s, n, bank)
+        def product_diag(s, n, bank):
+            diag_matmuls(s, n, bank)
+            diag_out(s, n, bank)
 
         def inject(s, n):
             t, h = n // 2, n % 2
@@ -313,7 +314,9 @@ def tile_pansharpen_detail_injection_s8_kernel(
             cols = slice(512 * n, 512 * (n + 1))
             out = out_sb[s % OUT_SLOTS]
             nc.vector.tensor_tensor(out=out[:, cols], in0=out[:, cols], in1=inj_bank(s, n), op=ADD)
-            nc.sync.dma_start(out=sharp_v[s // 2, s % 2][:, cols], in_=out[:, cols])
+            if n % 2 == 1:
+                row = slice(K * (n // 2), K * (n // 2 + 1))
+                nc.sync.dma_start(out=sharp_v[s // 2, s % 2][:, row], in_=out[:, row])
 
         coarse_banks = [turn_banks[1]] + int_banks + [turn_banks[0]]
 
@@ -335,12 +338,13 @@ def tile_pansharpen_detail_injection_s8_kernel(
                 for g in groups:
                     coarse_pass(r, g)
 
-        def coarse_out(r, engine_copy):
-            engine_copy(
-                out=res[r][:].rearrange("p (m u e) -> p m u e", u=2, e=2),
+        def coarse_out(r):
+            nc.scalar.copy(
+                out=res[r // 2][:, C * (r % 2) : C * (r % 2 + 1)].rearrange("p (m u e) -> p m u e", u=2, e=2),
                 in_=coarse_banks[r].rearrange("p (u m e) -> p m u e", u=2, e=2),
             )
-            nc.sync.dma_start(out=coarse_v[r], in_=res[r][:])
+            if r % 2 == 1:
+                nc.sync.dma_start(out=coarse_v[r // 2], in_=res[r // 2][:])
 
         build_diag()
         spread_scale(0)
@@ -386,8 +390,7 @@ def tile_pansharpen_detail_injection_s8_kernel(
         intensity(1, 0)
         intensity(1, 1)
         widen_mtf(3)
-        diag_matmuls(1, 3, turn_banks[1])
-        diag_out(1, 3, turn_banks[1])
+        product_diag(1, 3, turn_banks[1])
         turn_bands(3, 0, turn_banks[0])
 
         last = PAIRS - 1
@@ -406,8 +409,7 @@ def tile_pansharpen_detail_injection_s8_kernel(
                 interleave_dy((s - 2) // 2, 1)
             turn_mtf(s + 2, turn_banks[1], [0])
             subtract(s, 0)
-            diag_matmuls(s + 1, 3, int_banks[0])
-            diag_out(s + 1, 3, int_banks[0])
+            product_diag(s + 1, 3, int_banks[0])
             subtract(s, 1)
             turn_bands(s + 2, 1, int_banks[1])
             turn_detail(s, turn_banks[0])
@@ -427,7 +429,8 @@ def tile_pansharpen_detail_injection_s8_kernel(
         quantize_call(last)
         products_pool(last - 1)
         interleave_dy(GROUPS - 2, 1)
-        products_diag(last, turn_banks[::-1])
+        product_diag(last, 2, turn_banks[1])
+        product_diag(last, 3, turn_banks[0])
         for n in range(4):
             inject(last - 2, n)
         for t in range(2):
@@ -453,17 +456,15 @@ def tile_pansharpen_detail_injection_s8_kernel(
             inject(last - 1, n)
         coarse_passes(range(3), [2])
         coarse_passes([3], range(3))
-        finish_piece(last - 1, 0)
-        finish_piece(last - 1, 1)
-        finish_piece(last - 1, 2)
-        finish_piece(last - 1, 3)
+        for n in range(4):
+            finish_piece(last - 1, n)
         quantize_dx(last)
         quantize_call(CALLS - 1)
-        for r in range(4):
-            inject(last, r)
-            if r > 0:
-                coarse_pass(r - 1, GROUPS - 1)
-        coarse_pass(3, GROUPS - 1)
-        for r in range(4):
-            finish_piece(last, r)
-            coarse_out(r, nc.scalar.copy)
+        inject(last, 0)
+        for n in range(1, 4):
+            inject(last, n)
+            coarse_pass(n - 1, GROUPS - 1)
+        coarse_pass(ROW_TILES - 1, GROUPS - 1)
+        for n in range(4):
+            finish_piece(last, n)
+            coarse_out(n)

@@ -25,12 +25,13 @@ GROUPS = M // 512
 HALVES = K // 512
 PAIRS = M // (2 * P)
 ROW_TILES = R // P
-END_PAIRS = (0, PAIRS - 1)
-HEAD_SECTIONS = 3
+COPY = mybir.ActivationFunctionType.Copy
+SHORT_PAIRS = (0, 1)
 WHOLE_PAIRS = PAIRS - 3
-CALLS = PAIRS + 2
-STAGE_SLOTS = 3
-OUT_SLOTS = 4
+SLOTS = 5
+STAGE = 4096
+KEPT = 1024
+MADE_SLOTS = 3
 
 
 def tile_pansharpen_detail_injection_s8_kernel(
@@ -63,34 +64,46 @@ def tile_pansharpen_detail_injection_s8_kernel(
         ident_b = one("ident_b", P, BF16)
         ones_b = one("ones_b", P, BF16)
         scale_col = one("scale_col", 4 * GROUPS, F32)
-        scale_wide = tiles("scale_wide", 2, 1024, F32)
+        scale_wide = {g: one(f"scale_wide{g}_", 512, F32) for g in (0, 1, 3)}
         radio_col = one("radio_col", 8, BF16)
         radio_bc = one("radio_bc", K + 512, BF16)
         diag = one("diag", K, BF16)
         gain_w = one("gain_w", 2 * K, U8)
         gain_s = one("gain_s", K, U8)
-        mix_raw = tiles("mix_raw", HALVES, 4 * C, BF16)
         mix_c = tiles("mix_c", HALVES, C, U32)
         mix_s = tiles("mix_s", HALVES, C, U8)
         bands_sb = tiles("bands_sb", PAIRS, 2 * K, BF16)
         pan_sb = tiles("pan_sb", PAIRS, 2 * C, BF16)
-        codes = tiles("codes", ROW_TILES, M, U8)
-        mtf_b = tiles("mtf_b", 2, 1024, BF16)
-        stage = tiles("stage", STAGE_SLOTS, 4096, BF16)
-        call_c = tiles("call_c", CALLS, 1024, U32)
-        call_s = tiles("call_s", CALLS, 1024, U8)
+        codes = tiles("codes", GROUPS, ROW_TILES * 512, U8)
+        mtf_b = tiles("mtf_b", 4, 1024, BF16)
+        planes = one("planes", 1024, BF16)
+        work = tiles("work", SLOTS, KEPT + 2 * 2 * K, BF16)
+        made = tiles("made", MADE_SLOTS, STAGE, BF16)
         detail = tiles("detail", 2, 4 * C, BF16)
-        dx_c = tiles("dx_c", 2, 256, U32)
-        dx_s = tiles("dx_s", 2, 256, U8)
-        out_sb = tiles("out_sb", OUT_SLOTS, 2 * K, F32)
         res = tiles("res", ROW_TILES // 2, 2 * C, F32)
-        mix_il = [one("mix_il", 4 * C, BF16)[:], out_sb[0][:, 0:K].bitcast(BF16)]
+
+        last = PAIRS - 1
+        call_in = {("first", s): work[s % SLOTS][:, 0:2048] for s in range(-1, PAIRS)}
+        for s in range(1, PAIRS + 1):
+            call_in["made", s] = made[s % MADE_SLOTS][:, 0 : STAGE if s in (4, 6, 8) else 2048]
+        call_c = {c: one(f"call_c_{c[0]}{c[1] + 1}_", src.shape[1] // 4, U32) for c, src in call_in.items()}
+        call_s = {c: one(f"call_s_{c[0]}{c[1] + 1}_", src.shape[1] // 4, U8) for c, src in call_in.items()}
+        bands_place = [(("first", s - 1), 0) for s in range(PAIRS)]
+        dx_place = [(("made", s + 1), 0) for s in range(PAIRS)]
+        dy_place = [(("made", 4), 2048), (("made", 6), 2048), (("first", last), 0), (("made", PAIRS), 2048)]
+        units = [(a, g) for g in range(GROUPS) for a in range(2)]
+        mtf_place = {unit: (("made", n + 1), 1024) for n, unit in enumerate(units)}
+        mix_raw = [work[3][:, 2048 * h : 2048 * (h + 1)] for h in range(HALVES)]
+        mix_il = [made[0][:, 2048 * h : 2048 * (h + 1)] for h in range(HALVES)]
+
+        def out_sb(s):
+            return work[s % SLOTS][:, KEPT:].bitcast(F32)
 
         bands_v = bands.rearrange("(g p a t) k -> g a p (t k)", p=P, a=2, t=2)
         pan_v = pan.rearrange("(g p a t) c -> g a p (t c)", p=P, a=2, t=2)
         sharp_v = sharp.rearrange("(g p a t) k -> g a p (t k)", p=P, a=2, t=2)
         mix_v = mix.rearrange("(h p j) c -> h p (j c)", p=P, j=4)
-        mtf_v = mtf_bytes.rearrange("(p r) k -> r p k", r=ROW_TILES)
+        mtf_v = mtf_bytes.rearrange("(p r) (g k) -> g p r k", r=ROW_TILES, k=512)
         coarse_v = coarse.rearrange("(p i r) c -> i p (r c)", i=2, r=2)
 
         ctx.enter_context(tc.manual_schedule())
@@ -108,29 +121,50 @@ def tile_pansharpen_detail_injection_s8_kernel(
         def load_pan(s):
             load(pan_sb[s][:], pan_v[s // 2, s % 2])
 
+        def load_codes(g):
+            load(codes[g][:].rearrange("p (r k) -> p r k", r=ROW_TILES), mtf_v[g])
+
         load(radio_col[:].rearrange("p (h j) -> p h j", j=4), radio.rearrange("(h p j) -> p h j", p=P, j=4))
-        load(scale_col[:].rearrange("p (g j) -> p g j", j=4), mtf_scale.rearrange("o (g p j) -> p (o g) j", p=P, j=4))
-        load(codes[0][:], mtf_v[0])
-        load(mix_raw[0][:], mix_v[0])
+        load(mix_raw[0], mix_v[0])
         load_bands(0)
-        load(mix_raw[1][:], mix_v[1])
-        load_pan(0)
+        load(mix_raw[1], mix_v[1])
         load_bands(1)
-        load(codes[1][:], mtf_v[1])
+        load(scale_col[:].rearrange("p (g j) -> p g j", j=4), mtf_scale.rearrange("o (g p j) -> p (o g) j", p=P, j=4))
+        load_codes(0)
+        load_pan(0)
         load_bands(2)
         load_pan(1)
+        load_codes(1)
         load_bands(3)
         load(gain_w[:].bitcast(I32), gain_words[0].bitcast(I32))
         for q in range(4):
             load(gain_s[32 * q : 32 * q + 4, :].bitcast(I32), gain_scales[0][4 * q : 4 * q + 4, :].bitcast(I32))
         for s in range(2, PAIRS):
             load_pan(s)
+            if s < GROUPS:
+                load_codes(s)
             if s + 2 < PAIRS:
                 load_bands(s + 2)
-            if s < ROW_TILES:
-                load(codes[s][:], mtf_v[s])
 
-        nc.scalar.copy(out=ident_b[:], in_=ident[:])
+        nc.scalar.activation(out=ident_b[:], in_=ident[:], func=COPY)
+
+        def staged(place, start, width):
+            call, first = place
+            return call_in[call][:, first + start : first + start + width]
+
+        def operand(place, start, width):
+            call, first = place
+            cols = slice(first // 4 + start, first // 4 + start + width)
+            return call_c[call][:, cols].bitcast(FP8X4), call_s[call][:, cols]
+
+        def quantize(codes_out, scales_out, src):
+            nc.vector.quantize_mx(out=codes_out.bitcast(FP8X4), scales=scales_out, in_=src)
+
+        def quantize_call(call, start=0, width=None):
+            if width is None:
+                width = call_in[call].shape[1]
+            cols = slice(start // 4, (start + width) // 4)
+            quantize(call_c[call][:, cols], call_s[call][:, cols], call_in[call][:, start : start + width])
 
         def turn_out(bank, dst):
             nc.scalar.copy(
@@ -138,8 +172,10 @@ def tile_pansharpen_detail_injection_s8_kernel(
                 in_=bank.rearrange("p (h u x) -> p h x u", h=2, u=2),
             )
 
-        def quantize(codes_out, scales_out, src):
-            nc.vector.quantize_mx(out=codes_out.bitcast(FP8X4), scales=scales_out, in_=src)
+        def interleave(dst, rows):
+            nc.scalar.copy(
+                out=dst.rearrange("p (m i j) -> p m j i", i=4, j=4), in_=rows.rearrange("p j (m i) -> p m j i", i=4)
+            )
 
         def build_diag():
             nc.vector.tensor_tensor(
@@ -149,9 +185,10 @@ def tile_pansharpen_detail_injection_s8_kernel(
                 op=MULT,
             )
 
-        def spread_radio(h):
-            bank = int_banks[h]
+        def spread_radio(h, bank):
             nc.tensor.matmul(bank, ones_b[:], diag[:, 512 * h : 512 * (h + 1)], start=True, stop=True)
+
+        def radio_out(h, bank):
             nc.scalar.copy(
                 out=radio_bc[:, 512 * h : 512 * (h + 1)].rearrange("p (m j) -> p m j", j=4),
                 in_=bank.rearrange("p (j m) -> p m j", j=4),
@@ -163,82 +200,76 @@ def tile_pansharpen_detail_injection_s8_kernel(
         def interleave_mix(h, u):
             nc.vector.tensor_copy(
                 out=mix_il[h][:, K * u : K * (u + 1)].rearrange("p (m e j) -> p m j e", e=2, j=4),
-                in_=mix_raw[h][:].rearrange("p (j m u e) -> p u m j e", u=2, e=2, j=4)[:, u],
+                in_=mix_raw[h].rearrange("p (j m u e) -> p u m j e", u=2, e=2, j=4)[:, u],
             )
 
         def quantize_mix(h, u):
             cols = slice(256 * u, 256 * (u + 1))
             quantize(mix_c[h][:, cols], mix_s[h][:, cols], mix_il[h][:, K * u : K * (u + 1)])
 
-        mtf_place = [(2, 1), (3, 1), (5, 1), (7, 1)]
-        dy_place = [(4, 1), (6, 1), (8, 0), (9, 0)]
+        def widen_mtf(a, g):
+            nc.scalar.copy(out=mtf_b[2 * (g % 2) + a][:], in_=codes[g][:, 1024 * a : 1024 * (a + 1)].bitcast(FP8))
 
-        def staged(call, half, start, width):
-            first = 2048 * half + start
-            return stage[call % STAGE_SLOTS][:, first : first + width]
-
-        def operand(call, half, start, width):
-            cols = slice(512 * half + start, 512 * half + start + width)
-            return call_c[call][:, cols].bitcast(FP8X4), call_s[call][:, cols]
-
-        def quantize_call(call, start=0, width=None):
-            if width is None:
-                width = 4096 if (call, 1) in mtf_place + dy_place else 2048
-            cols = slice(start // 4, (start + width) // 4)
-            quantize(call_c[call][:, cols], call_s[call][:, cols], staged(call, 0, start, width))
-
-        def widen_mtf(n):
-            start = 1024 * (n % 2)
-            nc.scalar.copy(out=mtf_b[n % 2][:], in_=codes[n // 2][:, start : start + 1024].bitcast(FP8))
-
-        def spread_scale(side):
-            scales = scale_col[:, 8 * side : 8 * (side + 1)].rearrange("p (i j) -> p i j", i=2)
+        def spread_scale(g):
             nc.scalar.copy(
-                out=scale_wide[side][:].rearrange("p (i x j) -> p i x j", i=2, j=4),
-                in_=scales.unsqueeze(2).to_broadcast([P, 2, P, 4]),
+                out=scale_wide[g][:].rearrange("p (x j) -> p x j", j=4),
+                in_=scale_col[:, 4 * g : 4 * (g + 1)].unsqueeze(1).to_broadcast([P, P, 4]),
             )
 
-        def bank_doubles(n, bank):
-            if n < HEAD_SECTIONS:
-                return bank.rearrange("p (u i x) -> p i x u", u=2, i=2)
-            return bank.rearrange("p (i x u) -> p i x u", u=2, i=2)
+        def turn_mtf(a, g, bank):
+            doubles = mtf_b[2 * (g % 2) + a][:].bitcast(F32)
+            for n in range(4):
+                u, i = n // 2, n % 2
+                nc.tensor.transpose(bank[:, P * n : P * (n + 1)], doubles[:, 256 * i + u : 256 * (i + 1) : 2], ident[:])
 
-        def turn_mtf(n, bank, passes=(0, 1)):
-            doubles = mtf_b[n % 2][:].bitcast(F32)
-            for i in passes:
-                for u in range(2):
-                    nc.tensor.transpose(
-                        bank_doubles(n, bank)[:, i, :, u], doubles[:, 256 * i + u : 256 * (i + 1) : 2], ident[:]
-                    )
-
-        def scale_mtf(n, bank):
-            by_value = "p (i x u e) -> p i x u e"
+        def scale_mtf_vector(a, g, bank):
             nc.vector.tensor_tensor(
-                out=staged(*mtf_place[n // 2], 1024 * (n % 2), 1024).rearrange(by_value, i=2, u=2, e=2),
-                in0=bank_doubles(n, bank).unsqueeze(4).bitcast(BF16),
-                in1=scale_wide[n % 2][:].rearrange(by_value, i=2, u=2, e=2),
+                out=staged(mtf_place[a, g], 0, 1024).rearrange("p (i x u e) -> p i x u e", i=2, u=2, e=2),
+                in0=bank.bitcast(BF16).rearrange("p (u i x e) -> p i x u e", i=2, u=2, e=2),
+                in1=scale_wide[g][:].rearrange("p (x u e) -> p x u e", u=2, e=2).unsqueeze(1).to_broadcast([P, 2, P, 2, 2]),
                 op=MULT,
             )
+
+        def scale_mtf_scalar(g, bank):
+            values = bank.bitcast(BF16).rearrange("p (u x e) -> p u e x", u=2, e=2)
+            for j in range(4):
+                nc.scalar.activation(
+                    out=planes[:, 256 * j : 256 * (j + 1)],
+                    in_=values[:, j // 2, j % 2, :],
+                    func=COPY,
+                    scale=scale_col[:, 4 * g + j : 4 * g + j + 1],
+                )
+
+        def interleave_mtf(a, g):
+            interleave(staged(mtf_place[a, g], 0, 1024), planes[:].rearrange("p (j x) -> p j x", j=4))
+
+        def staged_bands(s, t):
+            return staged(bands_place[s], K * (1 - t), K)
 
         def turn_bands(s, t, bank):
             doubles = bands_sb[s][:, K * t : K * (t + 1)].bitcast(F32)
             for n in range(4):
                 start = 256 * (n // 2) + n % 2
                 nc.tensor.transpose(bank[:, P * n : P * (n + 1)], doubles[:, start : 256 * (n // 2 + 1) : 2], ident[:])
-            turn_out(bank, staged(s, 0, K * t, K))
+
+        def bands_out(s, t, bank):
+            turn_out(bank, staged_bands(s, t))
+
+        def intensity_pass(s, t, h):
+            x_c, x_s = operand(bands_place[s], 256 * (1 - t) + P * h, P)
+            nc.tensor.matmul_mx(
+                out=int_banks[t],
+                lhsT=x_c,
+                lhsT_scale=x_s,
+                rhs=mix_c[h][:].bitcast(FP8X4),
+                rhs_scale=mix_s[h][:],
+                start=(h == 0),
+                stop=(h == HALVES - 1),
+            )
 
         def intensity(s, t):
             for h in range(HALVES):
-                x_c, x_s = operand(s, 0, 256 * t + P * h, P)
-                nc.tensor.matmul_mx(
-                    out=int_banks[t],
-                    lhsT=x_c,
-                    lhsT_scale=x_s,
-                    rhs=mix_c[h][:].bitcast(FP8X4),
-                    rhs_scale=mix_s[h][:],
-                    start=(h == 0),
-                    stop=(h == HALVES - 1),
-                )
+                intensity_pass(s, t, h)
 
         def subtract(s, t):
             row = 2 * (s % 2) + t
@@ -249,56 +280,43 @@ def tile_pansharpen_detail_injection_s8_kernel(
                 op=SUB,
             )
 
-        def dx_il(s):
-            return out_sb[(s + 1) % OUT_SLOTS][:, 0:512].bitcast(BF16)
-
         def turn_detail(s, bank):
             doubles = detail[s // 2 % 2][:, 1024 * (s % 2) : 1024 * (s % 2 + 1)].bitcast(F32)
             for n in range(4):
                 nc.tensor.transpose(bank[:, P * n : P * (n + 1)], doubles[:, P * n : P * (n + 1)], ident[:])
-            turn_out(bank, dx_il(s))
 
-        def quantize_dx(s):
-            quantize(dx_c[s % 2][:], dx_s[s % 2][:], dx_il(s))
+        def detail_out(s, bank):
+            turn_out(bank, staged(dx_place[s], 0, 1024))
 
         def interleave_dy(g, half):
-            cols = slice(256 * half, 256 * (half + 1))
-            rows = detail[g % 2][:].rearrange("p (j c) -> p j c", j=4)[:, :, cols]
-            nc.scalar.copy(
-                out=staged(*dy_place[g], 1024 * half, 1024).rearrange("p (m i j) -> p m j i", i=4, j=4),
-                in_=rows.rearrange("p j (m i) -> p m j i", i=4),
-            )
+            rows = detail[g % 2][:].rearrange("p (j c) -> p j c", j=4)[:, :, 256 * half : 256 * (half + 1)]
+            interleave(staged(dy_place[g], 1024 * half, 1024), rows)
 
         def products_pool(s):
-            cols = slice(0, K if s in END_PAIRS else K + 512)
-            nc.gpsimd.tensor_tensor(
-                out=out_sb[s % OUT_SLOTS][:, cols], in0=bands_sb[s][:, cols], in1=radio_bc[:, cols], op=MULT
-            )
+            cols = slice(0, K + 512)
+            nc.gpsimd.tensor_tensor(out=out_sb(s)[:, cols], in0=bands_sb[s][:, cols], in1=radio_bc[:, cols], op=MULT)
 
-        def diag_matmuls(s, n, bank):
-            turned = staged(s, 0, 512 * n, 512)
+        def diag_matmuls(s, h, bank):
+            values = staged_bands(s, 1)[:, 512 * h : 512 * (h + 1)]
             for j in range(4):
-                d0 = 512 * (n % 2) + P * j
+                d0 = 512 * h + P * j
                 nc.tensor.matmul(
-                    bank[:, P * j : P * (j + 1)], turned[:, j:512:4], diag[:, d0 : d0 + P], start=True, stop=True
+                    bank[:, P * j : P * (j + 1)], values[:, j:512:4], diag[:, d0 : d0 + P], start=True, stop=True
                 )
 
-        def diag_out(s, n, bank):
+        def diag_out(s, h, bank):
             nc.scalar.copy(
-                out=out_sb[s % OUT_SLOTS][:, 512 * n : 512 * (n + 1)].rearrange("p (m j) -> p m j", j=4),
+                out=out_sb(s)[:, K + 512 * h : K + 512 * (h + 1)].rearrange("p (m j) -> p m j", j=4),
                 in_=bank.rearrange("p (j m) -> p m j", j=4),
             )
 
-        def product_diag(s, n, bank):
-            diag_matmuls(s, n, bank)
-            diag_out(s, n, bank)
-
         def inject(s, n):
             t, h = n // 2, n % 2
+            dx_c, dx_s = operand(dx_place[s], P * t, P)
             nc.tensor.matmul_mx(
                 out=inj_bank(s, n),
-                lhsT=dx_c[s % 2][:, P * t : P * (t + 1)].bitcast(FP8X4),
-                lhsT_scale=dx_s[s % 2][:, P * t : P * (t + 1)],
+                lhsT=dx_c,
+                lhsT_scale=dx_s,
                 rhs=gain_w[:, 1024 * h : 1024 * (h + 1)].bitcast(FP4X4),
                 rhs_scale=gain_s[:, 512 * h : 512 * (h + 1)],
                 start=True,
@@ -306,37 +324,34 @@ def tile_pansharpen_detail_injection_s8_kernel(
             )
 
         def finish(s):
-            out = out_sb[s % OUT_SLOTS]
-            nc.vector.tensor_tensor(out=out[:], in0=out[:], in1=inj_psum, op=ADD)
-            nc.sync.dma_start(out=sharp_v[s // 2, s % 2], in_=out[:])
+            out = out_sb(s)
+            nc.vector.tensor_tensor(out=out, in0=out, in1=inj_psum, op=ADD)
+            nc.sync.dma_start(out=sharp_v[s // 2, s % 2], in_=out)
 
         def finish_piece(s, n):
             cols = slice(512 * n, 512 * (n + 1))
-            out = out_sb[s % OUT_SLOTS]
+            out = out_sb(s)
             nc.vector.tensor_tensor(out=out[:, cols], in0=out[:, cols], in1=inj_bank(s, n), op=ADD)
             if n % 2 == 1:
                 row = slice(K * (n // 2), K * (n // 2 + 1))
                 nc.sync.dma_start(out=sharp_v[s // 2, s % 2][:, row], in_=out[:, row])
 
-        coarse_banks = [turn_banks[1]] + int_banks + [turn_banks[0]]
-
-        def coarse_pass(r, g):
-            mtf_c, mtf_s = operand(*mtf_place[r], P * g, P)
-            dy_c, dy_s = operand(*dy_place[g], 0, C)
-            nc.tensor.matmul_mx(
-                out=coarse_banks[r],
-                lhsT=mtf_c,
-                lhsT_scale=mtf_s,
-                rhs=dy_c,
-                rhs_scale=dy_s,
-                start=(g == 0),
-                stop=(g == GROUPS - 1),
-            )
+        coarse_banks = [turn_banks[1], int_banks[0], int_banks[1], turn_banks[0]]
 
         def coarse_passes(row_tiles, groups):
             for r in row_tiles:
                 for g in groups:
-                    coarse_pass(r, g)
+                    mtf_c, mtf_s = operand(mtf_place[r // 2, g], P * (r % 2), P)
+                    dy_c, dy_s = operand(dy_place[g], 0, C)
+                    nc.tensor.matmul_mx(
+                        out=coarse_banks[r],
+                        lhsT=mtf_c,
+                        lhsT_scale=mtf_s,
+                        rhs=dy_c,
+                        rhs_scale=dy_s,
+                        start=(g == 0),
+                        stop=(g == GROUPS - 1),
+                    )
 
         def coarse_out(r):
             nc.scalar.copy(
@@ -344,127 +359,151 @@ def tile_pansharpen_detail_injection_s8_kernel(
                 in_=coarse_banks[r].rearrange("p (u m e) -> p m u e", u=2, e=2),
             )
             if r % 2 == 1:
-                nc.sync.dma_start(out=coarse_v[r // 2], in_=res[r // 2][:])
+                nc.scalar.dma_start(out=coarse_v[r // 2], in_=res[r // 2][:])
+
+        H = head_banks
+        C0, C1 = turn_banks
+
+        def bands_through(s, t, bank):
+            turn_bands(s, t, bank)
+            bands_out(s, t, bank)
+
+        def diag_through(s, h, bank):
+            diag_matmuls(s, h, bank)
+            diag_out(s, h, bank)
+
+        def inject_pair(s):
+            for n in range(4):
+                inject(s, n)
 
         build_diag()
-        spread_scale(0)
-        widen_mtf(0)
-        widen_mtf(1)
-        spread_radio(0)
-        spread_radio(1)
         interleave_mix(0, 0)
         interleave_mix(0, 1)
         quantize_mix(0, 0)
         quantize_mix(0, 1)
-        turn_mtf(0, head_banks[2])
-        scale_mtf(0, head_banks[2])
-        turn_bands(0, 0, turn_banks[0])
-        turn_bands(0, 1, turn_banks[1])
-        turn_mtf(1, head_banks[3])
         interleave_mix(1, 0)
         interleave_mix(1, 1)
+        bands_through(0, 0, C0)
+        bands_through(0, 1, C1)
+        spread_radio(0, H[0])
+        spread_radio(1, H[1])
+        radio_out(0, H[0])
+        radio_out(1, H[1])
+        bands_through(1, 0, H[2])
+        bands_through(1, 1, H[3])
+        diag_matmuls(0, 1, C0)
         quantize_mix(1, 0)
-        quantize_call(0)
+        quantize_call(("first", -1))
         quantize_mix(1, 1)
-        products_pool(0)
-        spread_scale(1)
-        scale_mtf(1, head_banks[3])
-        widen_mtf(2)
-        for n in (2, 3):
-            diag_matmuls(0, n, head_banks[n - 2])
-        turn_bands(1, 0, turn_banks[0])
-        turn_bands(1, 1, turn_banks[1])
-        diag_out(0, 2, head_banks[0])
-        diag_out(0, 3, head_banks[1])
+        quantize_call(("first", 0))
+        widen_mtf(0, 0)
+        spread_scale(0)
+        widen_mtf(1, 0)
         repeat_radio()
+        diag_out(0, 1, C0)
         intensity(0, 0)
         intensity(0, 1)
+        products_pool(0)
+        turn_mtf(0, 0, C1)
+        turn_bands(2, 0, H[2])
+        turn_mtf(1, 0, H[1])
         subtract(0, 0)
         subtract(0, 1)
-        quantize_call(1)
-        turn_mtf(2, head_banks[3])
-        scale_mtf(2, head_banks[3])
-        turn_bands(2, 0, turn_banks[0])
-        turn_bands(2, 1, turn_banks[1])
-        turn_detail(0, head_banks[2])
+        scale_mtf_vector(0, 0, C1)
+        turn_detail(0, H[0])
+        widen_mtf(0, 1)
+        detail_out(0, H[0])
+        bands_out(2, 0, H[2])
+        bands_through(2, 1, H[3])
         intensity(1, 0)
         intensity(1, 1)
-        widen_mtf(3)
-        product_diag(1, 3, turn_banks[1])
-        turn_bands(3, 0, turn_banks[0])
+        scale_mtf_vector(1, 0, H[1])
+        widen_mtf(1, 1)
+        spread_scale(1)
+        turn_mtf(0, 1, H[0])
+        turn_mtf(1, 1, H[1])
+        widen_mtf(0, 2)
+        subtract(1, 0)
+        subtract(1, 1)
 
-        last = PAIRS - 1
-        for s in range(1, last - 1):
-            if s == 1:
-                quantize_call(s + 1, 0, 2048)
-            quantize_dx(s - 1)
-            if s == 1:
-                quantize_call(s + 1, 2048, 2048)
-            else:
-                quantize_call(s + 1)
+        def scale_unit(a, g):
+            turn_mtf(a, g, C1)
+            scale_mtf_scalar(g, C1)
+
+        early = {
+            1: [(interleave_dy, 0, 0), (spread_scale, 3)],
+            2: [(interleave_mtf, 0, 2)],
+            3: [(interleave_dy, 1, 0)],
+            4: [(interleave_mtf, 1, 2), (widen_mtf, 1, 3)],
+            5: [(interleave_dy, 2, 0)],
+            6: [(interleave_mtf, 0, 3), (interleave_dy, 2, 1)],
+        }
+        late = {
+            1: [(scale_unit, 0, 2)],
+            2: [(interleave_dy, 0, 1), (widen_mtf, 1, 2)],
+            3: [(scale_unit, 1, 2)],
+            4: [(interleave_dy, 1, 1), (widen_mtf, 0, 3)],
+            5: [(scale_unit, 0, 3)],
+            6: [(diag_through, 7, 1, C1)],
+        }
+        for s in range(1, last):
+            quantize_call(("first", s))
+            quantize_call(("made", s))
             products_pool(s)
-            for n in range(4):
-                inject(s - 1, n)
-            if s % 2 == 0:
-                interleave_dy((s - 2) // 2, 1)
-            turn_mtf(s + 2, turn_banks[1], [0])
-            subtract(s, 0)
-            product_diag(s + 1, 3, int_banks[0])
-            subtract(s, 1)
-            turn_bands(s + 2, 1, int_banks[1])
-            turn_detail(s, turn_banks[0])
-            turn_mtf(s + 2, turn_banks[1], [1])
-            if s + 3 <= last:
-                widen_mtf(s + 3)
-            if s % 2 == 1:
-                interleave_dy(s // 2, 0)
+            turn_detail(s, int_banks[1])
+            detail_out(s, int_banks[1])
+            if s + 2 <= last:
+                bands_through(s + 2, 0, C0)
+                bands_through(s + 2, 1, C1)
+            for f, *args in early[s]:
+                f(*args)
             intensity(s + 1, 0)
             intensity(s + 1, 1)
-            finish(s - 1)
-            scale_mtf(s + 2, turn_banks[1])
-            if s + 3 <= last:
-                turn_bands(s + 3, 0, turn_banks[0])
+            diag_through(s, 1, C0)
+            for f, *args in late[s]:
+                f(*args)
+            if s == 1:
+                scale_mtf_vector(0, 1, H[0])
+                scale_mtf_vector(1, 1, H[1])
+            else:
+                finish(s - 2)
+            inject_pair(s - 1)
+            subtract(s + 1, 0)
+            subtract(s + 1, 1)
 
-        quantize_dx(last - 2)
-        quantize_call(last)
-        products_pool(last - 1)
-        interleave_dy(GROUPS - 2, 1)
-        product_diag(last, 2, turn_banks[1])
-        product_diag(last, 3, turn_banks[0])
-        for n in range(4):
-            inject(last - 2, n)
-        for t in range(2):
-            subtract(last - 1, t)
-            intensity(last, t)
-        turn_detail(last - 1, turn_banks[0])
-        coarse_passes([0], range(2))
-        finish_piece(last - 2, 0)
-        finish_piece(last - 2, 1)
-        subtract(last, 0)
-        coarse_passes([1], range(2))
-        subtract(last, 1)
-        interleave_dy(GROUPS - 1, 0)
-        turn_detail(last, turn_banks[0])
-        interleave_dy(GROUPS - 1, 1)
-        coarse_passes([2], range(2))
-        finish_piece(last - 2, 2)
-        finish_piece(last - 2, 3)
-        quantize_dx(last - 1)
-        quantize_call(CALLS - 2)
+        quantize_call(("first", last))
+        quantize_call(("made", last))
         products_pool(last)
+        turn_detail(last, int_banks[1])
+        turn_mtf(1, 3, C0)
+        interleave_dy(GROUPS - 1, 0)
+        detail_out(last, int_banks[1])
+        interleave_dy(GROUPS - 1, 1)
+        coarse_passes([1], range(3))
         for n in range(4):
+            finish_piece(last - 2, n)
             inject(last - 1, n)
-        coarse_passes(range(3), [2])
-        coarse_passes([3], range(3))
-        for n in range(4):
-            finish_piece(last - 1, n)
-        quantize_dx(last)
-        quantize_call(CALLS - 1)
+            if n < 3:
+                coarse_passes([0], [n])
+        coarse_passes([2], range(3))
+        finish_piece(last - 1, 0)
+        finish_piece(last - 1, 1)
+        quantize_call(("made", PAIRS), 2048, 2048)
+        quantize_call(("made", PAIRS), 0, 1024)
+        coarse_passes([0, 1], [3])
         inject(last, 0)
-        for n in range(1, 4):
-            inject(last, n)
-            coarse_pass(n - 1, GROUPS - 1)
-        coarse_pass(ROW_TILES - 1, GROUPS - 1)
+        inject(last, 1)
+        coarse_out(0)
+        coarse_out(1)
+        scale_mtf_vector(1, 3, C0)
+        finish_piece(last - 1, 2)
+        quantize_call(("made", PAIRS), 1024, 1024)
+        coarse_passes([3], range(3))
+        coarse_passes([2, 3], [3])
+        finish_piece(last - 1, 3)
+        inject(last, 2)
+        inject(last, 3)
+        coarse_out(2)
+        coarse_out(3)
         for n in range(4):
             finish_piece(last, n)
-            coarse_out(n)

@@ -28,6 +28,7 @@ ROW_TILES = R // P
 COPY = mybir.ActivationFunctionType.Copy
 SHORT_PAIRS = (0, 1)
 WHOLE_PAIRS = PAIRS - 3
+VECTOR_COLUMNS = 192
 SLOTS = 5
 STAGE = 4096
 KEPT = 1024
@@ -64,7 +65,7 @@ def tile_pansharpen_detail_injection_s8_kernel(
         ident_b = one("ident_b", P, BF16)
         ones_b = one("ones_b", P, BF16)
         scale_col = one("scale_col", 4 * GROUPS, F32)
-        scale_wide = {g: one(f"scale_wide{g}_", 512, F32) for g in (0, 1, 3)}
+        scale_wide = {g: one(f"scale_wide{g}_", 512, F32) for g in (0, 1)}
         radio_col = one("radio_col", 8, BF16)
         radio_bc = one("radio_bc", K + 512, BF16)
         diag = one("diag", K, BF16)
@@ -293,8 +294,12 @@ def tile_pansharpen_detail_injection_s8_kernel(
             interleave(staged(dy_place[g], 1024 * half, 1024), rows)
 
         def products_pool(s):
-            cols = slice(0, K + 512)
+            cols = slice(0, K + 512 - (VECTOR_COLUMNS if s >= 2 else 0))
             nc.gpsimd.tensor_tensor(out=out_sb(s)[:, cols], in0=bands_sb[s][:, cols], in1=radio_bc[:, cols], op=MULT)
+
+        def products_vector(s):
+            cols = slice(K + 512 - VECTOR_COLUMNS, K + 512)
+            nc.vector.tensor_tensor(out=out_sb(s)[:, cols], in0=bands_sb[s][:, cols], in1=radio_bc[:, cols], op=MULT)
 
         def diag_matmuls(s, h, bank):
             values = staged_bands(s, 1)[:, 512 * h : 512 * (h + 1)]
@@ -431,7 +436,7 @@ def tile_pansharpen_detail_injection_s8_kernel(
             scale_mtf_scalar(g, C1)
 
         early = {
-            1: [(interleave_dy, 0, 0), (spread_scale, 3)],
+            1: [(interleave_dy, 0, 0)],
             2: [(interleave_mtf, 0, 2)],
             3: [(interleave_dy, 1, 0)],
             4: [(interleave_mtf, 1, 2), (widen_mtf, 1, 3)],
@@ -447,6 +452,8 @@ def tile_pansharpen_detail_injection_s8_kernel(
             6: [(diag_through, 7, 1, C1)],
         }
         for s in range(1, last):
+            if s >= 2:
+                products_vector(s)
             quantize_call(("first", s))
             quantize_call(("made", s))
             products_pool(s)
@@ -471,6 +478,7 @@ def tile_pansharpen_detail_injection_s8_kernel(
             subtract(s + 1, 0)
             subtract(s + 1, 1)
 
+        products_vector(last)
         quantize_call(("first", last))
         quantize_call(("made", last))
         products_pool(last)
@@ -479,6 +487,8 @@ def tile_pansharpen_detail_injection_s8_kernel(
         interleave_dy(GROUPS - 1, 0)
         detail_out(last, int_banks[1])
         interleave_dy(GROUPS - 1, 1)
+        scale_mtf_scalar(3, C0)
+        interleave_mtf(1, 3)
         coarse_passes([1], range(3))
         for n in range(4):
             finish_piece(last - 2, n)
@@ -490,17 +500,16 @@ def tile_pansharpen_detail_injection_s8_kernel(
         finish_piece(last - 1, 1)
         quantize_call(("made", PAIRS), 2048, 2048)
         quantize_call(("made", PAIRS), 0, 1024)
+        coarse_passes([3], range(3))
         coarse_passes([0, 1], [3])
         inject(last, 0)
         inject(last, 1)
         coarse_out(0)
         coarse_out(1)
-        scale_mtf_vector(1, 3, C0)
         finish_piece(last - 1, 2)
-        quantize_call(("made", PAIRS), 1024, 1024)
-        coarse_passes([3], range(3))
-        coarse_passes([2, 3], [3])
         finish_piece(last - 1, 3)
+        quantize_call(("made", PAIRS), 1024, 1024)
+        coarse_passes([2, 3], [3])
         inject(last, 2)
         inject(last, 3)
         coarse_out(2)

@@ -28,7 +28,6 @@ ROW_TILES = R // P
 COPY = mybir.ActivationFunctionType.Copy
 SHORT_PAIRS = (0, 1)
 WHOLE_PAIRS = PAIRS - 3
-VECTOR_COLUMNS = 192
 SLOTS = 5
 STAGE = 4096
 KEPT = 1024
@@ -76,7 +75,7 @@ def tile_pansharpen_detail_injection_s8_kernel(
         bands_sb = tiles("bands_sb", PAIRS, 2 * K, BF16)
         pan_sb = tiles("pan_sb", PAIRS, 2 * C, BF16)
         codes = tiles("codes", GROUPS, ROW_TILES * 512, U8)
-        mtf_b = tiles("mtf_b", 4, 1024, BF16)
+        mtf_b = tiles("mtf_b", 6, 1024, BF16)
         planes = one("planes", 1024, BF16)
         work = tiles("work", SLOTS, KEPT + 2 * 2 * K, BF16)
         made = tiles("made", MADE_SLOTS, STAGE, BF16)
@@ -137,15 +136,16 @@ def tile_pansharpen_detail_injection_s8_kernel(
         load_pan(1)
         load_codes(1)
         load_bands(3)
+        load_codes(2)
+        load_pan(2)
+        load_codes(3)
         load(gain_w[:].bitcast(I32), gain_words[0].bitcast(I32))
         for q in range(4):
             load(gain_s[32 * q : 32 * q + 4, :].bitcast(I32), gain_scales[0][4 * q : 4 * q + 4, :].bitcast(I32))
-        for s in range(2, PAIRS):
+        for s in range(3, PAIRS):
+            if s + 1 < PAIRS:
+                load_bands(s + 1)
             load_pan(s)
-            if s < GROUPS:
-                load_codes(s)
-            if s + 2 < PAIRS:
-                load_bands(s + 2)
 
         nc.scalar.activation(out=ident_b[:], in_=ident[:], func=COPY)
 
@@ -209,7 +209,7 @@ def tile_pansharpen_detail_injection_s8_kernel(
             quantize(mix_c[h][:, cols], mix_s[h][:, cols], mix_il[h][:, K * u : K * (u + 1)])
 
         def widen_mtf(a, g):
-            nc.scalar.copy(out=mtf_b[2 * (g % 2) + a][:], in_=codes[g][:, 1024 * a : 1024 * (a + 1)].bitcast(FP8))
+            nc.scalar.copy(out=mtf_b[2 * (g % 3) + a][:], in_=codes[g][:, 1024 * a : 1024 * (a + 1)].bitcast(FP8))
 
         def spread_scale(g):
             nc.scalar.copy(
@@ -218,7 +218,7 @@ def tile_pansharpen_detail_injection_s8_kernel(
             )
 
         def turn_mtf(a, g, bank):
-            doubles = mtf_b[2 * (g % 2) + a][:].bitcast(F32)
+            doubles = mtf_b[2 * (g % 3) + a][:].bitcast(F32)
             for n in range(4):
                 u, i = n // 2, n % 2
                 nc.tensor.transpose(bank[:, P * n : P * (n + 1)], doubles[:, 256 * i + u : 256 * (i + 1) : 2], ident[:])
@@ -294,12 +294,8 @@ def tile_pansharpen_detail_injection_s8_kernel(
             interleave(staged(dy_place[g], 1024 * half, 1024), rows)
 
         def products_pool(s):
-            cols = slice(0, K + 512 - (VECTOR_COLUMNS if s >= 2 else 0))
+            cols = slice(0, K + 512)
             nc.gpsimd.tensor_tensor(out=out_sb(s)[:, cols], in0=bands_sb[s][:, cols], in1=radio_bc[:, cols], op=MULT)
-
-        def products_vector(s):
-            cols = slice(K + 512 - VECTOR_COLUMNS, K + 512)
-            nc.vector.tensor_tensor(out=out_sb(s)[:, cols], in0=bands_sb[s][:, cols], in1=radio_bc[:, cols], op=MULT)
 
         def diag_matmuls(s, h, bank):
             values = staged_bands(s, 1)[:, 512 * h : 512 * (h + 1)]
@@ -428,6 +424,7 @@ def tile_pansharpen_detail_injection_s8_kernel(
         turn_mtf(0, 1, H[0])
         turn_mtf(1, 1, H[1])
         widen_mtf(0, 2)
+        widen_mtf(1, 2)
         subtract(1, 0)
         subtract(1, 1)
 
@@ -436,24 +433,22 @@ def tile_pansharpen_detail_injection_s8_kernel(
             scale_mtf_scalar(g, C1)
 
         early = {
-            1: [(interleave_dy, 0, 0)],
+            1: [(interleave_dy, 0, 0), (widen_mtf, 0, 3)],
             2: [(interleave_mtf, 0, 2)],
             3: [(interleave_dy, 1, 0)],
-            4: [(interleave_mtf, 1, 2), (widen_mtf, 1, 3)],
+            4: [(interleave_mtf, 1, 2)],
             5: [(interleave_dy, 2, 0)],
             6: [(interleave_mtf, 0, 3), (interleave_dy, 2, 1)],
         }
         late = {
             1: [(scale_unit, 0, 2)],
-            2: [(interleave_dy, 0, 1), (widen_mtf, 1, 2)],
+            2: [(interleave_dy, 0, 1)],
             3: [(scale_unit, 1, 2)],
-            4: [(interleave_dy, 1, 1), (widen_mtf, 0, 3)],
+            4: [(interleave_dy, 1, 1), (widen_mtf, 1, 3)],
             5: [(scale_unit, 0, 3)],
             6: [(diag_through, 7, 1, C1)],
         }
         for s in range(1, last):
-            if s >= 2:
-                products_vector(s)
             quantize_call(("first", s))
             quantize_call(("made", s))
             products_pool(s)
@@ -478,7 +473,6 @@ def tile_pansharpen_detail_injection_s8_kernel(
             subtract(s + 1, 0)
             subtract(s + 1, 1)
 
-        products_vector(last)
         quantize_call(("first", last))
         quantize_call(("made", last))
         products_pool(last)

@@ -175,7 +175,7 @@ def tile_pansharpen_detail_injection_s8_kernel(
 
         def interleave(dst, rows):
             nc.scalar.copy(
-                out=dst.rearrange("p (m i j) -> p m j i", i=4, j=4), in_=rows.rearrange("p j (m i) -> p m j i", i=4)
+                out=dst.rearrange("p (m i j) -> p m j i", i=2, j=4), in_=rows.rearrange("p j (m i) -> p m j i", i=2)
             )
 
         def build_diag():
@@ -189,8 +189,8 @@ def tile_pansharpen_detail_injection_s8_kernel(
         def spread_radio(h, bank):
             nc.tensor.matmul(bank, ones_b[:], diag[:, 512 * h : 512 * (h + 1)], start=True, stop=True)
 
-        def radio_out(h, bank):
-            nc.scalar.copy(
+        def radio_out(h, bank, copy=nc.scalar.copy):
+            copy(
                 out=radio_bc[:, 512 * h : 512 * (h + 1)].rearrange("p (m j) -> p m j", j=4),
                 in_=bank.rearrange("p (j m) -> p m j", j=4),
             )
@@ -389,16 +389,16 @@ def tile_pansharpen_detail_injection_s8_kernel(
         spread_radio(0, H[0])
         spread_radio(1, H[1])
         radio_out(0, H[0])
-        radio_out(1, H[1])
+        spread_scale(0)
         bands_through(1, 0, H[2])
         bands_through(1, 1, H[3])
         diag_matmuls(0, 1, C0)
         quantize_mix(1, 0)
         quantize_call(("first", -1))
         quantize_mix(1, 1)
+        radio_out(1, H[1], nc.vector.tensor_copy)
         quantize_call(("first", 0))
         widen_mtf(0, 0)
-        spread_scale(0)
         widen_mtf(1, 0)
         repeat_radio()
         diag_out(0, 1, C0)

@@ -85,14 +85,15 @@ def tile_pansharpen_detail_injection_s8_kernel(
         last = PAIRS - 1
         call_in = {("first", s): work[s % SLOTS][:, 0:2048] for s in range(-1, PAIRS)}
         for s in range(1, PAIRS + 1):
-            call_in["made", s] = made[s % MADE_SLOTS][:, 0 : STAGE if s in (4, 6, 8) else 2048]
+            call_in["made", s] = made[s % MADE_SLOTS][:, 0 : STAGE if s in (4, 6, 7, 8) else 2048]
         call_c = {c: one(f"call_c_{c[0]}{c[1] + 1}_", src.shape[1] // 4, U32) for c, src in call_in.items()}
         call_s = {c: one(f"call_s_{c[0]}{c[1] + 1}_", src.shape[1] // 4, U8) for c, src in call_in.items()}
         bands_place = [(("first", s - 1), 0) for s in range(PAIRS)]
         dx_place = [(("made", s + 1), 0) for s in range(PAIRS)]
-        dy_place = [(("made", 4), 2048), (("made", 6), 2048), (("first", last), 0), (("made", PAIRS), 2048)]
+        dy_place = [(("made", 4), 2048), (("made", 6), 2048), (("made", last), 2048), (("made", PAIRS), 2048)]
         units = [(a, g) for g in range(GROUPS) for a in range(2)]
         mtf_place = {unit: (("made", n + 1), 1024) for n, unit in enumerate(units)}
+        mtf_place[0, GROUPS - 1] = (("first", last), 1024)
         mix_raw = [work[3][:, 2048 * h : 2048 * (h + 1)] for h in range(HALVES)]
         mix_il = [made[0][:, 2048 * h : 2048 * (h + 1)] for h in range(HALVES)]
 
@@ -428,27 +429,10 @@ def tile_pansharpen_detail_injection_s8_kernel(
         subtract(1, 0)
         subtract(1, 1)
 
-        def scale_unit(a, g):
-            turn_mtf(a, g, C1)
-            scale_mtf_scalar(g, C1)
-
-        early = {
-            1: [(interleave_dy, 0, 0), (widen_mtf, 0, 3)],
-            2: [(interleave_mtf, 0, 2)],
-            3: [(interleave_dy, 1, 0)],
-            4: [(interleave_mtf, 1, 2)],
-            5: [(interleave_dy, 2, 0)],
-            6: [(interleave_mtf, 0, 3), (interleave_dy, 2, 1)],
-        }
-        late = {
-            1: [(scale_unit, 0, 2)],
-            2: [(interleave_dy, 0, 1)],
-            3: [(scale_unit, 1, 2)],
-            4: [(interleave_dy, 1, 1), (widen_mtf, 1, 3)],
-            5: [(scale_unit, 0, 3)],
-            6: [(diag_through, 7, 1, C1)],
-        }
+        scalar_units = units[4:]
         for s in range(1, last):
+            odd = s % 2 == 1
+            group = (s - 1) // 2
             quantize_call(("first", s))
             quantize_call(("made", s))
             products_pool(s)
@@ -457,13 +441,22 @@ def tile_pansharpen_detail_injection_s8_kernel(
             if s + 2 <= last:
                 bands_through(s + 2, 0, C0)
                 bands_through(s + 2, 1, C1)
-            for f, *args in early[s]:
-                f(*args)
+            if odd:
+                interleave_dy(group, 0)
+            else:
+                interleave_mtf(*scalar_units[group])
             intensity(s + 1, 0)
             intensity(s + 1, 1)
             diag_through(s, 1, C0)
-            for f, *args in late[s]:
-                f(*args)
+            if odd:
+                turn_mtf(*scalar_units[group], C1)
+                scale_mtf_scalar(scalar_units[group][1], C1)
+            elif s + 1 < last:
+                interleave_dy(group, 1)
+                widen_mtf(group, GROUPS - 1)
+            else:
+                diag_through(last, 1, C1)
+                interleave_dy(group, 1)
             if s == 1:
                 scale_mtf_vector(0, 1, H[0])
                 scale_mtf_vector(1, 1, H[1])
@@ -473,8 +466,8 @@ def tile_pansharpen_detail_injection_s8_kernel(
             subtract(s + 1, 0)
             subtract(s + 1, 1)
 
-        quantize_call(("first", last))
-        quantize_call(("made", last))
+        quantize_call(("first", last), 1024, 1024)
+        quantize_call(("made", last), 0, 1024)
         products_pool(last)
         turn_detail(last, int_banks[1])
         turn_mtf(1, 3, C0)
@@ -483,21 +476,24 @@ def tile_pansharpen_detail_injection_s8_kernel(
         interleave_dy(GROUPS - 1, 1)
         scale_mtf_scalar(3, C0)
         interleave_mtf(1, 3)
-        coarse_passes([1], range(3))
+        coarse_passes([1], range(2))
         for n in range(4):
             finish_piece(last - 2, n)
             inject(last - 1, n)
-            if n < 3:
+            if n < 2:
                 coarse_passes([0], [n])
-        coarse_passes([2], range(3))
+        coarse_passes([2], range(2))
         finish_piece(last - 1, 0)
         finish_piece(last - 1, 1)
+        quantize_call(("made", last), 2048, 2048)
         quantize_call(("made", PAIRS), 2048, 2048)
         quantize_call(("made", PAIRS), 0, 1024)
-        coarse_passes([3], range(3))
+        coarse_passes([0, 1], [2])
         coarse_passes([0, 1], [3])
         inject(last, 0)
         inject(last, 1)
+        coarse_passes([3], range(3))
+        coarse_passes([2], [2])
         coarse_out(0)
         coarse_out(1)
         finish_piece(last - 1, 2)

@@ -209,8 +209,8 @@ def tile_pansharpen_detail_injection_s8_kernel(
             cols = slice(256 * u, 256 * (u + 1))
             quantize(mix_c[h][:, cols], mix_s[h][:, cols], mix_il[h][:, K * u : K * (u + 1)])
 
-        def widen_mtf(a, g):
-            nc.scalar.copy(out=mtf_b[2 * (g % 3) + a][:], in_=codes[g][:, 1024 * a : 1024 * (a + 1)].bitcast(FP8))
+        def widen_mtf(a, g, copy=nc.scalar.copy):
+            copy(out=mtf_b[2 * (g % 3) + a][:], in_=codes[g][:, 1024 * a : 1024 * (a + 1)].bitcast(FP8))
 
         def spread_scale(g):
             nc.scalar.copy(
@@ -397,9 +397,9 @@ def tile_pansharpen_detail_injection_s8_kernel(
         quantize_mix(1, 0)
         quantize_call(("first", -1))
         quantize_mix(1, 1)
-        radio_out(1, H[1], nc.vector.tensor_copy)
+        widen_mtf(0, 0, nc.vector.tensor_copy)
         quantize_call(("first", 0))
-        widen_mtf(0, 0)
+        radio_out(1, H[1])
         widen_mtf(1, 0)
         repeat_radio()
         diag_out(0, 1, C0)

@@ -73,7 +73,8 @@ def tile_pansharpen_detail_injection_s8_kernel(
         mix_c = tiles("mix_c", HALVES, C, U32)
         mix_s = tiles("mix_s", HALVES, C, U8)
         bands_sb = tiles("bands_sb", PAIRS, 2 * K, BF16)
-        pan_sb = tiles("pan_sb", PAIRS, 2 * C, BF16)
+        pan_groups = tiles("pan_group", GROUPS, 4 * C, BF16)
+        pan_sb = [pan_groups[s // 2][:, 2 * C * (s % 2) : 2 * C * (s % 2 + 1)] for s in range(PAIRS)]
         codes = tiles("codes", GROUPS, ROW_TILES * 512, U8)
         mtf_b = tiles("mtf_b", 6, 1024, BF16)
         planes = one("planes", 1024, BF16)
@@ -88,12 +89,14 @@ def tile_pansharpen_detail_injection_s8_kernel(
             call_in["made", s] = made[s % MADE_SLOTS][:, 0 : STAGE if s in (4, 6, 7, 8) else 2048]
         call_c = {c: one(f"call_c_{c[0]}{c[1] + 1}_", src.shape[1] // 4, U32) for c, src in call_in.items()}
         call_s = {c: one(f"call_s_{c[0]}{c[1] + 1}_", src.shape[1] // 4, U8) for c, src in call_in.items()}
-        bands_place = [(("first", s - 1), 0) for s in range(PAIRS)]
-        dx_place = [(("made", s + 1), 0) for s in range(PAIRS)]
+        bands_place = {(s, t): (("first" if t else "made", s - 1), 0) for s in range(PAIRS) for t in range(2)}
+        bands_place[0, 0] = (("first", -1), K)
+        bands_place[1, 0] = (("first", 0), K)
+        dx_place = [(("first", s + 1), K) for s in range(last)] + [(("made", PAIRS), 0)]
         dy_place = [(("made", 4), 2048), (("made", 6), 2048), (("made", last), 2048), (("made", PAIRS), 2048)]
         units = [(a, g) for g in range(GROUPS) for a in range(2)]
         mtf_place = {unit: (("made", n + 1), 1024) for n, unit in enumerate(units)}
-        mtf_place[0, GROUPS - 1] = (("first", last), 1024)
+        mtf_place[0, GROUPS - 1] = (("first", last), 0)
         mix_raw = [work[3][:, 2048 * h : 2048 * (h + 1)] for h in range(HALVES)]
         mix_il = [made[0][:, 2048 * h : 2048 * (h + 1)] for h in range(HALVES)]
 
@@ -120,7 +123,10 @@ def tile_pansharpen_detail_injection_s8_kernel(
             load(bands_sb[s][:], bands_v[s // 2, s % 2])
 
         def load_pan(s):
-            load(pan_sb[s][:], pan_v[s // 2, s % 2])
+            load(pan_sb[s], pan_v[s // 2, s % 2])
+
+        def load_pan_group(g):
+            load(pan_groups[g][:], pan.rearrange("(g p j) c -> g p (j c)", p=P, j=4)[g])
 
         def load_codes(g):
             load(codes[g][:].rearrange("p (r k) -> p r k", r=ROW_TILES), mtf_v[g])
@@ -138,15 +144,15 @@ def tile_pansharpen_detail_injection_s8_kernel(
         load_codes(1)
         load_bands(3)
         load_codes(2)
-        load_pan(2)
+        load_pan_group(1)
         load_codes(3)
         load(gain_w[:].bitcast(I32), gain_words[0].bitcast(I32))
         for q in range(4):
             load(gain_s[32 * q : 32 * q + 4, :].bitcast(I32), gain_scales[0][4 * q : 4 * q + 4, :].bitcast(I32))
-        for s in range(3, PAIRS):
-            if s + 1 < PAIRS:
-                load_bands(s + 1)
-            load_pan(s)
+        for s in range(4, PAIRS):
+            load_bands(s)
+            if s % 2 == 0:
+                load_pan_group(s // 2)
 
         nc.scalar.activation(out=ident_b[:], in_=ident[:], func=COPY)
 
@@ -199,15 +205,14 @@ def tile_pansharpen_detail_injection_s8_kernel(
         def repeat_radio():
             nc.scalar.copy(out=radio_bc[:, K : K + 512], in_=radio_bc[:, 0:512])
 
-        def interleave_mix(h, u):
+        def interleave_mix(h):
             nc.vector.tensor_copy(
-                out=mix_il[h][:, K * u : K * (u + 1)].rearrange("p (m e j) -> p m j e", e=2, j=4),
-                in_=mix_raw[h].rearrange("p (j m u e) -> p u m j e", u=2, e=2, j=4)[:, u],
+                out=mix_il[h].rearrange("p (u m e j) -> p m j u e", u=2, e=2, j=4),
+                in_=mix_raw[h].rearrange("p (j m u e) -> p m j u e", u=2, e=2, j=4),
             )
 
-        def quantize_mix(h, u):
-            cols = slice(256 * u, 256 * (u + 1))
-            quantize(mix_c[h][:, cols], mix_s[h][:, cols], mix_il[h][:, K * u : K * (u + 1)])
+        def quantize_mix(h):
+            quantize(mix_c[h][:], mix_s[h][:], mix_il[h])
 
         def widen_mtf(a, g, copy=nc.scalar.copy):
             copy(out=mtf_b[2 * (g % 3) + a][:], in_=codes[g][:, 1024 * a : 1024 * (a + 1)].bitcast(FP8))
@@ -246,7 +251,7 @@ def tile_pansharpen_detail_injection_s8_kernel(
             interleave(staged(mtf_place[a, g], 0, 1024), planes[:].rearrange("p (j x) -> p j x", j=4))
 
         def staged_bands(s, t):
-            return staged(bands_place[s], K * (1 - t), K)
+            return staged(bands_place[s, t], 0, K)
 
         def turn_bands(s, t, bank):
             doubles = bands_sb[s][:, K * t : K * (t + 1)].bitcast(F32)
@@ -258,9 +263,9 @@ def tile_pansharpen_detail_injection_s8_kernel(
             turn_out(bank, staged_bands(s, t))
 
         def intensity_pass(s, t, h):
-            x_c, x_s = operand(bands_place[s], 256 * (1 - t) + P * h, P)
+            x_c, x_s = operand(bands_place[s, t], P * h, P)
             nc.tensor.matmul_mx(
-                out=int_banks[t],
+                out=int_banks[1 - t],
                 lhsT=x_c,
                 lhsT_scale=x_s,
                 rhs=mix_c[h][:].bitcast(FP8X4),
@@ -278,7 +283,7 @@ def tile_pansharpen_detail_injection_s8_kernel(
             nc.vector.tensor_tensor(
                 out=detail[s // 2 % 2][:, C * row : C * (row + 1)].rearrange("p (u m e) -> p u m e", u=2, e=2),
                 in0=pan_sb[s][:, C * t : C * (t + 1)].rearrange("p (m u e) -> p u m e", u=2, e=2),
-                in1=int_banks[t].rearrange("p (u m e) -> p u m e", u=2, e=2),
+                in1=int_banks[1 - t].rearrange("p (u m e) -> p u m e", u=2, e=2),
                 op=SUB,
             )
 
@@ -379,49 +384,44 @@ def tile_pansharpen_detail_injection_s8_kernel(
                 inject(s, n)
 
         build_diag()
-        interleave_mix(0, 0)
-        interleave_mix(0, 1)
-        quantize_mix(0, 0)
-        quantize_mix(0, 1)
-        interleave_mix(1, 0)
-        interleave_mix(1, 1)
-        bands_through(0, 0, C0)
-        bands_through(0, 1, C1)
         spread_radio(0, H[0])
         spread_radio(1, H[1])
         radio_out(0, H[0])
-        spread_scale(0)
+        radio_out(1, H[1])
+        interleave_mix(0)
+        quantize_mix(0)
+        interleave_mix(1)
+        bands_through(0, 0, C0)
+        bands_through(0, 1, C1)
+        repeat_radio()
         bands_through(1, 0, H[2])
         bands_through(1, 1, H[3])
         diag_matmuls(0, 1, C0)
-        quantize_mix(1, 0)
         quantize_call(("first", -1))
-        quantize_mix(1, 1)
+        quantize_mix(1)
         widen_mtf(0, 0, nc.vector.tensor_copy)
         quantize_call(("first", 0))
-        radio_out(1, H[1])
         widen_mtf(1, 0)
-        repeat_radio()
+        spread_scale(0)
         diag_out(0, 1, C0)
         intensity(0, 0)
         intensity(0, 1)
         products_pool(0)
+        spread_scale(1)
         turn_mtf(0, 0, C1)
-        turn_bands(2, 0, H[2])
-        turn_mtf(1, 0, H[1])
+        turn_mtf(1, 0, H[0])
+        widen_mtf(0, 1)
         subtract(0, 0)
         subtract(0, 1)
-        scale_mtf_vector(0, 0, C1)
-        turn_detail(0, H[0])
-        widen_mtf(0, 1)
-        detail_out(0, H[0])
-        bands_out(2, 0, H[2])
-        bands_through(2, 1, H[3])
+        turn_detail(0, H[3])
+        detail_out(0, H[3])
         intensity(1, 0)
-        intensity(1, 1)
-        scale_mtf_vector(1, 0, H[1])
         widen_mtf(1, 1)
-        spread_scale(1)
+        bands_through(2, 0, H[1])
+        bands_through(2, 1, H[2])
+        scale_mtf_vector(0, 0, C1)
+        scale_mtf_vector(1, 0, H[0])
+        intensity(1, 1)
         turn_mtf(0, 1, H[0])
         turn_mtf(1, 1, H[1])
         widen_mtf(0, 2)
@@ -430,7 +430,26 @@ def tile_pansharpen_detail_injection_s8_kernel(
         subtract(1, 1)
 
         scalar_units = units[4:]
-        for s in range(1, last):
+        quantize_call(("first", 1))
+        quantize_call(("made", 1))
+        products_pool(1)
+        diag_through(1, 1, C0)
+        intensity(2, 1)
+        interleave_dy(0, 0)
+        turn_detail(1, H[2])
+        detail_out(1, H[2])
+        bands_through(3, 0, H[3])
+        intensity(2, 0)
+        bands_through(3, 1, C0)
+        scale_mtf_vector(0, 1, H[0])
+        scale_mtf_vector(1, 1, H[1])
+        turn_mtf(*scalar_units[0], C1)
+        scale_mtf_scalar(scalar_units[0][1], C1)
+        inject_pair(0)
+        subtract(2, 1)
+        subtract(2, 0)
+
+        for s in range(2, last):
             odd = s % 2 == 1
             group = (s - 1) // 2
             quantize_call(("first", s))
@@ -445,8 +464,8 @@ def tile_pansharpen_detail_injection_s8_kernel(
                 interleave_dy(group, 0)
             else:
                 interleave_mtf(*scalar_units[group])
-            intensity(s + 1, 0)
             intensity(s + 1, 1)
+            intensity(s + 1, 0)
             diag_through(s, 1, C0)
             if odd:
                 turn_mtf(*scalar_units[group], C1)
@@ -457,17 +476,13 @@ def tile_pansharpen_detail_injection_s8_kernel(
             else:
                 diag_through(last, 1, C1)
                 interleave_dy(group, 1)
-            if s == 1:
-                scale_mtf_vector(0, 1, H[0])
-                scale_mtf_vector(1, 1, H[1])
-            else:
-                finish(s - 2)
+            finish(s - 2)
             inject_pair(s - 1)
-            subtract(s + 1, 0)
             subtract(s + 1, 1)
+            subtract(s + 1, 0)
 
-        quantize_call(("first", last), 1024, 1024)
-        quantize_call(("made", last), 0, 1024)
+        quantize_call(("first", last), K, K)
+        quantize_call(("first", last), 0, K)
         products_pool(last)
         turn_detail(last, int_banks[1])
         turn_mtf(1, 3, C0)

@@ -80,20 +80,20 @@ def tile_pansharpen_detail_injection_s8_kernel(
         planes = one("planes", 1024, BF16)
         work = tiles("work", SLOTS, KEPT + 2 * 2 * K, BF16)
         made = tiles("made", MADE_SLOTS, STAGE, BF16)
-        detail = tiles("detail", 2, 4 * C, BF16)
+        detail = tiles("detail", GROUPS, 4 * C, BF16)
         res = tiles("res", ROW_TILES // 2, 2 * C, F32)
 
         last = PAIRS - 1
         call_in = {("first", s): work[s % SLOTS][:, 0:2048] for s in range(-1, PAIRS)}
         for s in range(1, PAIRS + 1):
-            call_in["made", s] = made[s % MADE_SLOTS][:, 0 : STAGE if s in (4, 6, 7, 8) else 2048]
+            call_in["made", s] = made[s % MADE_SLOTS][:, 0 : STAGE if s in (4, 6, 8) else 2048]
         call_c = {c: one(f"call_c_{c[0]}{c[1] + 1}_", src.shape[1] // 4, U32) for c, src in call_in.items()}
         call_s = {c: one(f"call_s_{c[0]}{c[1] + 1}_", src.shape[1] // 4, U8) for c, src in call_in.items()}
         bands_place = {(s, t): (("first" if t else "made", s - 1), 0) for s in range(PAIRS) for t in range(2)}
         bands_place[0, 0] = (("first", -1), K)
         bands_place[1, 0] = (("first", 0), K)
         dx_place = [(("first", s + 1), K) for s in range(last)] + [(("made", PAIRS), 0)]
-        dy_place = [(("made", 4), 2048), (("made", 6), 2048), (("made", last), 2048), (("made", PAIRS), 2048)]
+        dy_place = [(("made", 4), 2048), (("made", 6), 2048), (("made", last), 0), (("made", PAIRS), 2048)]
         units = [(a, g) for g in range(GROUPS) for a in range(2)]
         mtf_place = {unit: (("made", n + 1), 1024) for n, unit in enumerate(units)}
         mtf_place[0, GROUPS - 1] = (("first", last), 0)
@@ -140,8 +140,8 @@ def tile_pansharpen_detail_injection_s8_kernel(
         load_codes(0)
         load_pan(0)
         load_bands(2)
-        load_pan(1)
         load_codes(1)
+        load_pan(1)
         load_bands(3)
         load_codes(2)
         load_pan_group(1)
@@ -281,14 +281,14 @@ def tile_pansharpen_detail_injection_s8_kernel(
         def subtract(s, t):
             row = 2 * (s % 2) + t
             nc.vector.tensor_tensor(
-                out=detail[s // 2 % 2][:, C * row : C * (row + 1)].rearrange("p (u m e) -> p u m e", u=2, e=2),
+                out=detail[s // 2][:, C * row : C * (row + 1)].rearrange("p (u m e) -> p u m e", u=2, e=2),
                 in0=pan_sb[s][:, C * t : C * (t + 1)].rearrange("p (m u e) -> p u m e", u=2, e=2),
                 in1=int_banks[1 - t].rearrange("p (u m e) -> p u m e", u=2, e=2),
                 op=SUB,
             )
 
         def turn_detail(s, bank):
-            doubles = detail[s // 2 % 2][:, 1024 * (s % 2) : 1024 * (s % 2 + 1)].bitcast(F32)
+            doubles = detail[s // 2][:, 1024 * (s % 2) : 1024 * (s % 2 + 1)].bitcast(F32)
             for n in range(4):
                 nc.tensor.transpose(bank[:, P * n : P * (n + 1)], doubles[:, P * n : P * (n + 1)], ident[:])
 
@@ -296,7 +296,7 @@ def tile_pansharpen_detail_injection_s8_kernel(
             turn_out(bank, staged(dx_place[s], 0, 1024))
 
         def interleave_dy(g, half):
-            rows = detail[g % 2][:].rearrange("p (j c) -> p j c", j=4)[:, :, 256 * half : 256 * (half + 1)]
+            rows = detail[g][:].rearrange("p (j c) -> p j c", j=4)[:, :, 256 * half : 256 * (half + 1)]
             interleave(staged(dy_place[g], 1024 * half, 1024), rows)
 
         def products_pool(s):
@@ -407,16 +407,15 @@ def tile_pansharpen_detail_injection_s8_kernel(
         intensity(0, 0)
         intensity(0, 1)
         products_pool(0)
-        spread_scale(1)
         turn_mtf(0, 0, C1)
         turn_mtf(1, 0, H[0])
         widen_mtf(0, 1)
+        widen_mtf(1, 1)
         subtract(0, 0)
         subtract(0, 1)
         turn_detail(0, H[3])
         detail_out(0, H[3])
         intensity(1, 0)
-        widen_mtf(1, 1)
         bands_through(2, 0, H[1])
         bands_through(2, 1, H[2])
         scale_mtf_vector(0, 0, C1)
@@ -424,8 +423,8 @@ def tile_pansharpen_detail_injection_s8_kernel(
         intensity(1, 1)
         turn_mtf(0, 1, H[0])
         turn_mtf(1, 1, H[1])
+        spread_scale(1)
         widen_mtf(0, 2)
-        widen_mtf(1, 2)
         subtract(1, 0)
         subtract(1, 1)
 
@@ -464,6 +463,8 @@ def tile_pansharpen_detail_injection_s8_kernel(
                 interleave_dy(group, 0)
             else:
                 interleave_mtf(*scalar_units[group])
+            if s == last - 1:
+                widen_mtf(*scalar_units[group + 1])
             intensity(s + 1, 1)
             intensity(s + 1, 0)
             diag_through(s, 1, C0)
@@ -472,7 +473,7 @@ def tile_pansharpen_detail_injection_s8_kernel(
                 scale_mtf_scalar(scalar_units[group][1], C1)
             elif s + 1 < last:
                 interleave_dy(group, 1)
-                widen_mtf(group, GROUPS - 1)
+                widen_mtf(*scalar_units[group + 1])
             else:
                 diag_through(last, 1, C1)
                 interleave_dy(group, 1)
@@ -500,7 +501,7 @@ def tile_pansharpen_detail_injection_s8_kernel(
         coarse_passes([2], range(2))
         finish_piece(last - 1, 0)
         finish_piece(last - 1, 1)
-        quantize_call(("made", last), 2048, 2048)
+        quantize_call(("made", last))
         quantize_call(("made", PAIRS), 2048, 2048)
         quantize_call(("made", PAIRS), 0, 1024)
         coarse_passes([0, 1], [2])

@@ -31,6 +31,9 @@ WHOLE_PAIRS = PAIRS - 3
 SLOTS = 5
 STAGE = 4096
 KEPT = 1024
+WORK = KEPT + 2 * 2 * K
+SHORT = 144
+AHEAD = range(2, 5)
 MADE_SLOTS = 3
 
 
@@ -72,13 +75,15 @@ def tile_pansharpen_detail_injection_s8_kernel(
         gain_s = one("gain_s", K, U8)
         mix_c = tiles("mix_c", HALVES, C, U32)
         mix_s = tiles("mix_s", HALVES, C, U8)
-        bands_sb = tiles("bands_sb", PAIRS, 2 * K, BF16)
+        bands_all = one("bands_all", PAIRS * 2 * K, BF16)
+        bands_sb = [bands_all[:, 2 * K * s : 2 * K * (s + 1)] for s in range(PAIRS)]
         pan_groups = tiles("pan_group", GROUPS, 4 * C, BF16)
         pan_sb = [pan_groups[s // 2][:, 2 * C * (s % 2) : 2 * C * (s % 2 + 1)] for s in range(PAIRS)]
         codes = tiles("codes", GROUPS, ROW_TILES * 512, U8)
         mtf_b = tiles("mtf_b", 6, 1024, BF16)
         planes = one("planes", 1024, BF16)
-        work = tiles("work", SLOTS, KEPT + 2 * 2 * K, BF16)
+        work_all = one("work", SLOTS * WORK, BF16)
+        work = [work_all[:, WORK * i : WORK * (i + 1)] for i in range(SLOTS)]
         made = tiles("made", MADE_SLOTS, STAGE, BF16)
         detail = tiles("detail", GROUPS, 4 * C, BF16)
         res = tiles("res", ROW_TILES // 2, 2 * C, F32)
@@ -120,7 +125,7 @@ def tile_pansharpen_detail_injection_s8_kernel(
             nc.sync.dma_start(out=dst, in_=src)
 
         def load_bands(s):
-            load(bands_sb[s][:], bands_v[s // 2, s % 2])
+            load(bands_sb[s], bands_v[s // 2, s % 2])
 
         def load_pan(s):
             load(pan_sb[s], pan_v[s // 2, s % 2])
@@ -143,16 +148,18 @@ def tile_pansharpen_detail_injection_s8_kernel(
         load_codes(1)
         load_pan(1)
         load_bands(3)
+        load_bands(4)
         load_codes(2)
         load_pan_group(1)
         load_codes(3)
         load(gain_w[:].bitcast(I32), gain_words[0].bitcast(I32))
         for q in range(4):
             load(gain_s[32 * q : 32 * q + 4, :].bitcast(I32), gain_scales[0][4 * q : 4 * q + 4, :].bitcast(I32))
-        for s in range(4, PAIRS):
-            load_bands(s)
-            if s % 2 == 0:
-                load_pan_group(s // 2)
+        for g in range(2, GROUPS):
+            load_bands(2 * g + 1)
+            load_pan_group(g)
+            if g == 2:
+                load_bands(6)
 
         nc.scalar.activation(out=ident_b[:], in_=ident[:], func=COPY)
 
@@ -299,8 +306,23 @@ def tile_pansharpen_detail_injection_s8_kernel(
             rows = detail[g][:].rearrange("p (j c) -> p j c", j=4)[:, :, 256 * half : 256 * (half + 1)]
             interleave(staged(dy_place[g], 1024 * half, 1024), rows)
 
-        def products_pool(s):
-            cols = slice(0, K + 512)
+        short = slice(K + 512 - SHORT, K + 512)
+
+        def products_ahead():
+            pairs = slice(AHEAD.start, AHEAD.stop)
+            results = work_all[:].bitcast(F32).rearrange("p (a c) -> p a c", a=SLOTS)[:, pairs, KEPT // 2 :]
+            nc.gpsimd.tensor_tensor(
+                out=results[:, :, short],
+                in0=bands_all[:].rearrange("p (a c) -> p a c", a=PAIRS)[:, pairs, short],
+                in1=radio_bc[:, short].unsqueeze(1).to_broadcast([P, len(AHEAD), SHORT]),
+                op=MULT,
+            )
+
+        def products_vector(s):
+            nc.vector.tensor_tensor(out=out_sb(s)[:, short], in0=bands_sb[s][:, short], in1=radio_bc[:, short], op=MULT)
+
+        def products_pool(s, width=K + 512):
+            cols = slice(0, width)
             nc.gpsimd.tensor_tensor(out=out_sb(s)[:, cols], in0=bands_sb[s][:, cols], in1=radio_bc[:, cols], op=MULT)
 
         def diag_matmuls(s, h, bank):
@@ -407,6 +429,7 @@ def tile_pansharpen_detail_injection_s8_kernel(
         intensity(0, 0)
         intensity(0, 1)
         products_pool(0)
+        products_ahead()
         turn_mtf(0, 0, C1)
         turn_mtf(1, 0, H[0])
         widen_mtf(0, 1)
@@ -453,9 +476,10 @@ def tile_pansharpen_detail_injection_s8_kernel(
             group = (s - 1) // 2
             quantize_call(("first", s))
             quantize_call(("made", s))
-            products_pool(s)
-            turn_detail(s, int_banks[1])
-            detail_out(s, int_banks[1])
+            products_pool(s, short.start if s in AHEAD else short.stop)
+            detail_bank = int_banks[1] if s + 2 <= last else C0
+            turn_detail(s, detail_bank)
+            detail_out(s, detail_bank)
             if s + 2 <= last:
                 bands_through(s + 2, 0, C0)
                 bands_through(s + 2, 1, C1)
@@ -467,7 +491,7 @@ def tile_pansharpen_detail_injection_s8_kernel(
                 widen_mtf(*scalar_units[group + 1])
             intensity(s + 1, 1)
             intensity(s + 1, 0)
-            diag_through(s, 1, C0)
+            diag_through(s, 1, C0 if s + 2 <= last else C1)
             if odd:
                 turn_mtf(*scalar_units[group], C1)
                 scale_mtf_scalar(scalar_units[group][1], C1)
@@ -475,7 +499,7 @@ def tile_pansharpen_detail_injection_s8_kernel(
                 interleave_dy(group, 1)
                 widen_mtf(*scalar_units[group + 1])
             else:
-                diag_through(last, 1, C1)
+                diag_through(last, 1, C0)
                 interleave_dy(group, 1)
             finish(s - 2)
             inject_pair(s - 1)

@@ -32,8 +32,8 @@ SLOTS = 5
 STAGE = 4096
 KEPT = 1024
 WORK = KEPT + 2 * 2 * K
-SHORT = 144
-AHEAD = range(2, 5)
+SHORT = 128
+AHEAD = range(2, 4)
 MADE_SLOTS = 3
 
 
@@ -148,18 +148,16 @@ def tile_pansharpen_detail_injection_s8_kernel(
         load_codes(1)
         load_pan(1)
         load_bands(3)
-        load_bands(4)
         load_codes(2)
         load_pan_group(1)
         load_codes(3)
         load(gain_w[:].bitcast(I32), gain_words[0].bitcast(I32))
         for q in range(4):
             load(gain_s[32 * q : 32 * q + 4, :].bitcast(I32), gain_scales[0][4 * q : 4 * q + 4, :].bitcast(I32))
-        for g in range(2, GROUPS):
-            load_bands(2 * g + 1)
-            load_pan_group(g)
-            if g == 2:
-                load_bands(6)
+        for s in range(4, PAIRS):
+            load_bands(s)
+            if s % 2 == 0:
+                load_pan_group(s // 2)
 
         nc.scalar.activation(out=ident_b[:], in_=ident[:], func=COPY)
 
@@ -236,11 +234,18 @@ def tile_pansharpen_detail_injection_s8_kernel(
                 u, i = n // 2, n % 2
                 nc.tensor.transpose(bank[:, P * n : P * (n + 1)], doubles[:, 256 * i + u : 256 * (i + 1) : 2], ident[:])
 
+        def turn_mtf_side_by_side(a, g, bank):
+            doubles = mtf_b[2 * (g % 3) + a][:].bitcast(F32)
+            for n in range(4):
+                u, i = n // 2, n % 2
+                rows = slice(256 * i + u, 256 * (i + 1), 2)
+                nc.tensor.transpose(bank[:, rows], doubles[:, rows], ident[:])
+
         def scale_mtf_vector(a, g, bank):
             nc.vector.tensor_tensor(
-                out=staged(mtf_place[a, g], 0, 1024).rearrange("p (i x u e) -> p i x u e", i=2, u=2, e=2),
-                in0=bank.bitcast(BF16).rearrange("p (u i x e) -> p i x u e", i=2, u=2, e=2),
-                in1=scale_wide[g][:].rearrange("p (x u e) -> p x u e", u=2, e=2).unsqueeze(1).to_broadcast([P, 2, P, 2, 2]),
+                out=staged(mtf_place[a, g], 0, 1024).rearrange("p (i c) -> p i c", i=2),
+                in0=bank.bitcast(BF16).rearrange("p (i c) -> p i c", i=2),
+                in1=scale_wide[g][:].unsqueeze(1).to_broadcast([P, 2, 512]),
                 op=MULT,
             )
 
@@ -430,8 +435,8 @@ def tile_pansharpen_detail_injection_s8_kernel(
         intensity(0, 1)
         products_pool(0)
         products_ahead()
-        turn_mtf(0, 0, C1)
-        turn_mtf(1, 0, H[0])
+        turn_mtf_side_by_side(0, 0, C1)
+        turn_mtf_side_by_side(1, 0, H[0])
         widen_mtf(0, 1)
         widen_mtf(1, 1)
         subtract(0, 0)
@@ -444,8 +449,8 @@ def tile_pansharpen_detail_injection_s8_kernel(
         scale_mtf_vector(0, 0, C1)
         scale_mtf_vector(1, 0, H[0])
         intensity(1, 1)
-        turn_mtf(0, 1, H[0])
-        turn_mtf(1, 1, H[1])
+        turn_mtf_side_by_side(0, 1, H[0])
+        turn_mtf_side_by_side(1, 1, H[1])
         spread_scale(1)
         widen_mtf(0, 2)
         subtract(1, 0)

from contextlib import ExitStack

import concourse.mybir as mybir
from concourse.masks import make_identity

M, K, C, R = 2048, 1024, 512, 512
FLOPS = 2 * M * K * C + 2 * M * C * K + 2 * R * M * C
BYTES = 2 * M * K + 2 * K * C + 2 * M * C + 2 * K + 128 * 2 * K + 16 * K + R * M + 4 * M + 4 * M * K + 4 * R * C

F32 = mybir.dt.float32
BF16 = mybir.dt.bfloat16
I32 = mybir.dt.int32
U32 = mybir.dt.uint32
U8 = mybir.dt.uint8
FP8 = mybir.dt.float8_e4m3fn
FP8X4 = mybir.dt.float8_e4m3fn_x4
FP4X4 = mybir.dt.float4_e2m1fn_x4
MULT = mybir.AluOpType.mult
ADD = mybir.AluOpType.add
SUB = mybir.AluOpType.subtract

P = 128
BANK = 512
GROUPS = M // 512
HALVES = K // 512
PAIRS = M // (2 * P)
ROW_TILES = R // P
COPY = mybir.ActivationFunctionType.Copy
SHORT_PAIRS = (0, 1)
WHOLE_PAIRS = PAIRS - 3
SLOTS = 5
STAGE = 4096
KEPT = 1024
WORK = KEPT + 2 * 2 * K
SHORT = 128
AHEAD = range(2, 4)
MADE_SLOTS = 3


def tile_pansharpen_detail_injection_s8_kernel(
    tc, bands, mix, pan, radio, gain_words, gain_scales, mtf_bytes, mtf_scale, sharp, coarse
):
    nc = tc.nc
    with ExitStack() as ctx:
        sb = ctx.enter_context(tc.tile_pool(name="sb", bufs=1))
        ps = ctx.enter_context(tc.psum_pool(name="ps", bufs=1))

        def tiles(name, count, width, dtype):
            return [sb.tile([P, width], dtype, name=f"{name}{i}", align_bytes=64) for i in range(count)]

        def one(name, width, dtype):
            return tiles(name, 1, width, dtype)[0]

        def bank_tile(name, first, count=1):
            return ps.tile([P, count * BANK], F32, name=name, offset=4 * BANK * first)[:]

        head_banks = [bank_tile(f"head_bank{i}", i) for i in range(4)]
        inj_psum = bank_tile("inj_psum", 0, 4)
        tail_banks = [bank_tile(f"tail_bank{i}", i) for i in range(4)]
        int_banks = [bank_tile(f"int_bank{i}", 4 + i) for i in range(2)]
        turn_banks = [bank_tile(f"turn_bank{i}", 6 + i) for i in range(2)]

        def inj_bank(s, n):
            return inj_psum[:, BANK * n : BANK * (n + 1)] if s < WHOLE_PAIRS else tail_banks[n]

        ident = one("ident", P, F32)
        ident_b = one("ident_b", P, BF16)
        ones_b = one("ones_b", P, BF16)
        scale_col = one("scale_col", 4 * GROUPS, F32)
        scale_wide = {g: one(f"scale_wide{g}_", 512, F32) for g in (0, 1)}
        radio_col = one("radio_col", 8, BF16)
        radio_bc = one("radio_bc", K + 512, BF16)
        diag = one("diag", K, BF16)
        gain_w = one("gain_w", 2 * K, U8)
        gain_s = one("gain_s", K, U8)
        mix_c = tiles("mix_c", HALVES, C, U32)
        mix_s = tiles("mix_s", HALVES, C, U8)
        bands_all = one("bands_all", PAIRS * 2 * K, BF16)
        bands_sb = [bands_all[:, 2 * K * s : 2 * K * (s + 1)] for s in range(PAIRS)]
        pan_groups = tiles("pan_group", GROUPS, 4 * C, BF16)
        pan_sb = [pan_groups[s // 2][:, 2 * C * (s % 2) : 2 * C * (s % 2 + 1)] for s in range(PAIRS)]
        codes = tiles("codes", GROUPS, ROW_TILES * 512, U8)
        mtf_b = tiles("mtf_b", 6, 1024, BF16)
        planes = one("planes", 1024, BF16)
        work_all = one("work", SLOTS * WORK, BF16)
        work = [work_all[:, WORK * i : WORK * (i + 1)] for i in range(SLOTS)]
        made = tiles("made", MADE_SLOTS, STAGE, BF16)
        detail = tiles("detail", GROUPS, 4 * C, BF16)
        res = tiles("res", ROW_TILES // 2, 2 * C, F32)

        last = PAIRS - 1
        call_in = {("first", s): work[s % SLOTS][:, 0:2048] for s in range(-1, PAIRS)}
        for s in range(1, PAIRS + 1):
            call_in["made", s] = made[s % MADE_SLOTS][:, 0 : STAGE if s in (4, 6, 8) else 2048]
        call_c = {c: one(f"call_c_{c[0]}{c[1] + 1}_", src.shape[1] // 4, U32) for c, src in call_in.items()}
        call_s = {c: one(f"call_s_{c[0]}{c[1] + 1}_", src.shape[1] // 4, U8) for c, src in call_in.items()}
        bands_place = {(s, t): (("first" if t else "made", s - 1), 0) for s in range(PAIRS) for t in range(2)}
        bands_place[0, 0] = (("first", -1), K)
        bands_place[1, 0] = (("first", 0), K)
        dx_place = [(("first", s + 1), K) for s in range(last)] + [(("made", PAIRS), 0)]
        dy_place = [(("made", 4), 2048), (("made", 6), 2048), (("made", last), 0), (("made", PAIRS), 2048)]
        units = [(a, g) for g in range(GROUPS) for a in range(2)]
        mtf_place = {unit: (("made", n + 1), 1024) for n, unit in enumerate(units)}
        mtf_place[0, GROUPS - 1] = (("first", last), 0)
        mix_raw = [work[3][:, 2048 * h : 2048 * (h + 1)] for h in range(HALVES)]
        mix_il = [made[0][:, 2048 * h : 2048 * (h + 1)] for h in range(HALVES)]

        def out_sb(s):
            return work[s % SLOTS][:, KEPT:].bitcast(F32)

        bands_v = bands.rearrange("(g p a t) k -> g a p (t k)", p=P, a=2, t=2)
        pan_v = pan.rearrange("(g p a t) c -> g a p (t c)", p=P, a=2, t=2)
        sharp_v = sharp.rearrange("(g p a t) k -> g a p (t k)", p=P, a=2, t=2)
        mix_v = mix.rearrange("(h p j) c -> h p (j c)", p=P, j=4)
        mtf_v = mtf_bytes.rearrange("(p r) (g k) -> g p r k", r=ROW_TILES, k=512)
        coarse_v = coarse.rearrange("(p i r) c -> i p (r c)", i=2, r=2)

        ctx.enter_context(tc.manual_schedule())

        make_identity(nc, ident[:])
        nc.gpsimd.memset(ones_b[:], 1.0)
        nc.vector.memset(gain_s[:].bitcast(I32), 0)

        def load(dst, src):
            nc.sync.dma_start(out=dst, in_=src)

        def load_bands(s):
            load(bands_sb[s], bands_v[s // 2, s % 2])

        def load_pan(s):
            load(pan_sb[s], pan_v[s // 2, s % 2])

        def load_pan_group(g):
            load(pan_groups[g][:], pan.rearrange("(g p j) c -> g p (j c)", p=P, j=4)[g])

        def load_codes(g):
            load(codes[g][:].rearrange("p (r k) -> p r k", r=ROW_TILES), mtf_v[g])

        load(radio_col[:].rearrange("p (h j) -> p h j", j=4), radio.rearrange("(h p j) -> p h j", p=P, j=4))
        load(mix_raw[0], mix_v[0])
        load_bands(0)
        load(mix_raw[1], mix_v[1])
        load_bands(1)
        load(scale_col[:].rearrange("p (g j) -> p g j", j=4), mtf_scale.rearrange("o (g p j) -> p (o g) j", p=P, j=4))
        load_codes(0)
        load_pan(0)
        load_bands(2)
        load_codes(1)
        load_pan(1)
        load_bands(3)
        load_codes(2)
        load_pan_group(1)
        load_codes(3)
        load(gain_w[:].bitcast(I32), gain_words[0].bitcast(I32))
        for q in range(4):
            load(gain_s[32 * q : 32 * q + 4, :].bitcast(I32), gain_scales[0][4 * q : 4 * q + 4, :].bitcast(I32))
        for s in range(4, PAIRS):
            load_bands(s)
            if s % 2 == 0:
                load_pan_group(s // 2)

        nc.scalar.activation(out=ident_b[:], in_=ident[:], func=COPY)

        def staged(place, start, width):
            call, first = place
            return call_in[call][:, first + start : first + start + width]

        def operand(place, start, width):
            call, first = place
            cols = slice(first // 4 + start, first // 4 + start + width)
            return call_c[call][:, cols].bitcast(FP8X4), call_s[call][:, cols]

        def quantize(codes_out, scales_out, src):
            nc.vector.quantize_mx(out=codes_out.bitcast(FP8X4), scales=scales_out, in_=src)

        def quantize_call(call, start=0, width=None):
            if width is None:
                width = call_in[call].shape[1]
            cols = slice(start // 4, (start + width) // 4)
            quantize(call_c[call][:, cols], call_s[call][:, cols], call_in[call][:, start : start + width])

        def turn_out(bank, dst):
            nc.scalar.copy(
                out=dst.bitcast(F32).rearrange("p (h x u) -> p h x u", h=2, u=2),
                in_=bank.rearrange("p (h u x) -> p h x u", h=2, u=2),
            )

        def interleave(dst, rows):
            nc.scalar.copy(
                out=dst.rearrange("p (m i j) -> p m j i", i=2, j=4), in_=rows.rearrange("p j (m i) -> p m j i", i=2)
            )

        def build_diag():
            nc.vector.tensor_tensor(
                out=diag[:].rearrange("p (n m) -> p n m", m=P),
                in0=ident_b[:].unsqueeze(1).to_broadcast([P, 8, P]),
                in1=radio_col[:].unsqueeze(2).to_broadcast([P, 8, P]),
                op=MULT,
            )

        def spread_radio(h, bank):
            nc.tensor.matmul(bank, ones_b[:], diag[:, 512 * h : 512 * (h + 1)], start=True, stop=True)

        def radio_out(h, bank, copy=nc.scalar.copy):
            copy(
                out=radio_bc[:, 512 * h : 512 * (h + 1)].rearrange("p (m j) -> p m j", j=4),
                in_=bank.rearrange("p (j m) -> p m j", j=4),
            )

        def repeat_radio():
            nc.scalar.copy(out=radio_bc[:, K : K + 512], in_=radio_bc[:, 0:512])

        def interleave_mix(h):
            nc.vector.tensor_copy(
                out=mix_il[h].rearrange("p (u m e j) -> p m j u e", u=2, e=2, j=4),
                in_=mix_raw[h].rearrange("p (j m u e) -> p m j u e", u=2, e=2, j=4),
            )

        def quantize_mix(h):
            quantize(mix_c[h][:], mix_s[h][:], mix_il[h])

        def widen_mtf(a, g, copy=nc.scalar.copy):
            copy(out=mtf_b[2 * (g % 3) + a][:], in_=codes[g][:, 1024 * a : 1024 * (a + 1)].bitcast(FP8))

        def spread_scale(g):
            nc.scalar.copy(
                out=scale_wide[g][:].rearrange("p (x j) -> p x j", j=4),
                in_=scale_col[:, 4 * g : 4 * (g + 1)].unsqueeze(1).to_broadcast([P, P, 4]),
            )

        def turn_mtf(a, g, bank):
            doubles = mtf_b[2 * (g % 3) + a][:].bitcast(F32)
            for n in range(4):
                u, i = n // 2, n % 2
                nc.tensor.transpose(bank[:, P * n : P * (n + 1)], doubles[:, 256 * i + u : 256 * (i + 1) : 2], ident[:])

        def turn_mtf_side_by_side(a, g, bank):
            doubles = mtf_b[2 * (g % 3) + a][:].bitcast(F32)
            for n in range(4):
                u, i = n // 2, n % 2
                rows = slice(256 * i + u, 256 * (i + 1), 2)
                nc.tensor.transpose(bank[:, rows], doubles[:, rows], ident[:])

        def scale_mtf_vector(a, g, bank):
            nc.vector.tensor_tensor(
                out=staged(mtf_place[a, g], 0, 1024).rearrange("p (i c) -> p i c", i=2),
                in0=bank.bitcast(BF16).rearrange("p (i c) -> p i c", i=2),
                in1=scale_wide[g][:].unsqueeze(1).to_broadcast([P, 2, 512]),
                op=MULT,
            )

        def scale_mtf_scalar(g, bank):
            values = bank.bitcast(BF16).rearrange("p (u x e) -> p u e x", u=2, e=2)
            for j in range(4):
                nc.scalar.activation(
                    out=planes[:, 256 * j : 256 * (j + 1)],
                    in_=values[:, j // 2, j % 2, :],
                    func=COPY,
                    scale=scale_col[:, 4 * g + j : 4 * g + j + 1],
                )

        def interleave_mtf(a, g):
            interleave(staged(mtf_place[a, g], 0, 1024), planes[:].rearrange("p (j x) -> p j x", j=4))

        def staged_bands(s, t):
            return staged(bands_place[s, t], 0, K)

        def turn_bands(s, t, bank):
            doubles = bands_sb[s][:, K * t : K * (t + 1)].bitcast(F32)
            for n in range(4):
                start = 256 * (n // 2) + n % 2
                nc.tensor.transpose(bank[:, P * n : P * (n + 1)], doubles[:, start : 256 * (n // 2 + 1) : 2], ident[:])

        def bands_out(s, t, bank):
            turn_out(bank, staged_bands(s, t))

        def intensity_pass(s, t, h):
            x_c, x_s = operand(bands_place[s, t], P * h, P)
            nc.tensor.matmul_mx(
                out=int_banks[1 - t],
                lhsT=x_c,
                lhsT_scale=x_s,
                rhs=mix_c[h][:].bitcast(FP8X4),
                rhs_scale=mix_s[h][:],
                start=(h == 0),
                stop=(h == HALVES - 1),
            )

        def intensity(s, t):
            for h in range(HALVES):
                intensity_pass(s, t, h)

        def subtract(s, t):
            row = 2 * (s % 2) + t
            nc.vector.tensor_tensor(
                out=detail[s // 2][:, C * row : C * (row + 1)].rearrange("p (u m e) -> p u m e", u=2, e=2),
                in0=pan_sb[s][:, C * t : C * (t + 1)].rearrange("p (m u e) -> p u m e", u=2, e=2),
                in1=int_banks[1 - t].rearrange("p (u m e) -> p u m e", u=2, e=2),
                op=SUB,
            )

        def turn_detail(s, bank):
            doubles = detail[s // 2][:, 1024 * (s % 2) : 1024 * (s % 2 + 1)].bitcast(F32)
            for n in range(4):
                nc.tensor.transpose(bank[:, P * n : P * (n + 1)], doubles[:, P * n : P * (n + 1)], ident[:])

        def detail_out(s, bank):
            turn_out(bank, staged(dx_place[s], 0, 1024))

        def interleave_dy(g, half):
            rows = detail[g][:].rearrange("p (j c) -> p j c", j=4)[:, :, 256 * half : 256 * (half + 1)]
            interleave(staged(dy_place[g], 1024 * half, 1024), rows)

        short = slice(K + 512 - SHORT, K + 512)

        def products_ahead():
            pairs = slice(AHEAD.start, AHEAD.stop)
            results = work_all[:].bitcast(F32).rearrange("p (a c) -> p a c", a=SLOTS)[:, pairs, KEPT // 2 :]
            nc.gpsimd.tensor_tensor(
                out=results[:, :, short],
                in0=bands_all[:].rearrange("p (a c) -> p a c", a=PAIRS)[:, pairs, short],
                in1=radio_bc[:, short].unsqueeze(1).to_broadcast([P, len(AHEAD), SHORT]),
                op=MULT,
            )

        def products_vector(s):
            nc.vector.tensor_tensor(out=out_sb(s)[:, short], in0=bands_sb[s][:, short], in1=radio_bc[:, short], op=MULT)

        def products_pool(s, width=K + 512):
            cols = slice(0, width)
            nc.gpsimd.tensor_tensor(out=out_sb(s)[:, cols], in0=bands_sb[s][:, cols], in1=radio_bc[:, cols], op=MULT)

        def diag_matmuls(s, h, bank):
            values = staged_bands(s, 1)[:, 512 * h : 512 * (h + 1)]
            for j in range(4):
                d0 = 512 * h + P * j
                nc.tensor.matmul(
                    bank[:, P * j : P * (j + 1)], values[:, j:512:4], diag[:, d0 : d0 + P], start=True, stop=True
                )

        def diag_out(s, h, bank):
            nc.scalar.copy(
                out=out_sb(s)[:, K + 512 * h : K + 512 * (h + 1)].rearrange("p (m j) -> p m j", j=4),
                in_=bank.rearrange("p (j m) -> p m j", j=4),
            )

        def inject(s, n):
            t, h = n // 2, n % 2
            dx_c, dx_s = operand(dx_place[s], P * t, P)
            nc.tensor.matmul_mx(
                out=inj_bank(s, n),
                lhsT=dx_c,
                lhsT_scale=dx_s,
                rhs=gain_w[:, 1024 * h : 1024 * (h + 1)].bitcast(FP4X4),
                rhs_scale=gain_s[:, 512 * h : 512 * (h + 1)],
                start=True,
                stop=True,
            )

        def finish(s):
            out = out_sb(s)
            nc.vector.tensor_tensor(out=out, in0=out, in1=inj_psum, op=ADD)
            nc.sync.dma_start(out=sharp_v[s // 2, s % 2], in_=out)

        def finish_piece(s, n):
            cols = slice(512 * n, 512 * (n + 1))
            out = out_sb(s)
            nc.vector.tensor_tensor(out=out[:, cols], in0=out[:, cols], in1=inj_bank(s, n), op=ADD)
            if n % 2 == 1:
                row = slice(K * (n // 2), K * (n // 2 + 1))
                nc.sync.dma_start(out=sharp_v[s // 2, s % 2][:, row], in_=out[:, row])

        coarse_banks = [turn_banks[1], int_banks[0], int_banks[1], turn_banks[0]]

        def coarse_passes(row_tiles, groups):
            for r in row_tiles:
                for g in groups:
                    mtf_c, mtf_s = operand(mtf_place[r // 2, g], P * (r % 2), P)
                    dy_c, dy_s = operand(dy_place[g], 0, C)
                    nc.tensor.matmul_mx(
                        out=coarse_banks[r],
                        lhsT=mtf_c,
                        lhsT_scale=mtf_s,
                        rhs=dy_c,
                        rhs_scale=dy_s,
                        start=(g == 0),
                        stop=(g == GROUPS - 1),
                    )

        def coarse_out(r):
            nc.scalar.copy(
                out=res[r // 2][:, C * (r % 2) : C * (r % 2 + 1)].rearrange("p (m u e) -> p m u e", u=2, e=2),
                in_=coarse_banks[r].rearrange("p (u m e) -> p m u e", u=2, e=2),
            )
            if r % 2 == 1:
                nc.scalar.dma_start(out=coarse_v[r // 2], in_=res[r // 2][:])

        H = head_banks
        C0, C1 = turn_banks

        def bands_through(s, t, bank):
            turn_bands(s, t, bank)
            bands_out(s, t, bank)

        def diag_through(s, h, bank):
            diag_matmuls(s, h, bank)
            diag_out(s, h, bank)

        def inject_pair(s):
            for n in range(4):
                inject(s, n)

        build_diag()
        spread_radio(0, H[0])
        spread_radio(1, H[1])
        radio_out(0, H[0])
        radio_out(1, H[1])
        interleave_mix(0)
        quantize_mix(0)
        interleave_mix(1)
        bands_through(0, 0, C0)
        bands_through(0, 1, C1)
        repeat_radio()
        bands_through(1, 0, H[2])
        bands_through(1, 1, H[3])
        diag_matmuls(0, 1, C0)
        quantize_call(("first", -1))
        quantize_mix(1)
        widen_mtf(0, 0, nc.vector.tensor_copy)
        quantize_call(("first", 0))
        widen_mtf(1, 0)
        spread_scale(0)
        diag_out(0, 1, C0)
        intensity(0, 0)
        intensity(0, 1)
        products_pool(0)
        products_ahead()
        turn_mtf_side_by_side(0, 0, C1)
        turn_mtf_side_by_side(1, 0, H[0])
        widen_mtf(0, 1)
        widen_mtf(1, 1)
        subtract(0, 0)
        subtract(0, 1)
        turn_detail(0, H[3])
        detail_out(0, H[3])
        intensity(1, 0)
        bands_through(2, 0, H[1])
        bands_through(2, 1, H[2])
        scale_mtf_vector(0, 0, C1)
        scale_mtf_vector(1, 0, H[0])
        intensity(1, 1)
        turn_mtf_side_by_side(0, 1, H[0])
        turn_mtf_side_by_side(1, 1, H[1])
        spread_scale(1)
        widen_mtf(0, 2)
        subtract(1, 0)
        subtract(1, 1)

        scalar_units = units[4:]
        quantize_call(("first", 1))
        quantize_call(("made", 1))
        products_pool(1)
        diag_through(1, 1, C0)
        intensity(2, 1)
        interleave_dy(0, 0)
        turn_detail(1, H[2])
        detail_out(1, H[2])
        bands_through(3, 0, H[3])
        intensity(2, 0)
        bands_through(3, 1, C0)
        scale_mtf_vector(0, 1, H[0])
        scale_mtf_vector(1, 1, H[1])
        turn_mtf(*scalar_units[0], C1)
        scale_mtf_scalar(scalar_units[0][1], C1)
        inject_pair(0)
        subtract(2, 1)
        subtract(2, 0)

        for s in range(2, last):
            odd = s % 2 == 1
            group = (s - 1) // 2
            quantize_call(("first", s))
            quantize_call(("made", s))
            products_pool(s, short.start if s in AHEAD else short.stop)
            detail_bank = int_banks[1] if s + 2 <= last else C0
            turn_detail(s, detail_bank)
            detail_out(s, detail_bank)
            if s + 2 <= last:
                bands_through(s + 2, 0, C0)
                bands_through(s + 2, 1, C1)
            if odd:
                interleave_dy(group, 0)
            else:
                interleave_mtf(*scalar_units[group])
            if s == last - 1:
                widen_mtf(*scalar_units[group + 1])
            intensity(s + 1, 1)
            intensity(s + 1, 0)
            diag_through(s, 1, C0 if s + 2 <= last else C1)
            if odd:
                turn_mtf(*scalar_units[group], C1)
                scale_mtf_scalar(scalar_units[group][1], C1)
            elif s + 1 < last:
                interleave_dy(group, 1)
                widen_mtf(*scalar_units[group + 1])
            else:
                diag_through(last, 1, C0)
                interleave_dy(group, 1)
            finish(s - 2)
            inject_pair(s - 1)
            subtract(s + 1, 1)
            subtract(s + 1, 0)

        quantize_call(("first", last), K, K)
        quantize_call(("first", last), 0, K)
        products_pool(last)
        turn_detail(last, int_banks[1])
        turn_mtf(1, 3, C0)
        interleave_dy(GROUPS - 1, 0)
        detail_out(last, int_banks[1])
        interleave_dy(GROUPS - 1, 1)
        scale_mtf_scalar(3, C0)
        interleave_mtf(1, 3)
        coarse_passes([1], range(2))
        for n in range(4):
            finish_piece(last - 2, n)
            inject(last - 1, n)
            if n < 2:
                coarse_passes([0], [n])
        coarse_passes([2], range(2))
        finish_piece(last - 1, 0)
        finish_piece(last - 1, 1)
        quantize_call(("made", last))
        quantize_call(("made", PAIRS), 2048, 2048)
        quantize_call(("made", PAIRS), 0, 1024)
        coarse_passes([0, 1], [2])
        coarse_passes([0, 1], [3])
        inject(last, 0)
        inject(last, 1)
        coarse_passes([3], range(3))
        coarse_passes([2], [2])
        coarse_out(0)
        coarse_out(1)
        finish_piece(last - 1, 2)
        finish_piece(last - 1, 3)
        quantize_call(("made", PAIRS), 1024, 1024)
        coarse_passes([2, 3], [3])
        inject(last, 2)
        inject(last, 3)
        coarse_out(2)
        coarse_out(3)
        for n in range(4):
            finish_piece(last, n)
